import numpy as np
import ml_dtypes


def mxq(x, axis, fmt="e4m3"):
    dtype, down = {"e4m3": (ml_dtypes.float8_e4m3fn, 7), "e5m2": (ml_dtypes.float8_e5m2, 14)}[fmt]
    v = np.moveaxis(np.asarray(x, np.float32).astype(ml_dtypes.bfloat16).astype(np.float64), axis, -1)
    blocks = v.reshape(v.shape[:-1] + (-1, 32))
    amax = np.abs(blocks).max(-1, keepdims=True)
    byte = np.maximum(np.where(amax > 0, np.frexp(amax)[1] - 1 + 127, 0) - down, 1)
    scale = np.exp2(byte - 127.0)
    codes = (blocks / scale).astype(np.float32).astype(dtype).astype(np.float64)
    return np.moveaxis((codes * scale).reshape(v.shape), -1, axis)


WIDE = False


def mx_kscale(k):
    if not WIDE:
        return np.ones(k)
    levels = np.array([30, -30])
    if k % 512:
        return np.exp2(np.random.permutation(np.resize(levels, k // 32))).repeat(32)
    a = np.empty((k // 512, 16))
    for p in range(k // 512):
        a[p, :8] = np.random.permutation(np.resize(levels, 8))
        for g in range(8):
            far = levels[np.abs(levels - a[p, g]) >= 10]
            a[p, g + 8] = far[np.random.randint(len(far))]
    return np.exp2(a.ravel()).repeat(32)


BF16 = ml_dtypes.bfloat16


def bf(x):
    return np.asarray(x, np.float32).astype(BF16)


def f64(x):
    return np.asarray(x).astype(np.float64)


E2M1 = np.array([0.0, 0.5, 1.0, 1.5, 2.0, 3.0, 4.0, 6.0, -0.0, -0.5, -1.0, -1.5, -2.0, -3.0, -4.0, -6.0])


def pack_weight(w, fmt):
    k, n = w.shape
    w = f64(bf(w)).reshape(k // 32, 32, n)
    amax = np.abs(w).max(1)
    if fmt in ("e4m3", "e5m2"):
        byte = np.frexp(amax)[1] - 1 + 127 - (7 if fmt == "e4m3" else 14)
    else:
        mant, ex = np.frexp(amax / 6.0)
        byte = np.where(mant > 0.5, ex, ex - 1) + 127
    byte = np.clip(np.where(amax > 0, byte, 1), 1, 254)
    scaled = (w * np.exp2(127.0 - byte)[:, None, :]).reshape(k, n).astype(np.float32)
    by_word = np.ascontiguousarray(scaled.reshape(k // 512, 128, 4, n).transpose(0, 1, 3, 2))
    if fmt in ("e4m3", "e5m2"):
        words = by_word.astype(ml_dtypes.float8_e4m3fn if fmt == "e4m3" else ml_dtypes.float8_e5m2).view(np.uint8)
    else:
        c = by_word.astype(ml_dtypes.float4_e2m1fn).view(np.uint8) & 0xF
        words = c[..., 0::2] | (c[..., 1::2] << 4)
    return np.ascontiguousarray(words), np.ascontiguousarray(byte.astype(np.uint8).reshape(k // 512, 16, n))


def unpack_weight(words, scales, fmt):
    g, p, n, _ = words.shape
    if fmt in ("e4m3", "e5m2"):
        vals = np.ascontiguousarray(words).view(ml_dtypes.float8_e4m3fn if fmt == "e4m3" else ml_dtypes.float8_e5m2).astype(np.float64)
    else:
        nib = np.empty((g, p, n, 4), np.uint8)
        nib[..., 0::2] = words & 0xF
        nib[..., 1::2] = words >> 4
        vals = E2M1[nib]
    vals = vals * np.repeat(np.exp2(scales.astype(np.float64) - 127.0), 8, axis=1)[..., None]
    return vals.transpose(0, 1, 3, 2).reshape(g * 512, n)


F, S, I, B = 1536, 2048, 1024, 512


def setup_inputs():
    s, t = mx_kscale(F), mx_kscale(I)
    shocks = np.random.standard_t(5, (F, S)) * s[:, None]
    g_words, g_scales = pack_weight(shocks, "e5m2")
    delta = np.random.standard_normal((I, F)) / np.sqrt(F) / s * t[:, None]
    carry = 0.3 * np.random.standard_normal(I) * t
    stress = np.exp(0.4 * np.random.standard_normal((S, I)))
    hold = np.random.standard_normal((I, B)) / np.sqrt(I) / t[:, None]
    hedge = 0.5 * np.random.standard_normal((S, B))
    return {"g_words": g_words, "g_scales": g_scales,
            "delta": bf(delta), "carry": bf(carry), "stress": bf(stress),
            "hold": bf(hold), "hedge": bf(hedge)}


def reference(g_words, g_scales, delta, carry, stress, hold, hedge):
    g = unpack_weight(g_words, g_scales, "e5m2")
    d = mxq(f64(delta), 1, "e4m3")
    unit = g.T @ d.T
    pnl = (unit + f64(carry)) * f64(stress)
    h = mxq(f64(hold), 0, "e4m3")
    book = mxq(pnl, 1, "e5m2") @ h
    return book + f64(hedge)

@@ -1,0 +1,393 @@
+from contextlib import ExitStack
+
+import concourse.mybir as mybir
+from concourse.masks import make_identity
+
+F, S, I, B = 1536, 2048, 1024, 512
+FLOPS = 2 * S * F * I + 2 * S * I * B
+
+F32 = mybir.dt.float32
+BF16 = mybir.dt.bfloat16
+U32 = mybir.dt.uint32
+I32 = mybir.dt.int32
+U8 = mybir.dt.uint8
+E4 = mybir.dt.float8_e4m3fn_x4
+E5 = mybir.dt.float8_e5m2_x4
+ACT = mybir.ActivationFunctionType
+ALU = mybir.AluOpType
+
+P = 128
+A = F // 512
+G = I // 512
+SC = 512
+C = S // SC
+J = SC // P
+
+
+def tile_scenario_book_pnl_e3_kernel(tc, g_words, g_scales, delta, carry, stress, hold, hedge, out):
+    nc = tc.nc
+    with ExitStack() as ctx:
+        keep = ctx.enter_context(tc.tile_pool(name="keep", bufs=1))
+        work = ctx.enter_context(tc.tile_pool(name="work", bufs=3))
+        psum = ctx.enter_context(tc.psum_pool(name="psum", bufs=2))
+
+        ident = keep.tile([P, P], F32, name="ident")
+        make_identity(nc, ident[:])
+
+        d_raw = []
+        for i in range(8):
+            d_raw.append(keep.tile([P, F], BF16, name="d_raw%d" % i))
+        gw = []
+        st = []
+        hg = []
+        for c in range(C):
+            gw.append(keep.tile([P, A, SC], U32, name="gw%d" % c, align_bytes=64))
+            st.append(keep.tile([P, J, I], BF16, name="st%d" % c))
+            hg.append(keep.tile([P, J, B], BF16, name="hg%d" % c))
+        gs = []
+        for c in range(C):
+            gs.append(keep.tile([P, A, SC], U8, name="gs%d" % c, align_bytes=64))
+        h_raw = keep.tile([P, G, 4, B], BF16, name="h_raw")
+        h_grp = keep.tile([P, G, B, 4], BF16, name="h_grp", align_bytes=64)
+        h_codes = keep.tile([P, G, B], U32, name="h_codes", align_bytes=64)
+        h_sc = keep.tile([P, G, B], U8, name="h_sc", align_bytes=64)
+        ca_raw = keep.tile([P, 512], BF16, name="ca_raw")
+        ca = keep.tile([P, G, 4], F32, name="ca")
+        d_codes = []
+        d_sc = []
+        for i in range(8):
+            d_codes.append(keep.tile([P, A, P], U32, name="d_codes%d" % i, align_bytes=64))
+            d_sc.append(keep.tile([P, A, P], U8, name="d_sc%d" % i, align_bytes=64))
+
+        d_view = delta.rearrange("(g m t) k -> g t m k", g=G, t=4)
+        gw_view = g_words.rearrange("g p n t -> p g (n t)")
+        gs_view = g_scales.bitcast(I32).rearrange("a r n -> r a n")
+        st_view = stress.rearrange("(c j p) i -> c p j i", c=C, p=P)
+        hg_view = hedge.rearrange("(c j p) b -> c p j b", c=C, p=P)
+
+        units = {}
+        stress_t = {}
+        st_re = {}
+        pnl = {}
+        pnl_codes = {}
+        pnl_sc = {}
+        d_bank = {}
+        d_grp = {}
+
+        def load_d(i):
+            nc.sync.dma_start(out=d_raw[i][:], in_=d_view[i // 4, i % 4])
+
+        def load_g(c):
+            nc.sync.dma_start(out=gw[c][:].bitcast(I32), in_=gw_view[:, :, 2048 * c : 2048 * (c + 1)].bitcast(I32))
+
+        def load_st(c):
+            nc.sync.dma_start(out=st[c][:], in_=st_view[c])
+
+        def load_hg(c):
+            nc.sync.dma_start(out=hg[c][:], in_=hg_view[c])
+
+        def load_gs(c):
+            for q in range(4):
+                nc.sync.dma_start(
+                    out=gs[c][32 * q : 32 * q + 4].bitcast(I32), in_=gs_view[4 * q : 4 * q + 4, :, P * c : P * (c + 1)]
+                )
+
+        def zero_gs(c):
+            nc.vector.memset(gs[c][:].rearrange("p a n -> p (a n)").bitcast(I32), 0)
+
+        def t_carry():
+            bank = psum.tile([P, 2, P], F32, name="out_ps", bufs=2)
+            words = ca_raw[:].bitcast(F32)
+            for u in range(2):
+                nc.tensor.transpose(bank[:, u, :], words[:, u : 256 : 2], ident[:])
+            nc.vector.tensor_copy(
+                out=ca[:].rearrange("p g (u e) -> p g u e", u=2),
+                in_=bank[:, :, 0:G].bitcast(BF16).rearrange("p u (g e) -> p g u e", e=2),
+            )
+
+        def t_delta(i):
+            bank_a = psum.tile([P, 2, 2, P], F32, name="tr", bufs=4)
+            bank_b = psum.tile([P, 1, 2, P], F32, name="tr", bufs=4)
+            words = d_raw[i][:].bitcast(F32)
+            for a in range(A):
+                for u in range(2):
+                    dst = bank_a[:, a, u, :] if a < 2 else bank_b[:, 0, u, :]
+                    nc.tensor.transpose(dst, words[:, 256 * a + u : 256 * (a + 1) : 2], ident[:])
+            grp = work.tile([P, A, P, 4], BF16, name="d_grp", align_bytes=64)
+            d_bank[i] = (bank_a, bank_b)
+            d_grp[i] = grp
+
+        def s_delta(i):
+            nc.scalar.copy(
+                out=d_grp[i][:, 0:2].rearrange("p a m t -> p a (m t)").bitcast(F32).rearrange("p a (m u) -> p a m u", u=2),
+                in_=d_bank[i][0][:].rearrange("p a u m -> p a m u"),
+            )
+
+        def v_delta(i):
+            grp = d_grp[i]
+            nc.vector.tensor_copy(
+                out=grp[:, 2:3].rearrange("p a m t -> p a (m t)").bitcast(F32).rearrange("p a (m u) -> p a m u", u=2),
+                in_=d_bank[i][1][:].rearrange("p a u m -> p a m u"),
+            )
+            nc.vector.quantize_mx(
+                out=d_codes[i][:, 0:2].rearrange("p a m -> p (a m)").bitcast(E4),
+                scales=d_sc[i][:, 0:2].rearrange("p a m -> p (a m)"),
+                in_=grp[:, 0:2].rearrange("p a m t -> p (a m t)"),
+            )
+            nc.vector.quantize_mx(
+                out=d_codes[i][:, 2].bitcast(E4), scales=d_sc[i][:, 2], in_=grp[:, 2].rearrange("p m t -> p (m t)")
+            )
+
+        def mx1(c, i):
+            acc = psum.tile([P, SC], F32, name="unit_ps", bufs=2)
+            for a in range(A):
+                nc.tensor.matmul_mx(
+                    out=acc[:],
+                    lhsT=d_codes[i][:, a, :].bitcast(E4),
+                    lhsT_scale=d_sc[i][:, a, :],
+                    rhs=gw[c][:, a, :].bitcast(E5),
+                    rhs_scale=gs[c][:, a, :],
+                    start=(a == 0),
+                    stop=(a == A - 1),
+                )
+            g, t = i // 4, i % 4
+            if t == 0:
+                units[(c, g)] = work.tile([P, 4, SC], F32, name="unit")
+            nc.scalar.activation(
+                out=units[(c, g)][:, t, :], in_=acc[:], func=ACT.Identity, bias=ca[:, g, t : t + 1], scale=1.0
+            )
+
+        def reorder(c, g, h):
+            if g == 0 and h == 0:
+                st_re[c] = work.tile([P, G, J, 2, P], F32, name="st_re", bufs=2)
+            nc.scalar.copy(
+                out=st_re[c][:, g, 2 * h : 2 * h + 2],
+                in_=st[c][:].bitcast(F32).rearrange("p j (g m u) -> p g j u m", g=G, u=2)[:, g, 2 * h : 2 * h + 2],
+            )
+
+        def t_stress(c, g, tag, bufs):
+            banks = []
+            for h in range(2):
+                bank = psum.tile([P, 2, 2, P], F32, name=tag, bufs=bufs)
+                for jj in range(2):
+                    for u in range(2):
+                        if c == 0:
+                            words = st[c][:, 2 * h + jj, :].bitcast(F32)[:, 256 * g + u : 256 * (g + 1) : 2]
+                        else:
+                            words = st_re[c][:, g, 2 * h + jj, u, :]
+                        nc.tensor.transpose(bank[:, u, jj, :], words, ident[:])
+                banks.append(bank)
+            stress_t[(c, g)] = banks
+            pnl[(c, g)] = work.tile([P, SC, 4], BF16, name="pnl", align_bytes=64, bufs=2)
+            pnl_codes[(c, g)] = work.tile([P, SC], U32, name="pnl_codes", align_bytes=64, bufs=4)
+            pnl_sc[(c, g)] = work.tile([P, SC], U8, name="pnl_sc", align_bytes=64, bufs=4)
+
+        def v_mul(c, g, lo, hi):
+            h = lo // 256
+            cols = slice(lo, hi)
+            bank = stress_t[(c, g)][h]
+            nc.vector.tensor_tensor(
+                out=pnl[(c, g)][:, cols, :].rearrange("p s (u e) -> p s u e", u=2),
+                in0=units[(c, g)][:, :, cols].rearrange("p (u e) s -> p s u e", u=2),
+                in1=bank[:].rearrange("p u j s -> p u (j s)")[:, :, lo - 256 * h : hi - 256 * h]
+                .bitcast(BF16)
+                .rearrange("p u (s e) -> p s u e", e=2),
+                op=ALU.mult,
+            )
+
+        def v_quant(c, g, h):
+            cols = slice(256 * h, 256 * (h + 1))
+            nc.vector.quantize_mx(
+                out=pnl_codes[(c, g)][:, cols].bitcast(E5),
+                scales=pnl_sc[(c, g)][:, cols],
+                in_=pnl[(c, g)][:, cols, :].rearrange("p s t -> p (s t)"),
+            )
+
+        def mx2_pass(c, j, g, acc):
+            cols = slice(P * j, P * (j + 1))
+            nc.tensor.matmul_mx(
+                out=acc[:],
+                lhsT=pnl_codes[(c, g)][:, cols].bitcast(E5),
+                lhsT_scale=pnl_sc[(c, g)][:, cols],
+                rhs=h_codes[:, g, :].bitcast(E4),
+                rhs_scale=h_sc[:, g, :],
+                start=(g == 0),
+                stop=(g == G - 1),
+            )
+
+        def mx2(c, j):
+            acc = psum.tile([P, B], F32, name="out_ps", bufs=2)
+            for g in range(G):
+                mx2_pass(c, j, g, acc)
+            return (c, j, acc)
+
+        def v_out(item):
+            c, j, acc = item
+            res = work.tile([P, B], F32, name="res", bufs=5)
+            nc.vector.tensor_tensor(out=res[:], in0=acc[:], in1=hg[c][:, j, :], op=ALU.add)
+            s0 = SC * c + P * j
+            nc.sync.dma_start(out=out[s0 : s0 + P, :], in_=res[:])
+
+        def store(c, j, res):
+            s0 = SC * c + P * j
+            nc.sync.dma_start(out=out[s0 : s0 + P, :], in_=res[:])
+
+        def s_evac(item):
+            raw = work.tile([P, B], F32, name="res_raw", bufs=4)
+            nc.scalar.copy(out=raw[:], in_=item[2][:])
+            return raw
+
+        def v_add(item, raw):
+            res = work.tile([P, B], F32, name="res", bufs=5)
+            nc.vector.tensor_tensor(out=res[:], in0=raw[:], in1=hg[item[0]][:, item[1], :], op=ALU.add)
+            store(item[0], item[1], res)
+
+        def g_add(item, raw):
+            res = work.tile([P, B], F32, name="res_g", bufs=4)
+            for k in range(0, B, 256):
+                cols = slice(k, k + 256)
+                nc.gpsimd.tensor_tensor(out=res[:, cols], in0=raw[:, cols], in1=hg[item[0]][:, item[1], cols], op=ALU.add)
+            return (item[0], item[1], res)
+
+        def v_hold(g):
+            nc.vector.tensor_copy(out=h_grp[:, g], in_=h_raw[:, g].rearrange("p j w -> p w j"))
+
+        def v_hold_q(g):
+            nc.vector.quantize_mx(
+                out=h_codes[:, g].bitcast(E4), scales=h_sc[:, g], in_=h_grp[:, g].rearrange("p w j -> p (w j)")
+            )
+
+        with tc.manual_schedule():
+            nc.vector.memset(ca_raw[:].bitcast(I32), 0)
+            for c in range(C):
+                zero_gs(c)
+            warm = keep.tile([P, 1], F32, name="warm")
+            nc.vector.memset(warm[:], 0.0)
+            nc.scalar.activation(out=warm[:], in_=warm[:], func=ACT.Identity, scale=1.0)
+            load_d(0)
+            nc.sync.dma_start(out=ca_raw[0:G, :], in_=carry.rearrange("(g k) -> g k", g=G))
+            load_gs(0)
+            load_d(1)
+            load_g(0)
+            for i in range(2, 8):
+                load_d(i)
+            load_st(0)
+            load_gs(1)
+            load_g(1)
+            load_st(1)
+            nc.sync.dma_start(out=h_raw[:], in_=hold.rearrange("(g p j) w -> p g j w", g=G, j=4))
+            load_hg(0)
+            load_gs(2)
+            load_g(2)
+            load_st(2)
+            load_hg(1)
+            load_gs(3)
+            load_g(3)
+            load_st(3)
+            load_hg(2)
+            load_hg(3)
+
+            def t_d(i):
+                t_delta(i)
+                s_delta(i)
+                v_delta(i)
+
+            t_d(0)
+            t_d(1)
+            t_carry()
+            mx1(0, 0)
+            t_d(2)
+            t_d(3)
+            mx1(0, 1)
+            mx1(0, 2)
+            t_d(4)
+            t_d(5)
+            mx1(0, 3)
+            t_stress(0, 0, "out_ps", 2)
+            mx1(0, 4)
+            v_mul(0, 0, 0, 256)
+            t_d(6)
+            v_mul(0, 0, 256, 512)
+            mx1(0, 5)
+            t_d(7)
+            v_quant(0, 0, 0)
+            v_quant(0, 0, 1)
+            mx1(0, 6)
+            reorder(1, 0, 0)
+            v_hold(0)
+            reorder(1, 0, 1)
+            mx1(0, 7)
+            reorder(1, 1, 0)
+            t_stress(0, 1, "tr", 4)
+            reorder(1, 1, 1)
+
+            for c in range(1, C):
+                for i in range(4):
+                    mx1(c, i)
+                    if c + 1 < C and i in (1, 3):
+                        reorder(c + 1, 0, i // 2)
+                v_mul(c - 1, 1, 0, 256)
+                v_mul(c - 1, 1, 256, 512)
+                v_quant(c - 1, 1, 0)
+                if c == 1:
+                    v_hold(1)
+                    v_quant(c - 1, 1, 1)
+                    v_hold_q(0)
+                    v_hold_q(1)
+                else:
+                    v_quant(c - 1, 1, 1)
+                t_stress(c, 0, "tr", 4)
+                t_stress(c, 1, "tr", 4)
+                outs = []
+                if c == 2:
+                    outs.append(mx2(c - 1, 0))
+                    outs.append(mx2(c - 1, 1))
+                for i in range(4, 8):
+                    mx1(c, i)
+                    if c == 2 and i in (5, 6):
+                        outs.append(mx2(c - 1, i - 3))
+                    if c + 1 < C and i in (5, 7):
+                        reorder(c + 1, 1, (i - 5) // 2)
+                if c == 1:
+                    outs = [mx2(c - 1, j) for j in range(J)]
+                v_mul(c, 0, 0, 256)
+                if c == 2:
+                    v_out(outs.pop(0))
+                v_mul(c, 0, 256, 512)
+                if c == 2:
+                    v_out(outs.pop(0))
+                v_quant(c, 0, 0)
+                if c < 3:
+                    v_out(outs.pop(0))
+                v_quant(c, 0, 1)
+                while outs:
+                    v_out(outs.pop(0))
+            c = C - 1
+            held = []
+            for j in range(J):
+                item = mx2(c - 1, j)
+                held.append(g_add(item, s_evac(item)))
+            accs = []
+            for j in range(J):
+                if j < 2:
+                    acc = psum.tile([P, B], F32, name="out_ps", bufs=2)
+                else:
+                    acc = psum.tile([P, B], F32, name="tr", bufs=4)
+                accs.append((c, j, acc))
+            for j in (2, 3, 0, 1):
+                mx2_pass(c, j, 0, accs[j][2])
+            v_mul(c, 1, 0, 128)
+            v_mul(c, 1, 128, 256)
+            v_mul(c, 1, 256, 384)
+            v_quant(c, 1, 0)
+            v_mul(c, 1, 384, 512)
+            store(*held[0])
+            store(*held[1])
+            store(*held[2])
+            for j in range(J):
+                mx2_pass(c, j, 1, accs[j][2])
+                if j == 1:
+                    v_quant(c, 1, 1)
+                v_out(accs[j])
+                if j == 1:
+                    store(*held[3])

@@ -29,365 +29,336 @@ def tile_scenario_book_pnl_e3_kernel(tc, g_words, g_scales, delta, carry, stress
     with ExitStack() as ctx:
         keep = ctx.enter_context(tc.tile_pool(name="keep", bufs=1))
         work = ctx.enter_context(tc.tile_pool(name="work", bufs=3))
-        psum = ctx.enter_context(tc.psum_pool(name="psum", bufs=2))
+        psum = ctx.enter_context(tc.psum_pool(name="psum", bufs=1))
 
         ident = keep.tile([P, P], F32, name="ident")
         make_identity(nc, ident[:])
+        banks = [psum.tile([P, 512], F32, name="bank%d" % k) for k in range(8)]
 
-        d_raw = []
-        for i in range(8):
-            d_raw.append(keep.tile([P, F], BF16, name="d_raw%d" % i))
-        gw = []
-        st = []
-        hg = []
-        for c in range(C):
-            gw.append(keep.tile([P, A, SC], U32, name="gw%d" % c, align_bytes=64))
-            st.append(keep.tile([P, J, I], BF16, name="st%d" % c))
-            hg.append(keep.tile([P, J, B], BF16, name="hg%d" % c))
-        gs = []
-        for c in range(C):
-            gs.append(keep.tile([P, A, SC], U8, name="gs%d" % c, align_bytes=64))
-        h_raw = keep.tile([P, G, 4, B], BF16, name="h_raw")
-        h_grp = keep.tile([P, G, B, 4], BF16, name="h_grp", align_bytes=64)
+        d_raw = [keep.tile([P, F], BF16, name="d_raw%d" % i) for i in range(8)]
+        gw = [keep.tile([P, A, SC], U32, name="gw%d" % c, align_bytes=64) for c in range(C)]
+        st = [keep.tile([P, 2, I], BF16, name="st%d" % k) for k in range(S // (2 * P))]
+        hg = [keep.tile([P, J, B], BF16, name="hg%d" % c) for c in range(C)]
+        gs_first = keep.tile([P, A, SC], U8, name="gs_first", align_bytes=64)
+        gs_rest = keep.tile([P, A, S - SC], U8, name="gs_rest", align_bytes=64)
+        h_raw = [keep.tile([P, 4, B], BF16, name="h_raw%d" % g) for g in range(G)]
+        h_grp = [keep.tile([P, B, 4], BF16, name="h_grp%d" % g, align_bytes=64) for g in range(G)]
         h_codes = keep.tile([P, G, B], U32, name="h_codes", align_bytes=64)
         h_sc = keep.tile([P, G, B], U8, name="h_sc", align_bytes=64)
-        ca_raw = keep.tile([P, 512], BF16, name="ca_raw")
+        ca_raw = keep.tile([P, G, 16], BF16, name="ca_raw")
         ca = keep.tile([P, G, 4], F32, name="ca")
-        d_codes = []
-        d_sc = []
-        for i in range(8):
-            d_codes.append(keep.tile([P, A, P], U32, name="d_codes%d" % i, align_bytes=64))
-            d_sc.append(keep.tile([P, A, P], U8, name="d_sc%d" % i, align_bytes=64))
+        d_codes = [keep.tile([P, A, P], U32, name="d_codes%d" % i, align_bytes=64) for i in range(8)]
+        d_sc = [keep.tile([P, A, P], U8, name="d_sc%d" % i, align_bytes=64) for i in range(8)]
 
         d_view = delta.rearrange("(g m t) k -> g t m k", g=G, t=4)
         gw_view = g_words.rearrange("g p n t -> p g (n t)")
         gs_view = g_scales.bitcast(I32).rearrange("a r n -> r a n")
-        st_view = stress.rearrange("(c j p) i -> c p j i", c=C, p=P)
+        st_view = stress.rearrange("(k j p) i -> k p j i", j=2, p=P)
         hg_view = hedge.rearrange("(c j p) b -> c p j b", c=C, p=P)
+        h_view = hold.rearrange("(g p j) w -> g p j w", g=G, j=4)
 
         units = {}
-        stress_t = {}
         st_re = {}
+        st_bank = {}
         pnl = {}
         pnl_codes = {}
         pnl_sc = {}
-        d_bank = {}
         d_grp = {}
+        acc_out = {}
+        unit_turn = [0]
 
         def load_d(i):
             nc.sync.dma_start(out=d_raw[i][:], in_=d_view[i // 4, i % 4])
 
-        def load_g(c):
-            nc.sync.dma_start(out=gw[c][:].bitcast(I32), in_=gw_view[:, :, 2048 * c : 2048 * (c + 1)].bitcast(I32))
+        def load_g(c, lo, hi):
+            nc.sync.dma_start(
+                out=gw[c][:, lo:hi].bitcast(I32), in_=gw_view[:, lo:hi, 2048 * c : 2048 * (c + 1)].bitcast(I32)
+            )
 
-        def load_st(c):
-            nc.sync.dma_start(out=st[c][:], in_=st_view[c])
+        def load_st(k):
+            nc.sync.dma_start(out=st[k][:], in_=st_view[k])
 
         def load_hg(c):
             nc.sync.dma_start(out=hg[c][:], in_=hg_view[c])
 
-        def load_gs(c):
+        def load_h(g):
+            nc.sync.dma_start(out=h_raw[g][:], in_=h_view[g])
+
+        def load_gs(plane, lo, hi):
             for q in range(4):
                 nc.sync.dma_start(
-                    out=gs[c][32 * q : 32 * q + 4].bitcast(I32), in_=gs_view[4 * q : 4 * q + 4, :, P * c : P * (c + 1)]
+                    out=plane[32 * q : 32 * q + 4].bitcast(I32), in_=gs_view[4 * q : 4 * q + 4, :, lo // 4 : hi // 4]
                 )
 
-        def zero_gs(c):
-            nc.vector.memset(gs[c][:].rearrange("p a n -> p (a n)").bitcast(I32), 0)
+        def unit_bank(pool_banks):
+            k = pool_banks[unit_turn[0] % len(pool_banks)]
+            unit_turn[0] = unit_turn[0] + 1
+            return banks[k]
 
-        def t_carry():
-            bank = psum.tile([P, 2, P], F32, name="out_ps", bufs=2)
-            words = ca_raw[:].bitcast(F32)
-            for u in range(2):
-                nc.tensor.transpose(bank[:, u, :], words[:, u : 256 : 2], ident[:])
-            nc.vector.tensor_copy(
-                out=ca[:].rearrange("p g (u e) -> p g u e", u=2),
-                in_=bank[:, :, 0:G].bitcast(BF16).rearrange("p u (g e) -> p g u e", e=2),
-            )
+        def d_banks(i):
+            one = banks[4 + 2 * (i % 2)][:, 0:256].rearrange("p (u m) -> p u m", u=2)
+            two = banks[5 + 2 * (i % 2)][:].rearrange("p (a u m) -> p a u m", a=2, u=2)
+            return one, two
 
         def t_delta(i):
-            bank_a = psum.tile([P, 2, 2, P], F32, name="tr", bufs=4)
-            bank_b = psum.tile([P, 1, 2, P], F32, name="tr", bufs=4)
+            one, two = d_banks(i)
             words = d_raw[i][:].bitcast(F32)
             for a in range(A):
                 for u in range(2):
-                    dst = bank_a[:, a, u, :] if a < 2 else bank_b[:, 0, u, :]
+                    dst = one[:, u, :] if a == 0 else two[:, a - 1, u, :]
                     nc.tensor.transpose(dst, words[:, 256 * a + u : 256 * (a + 1) : 2], ident[:])
+
+        def c_delta(i, first_on_scalar):
+            one, two = d_banks(i)
             grp = work.tile([P, A, P, 4], BF16, name="d_grp", align_bytes=64)
-            d_bank[i] = (bank_a, bank_b)
             d_grp[i] = grp
-
-        def s_delta(i):
+            first_copy = nc.scalar.copy if first_on_scalar else nc.vector.tensor_copy
+            first_copy(
+                out=grp[:, 0].rearrange("p m t -> p (m t)").bitcast(F32).rearrange("p (m u) -> p m u", u=2),
+                in_=one.rearrange("p u m -> p m u"),
+            )
             nc.scalar.copy(
-                out=d_grp[i][:, 0:2].rearrange("p a m t -> p a (m t)").bitcast(F32).rearrange("p a (m u) -> p a m u", u=2),
-                in_=d_bank[i][0][:].rearrange("p a u m -> p a m u"),
+                out=grp[:, 1:3].rearrange("p a m t -> p a (m t)").bitcast(F32).rearrange("p a (m u) -> p a m u", u=2),
+                in_=two.rearrange("p a u m -> p a m u"),
             )
 
-        def v_delta(i):
-            grp = d_grp[i]
-            nc.vector.tensor_copy(
-                out=grp[:, 2:3].rearrange("p a m t -> p a (m t)").bitcast(F32).rearrange("p a (m u) -> p a m u", u=2),
-                in_=d_bank[i][1][:].rearrange("p a u m -> p a m u"),
-            )
+        def q_delta(i, lo, hi):
             nc.vector.quantize_mx(
-                out=d_codes[i][:, 0:2].rearrange("p a m -> p (a m)").bitcast(E4),
-                scales=d_sc[i][:, 0:2].rearrange("p a m -> p (a m)"),
-                in_=grp[:, 0:2].rearrange("p a m t -> p (a m t)"),
-            )
-            nc.vector.quantize_mx(
-                out=d_codes[i][:, 2].bitcast(E4), scales=d_sc[i][:, 2], in_=grp[:, 2].rearrange("p m t -> p (m t)")
+                out=d_codes[i][:, lo:hi].rearrange("p a m -> p (a m)").bitcast(E4),
+                scales=d_sc[i][:, lo:hi].rearrange("p a m -> p (a m)"),
+                in_=d_grp[i][:, lo:hi].rearrange("p a m t -> p (a m t)"),
             )
 
-        def mx1(c, i):
-            acc = psum.tile([P, SC], F32, name="unit_ps", bufs=2)
+        def mx1(s0, n, i, pool_banks):
+            c, lo = s0 // SC, s0 % SC
+            acc = unit_bank(pool_banks)[:, 0:n]
             for a in range(A):
                 nc.tensor.matmul_mx(
-                    out=acc[:],
+                    out=acc,
                     lhsT=d_codes[i][:, a, :].bitcast(E4),
                     lhsT_scale=d_sc[i][:, a, :],
-                    rhs=gw[c][:, a, :].bitcast(E5),
-                    rhs_scale=gs[c][:, a, :],
+                    rhs=gw[c][:, a, lo : lo + n].bitcast(E5),
+                    rhs_scale=gs_first[:, a, s0 : s0 + n] if c == 0 else gs_rest[:, a, s0 - SC : s0 - SC + n],
                     start=(a == 0),
                     stop=(a == A - 1),
                 )
             g, t = i // 4, i % 4
             if t == 0:
-                units[(c, g)] = work.tile([P, 4, SC], F32, name="unit")
+                units[(s0, g)] = work.tile([P, 4, n], F32, name="unit")
             nc.scalar.activation(
-                out=units[(c, g)][:, t, :], in_=acc[:], func=ACT.Identity, bias=ca[:, g, t : t + 1], scale=1.0
+                out=units[(s0, g)][:, t, :], in_=acc, func=ACT.Identity, bias=ca[:, g, t : t + 1], scale=1.0
             )
 
-        def reorder(c, g, h):
-            if g == 0 and h == 0:
-                st_re[c] = work.tile([P, G, J, 2, P], F32, name="st_re", bufs=2)
-            nc.scalar.copy(
-                out=st_re[c][:, g, 2 * h : 2 * h + 2],
-                in_=st[c][:].bitcast(F32).rearrange("p j (g m u) -> p g j u m", g=G, u=2)[:, g, 2 * h : 2 * h + 2],
-            )
+        def reorder(j, g):
+            st_re[(j, g)] = work.tile([P, 2, 2, P], F32, name="st_re", bufs=6)
+            words = st[j // 2][:].bitcast(F32).rearrange("p j (g m u) -> p g j u m", g=G, u=2)
+            nc.scalar.copy(out=st_re[(j, g)][:], in_=words[:, g])
 
-        def t_stress(c, g, tag, bufs):
-            banks = []
-            for h in range(2):
-                bank = psum.tile([P, 2, 2, P], F32, name=tag, bufs=bufs)
-                for jj in range(2):
-                    for u in range(2):
-                        if c == 0:
-                            words = st[c][:, 2 * h + jj, :].bitcast(F32)[:, 256 * g + u : 256 * (g + 1) : 2]
-                        else:
-                            words = st_re[c][:, g, 2 * h + jj, u, :]
-                        nc.tensor.transpose(bank[:, u, jj, :], words, ident[:])
-                banks.append(bank)
-            stress_t[(c, g)] = banks
-            pnl[(c, g)] = work.tile([P, SC, 4], BF16, name="pnl", align_bytes=64, bufs=2)
-            pnl_codes[(c, g)] = work.tile([P, SC], U32, name="pnl_codes", align_bytes=64, bufs=4)
-            pnl_sc[(c, g)] = work.tile([P, SC], U8, name="pnl_sc", align_bytes=64, bufs=4)
+        def t_stress(j, g, k, half):
+            dst = banks[k][:, 256 * half : 256 * (half + 1)].rearrange("p (u s) -> p u s", u=2)
+            for u in range(2):
+                if (j - j % 2, g) in st_re:
+                    words = st_re[(j - j % 2, g)][:, j % 2, u, :]
+                else:
+                    words = st[j // 2][:, j % 2, :].bitcast(F32)[:, 256 * g + u : 256 * (g + 1) : 2]
+                nc.tensor.transpose(dst[:, u, :], words, ident[:])
+            st_bank[(j, g)] = dst
 
-        def v_mul(c, g, lo, hi):
-            h = lo // 256
-            cols = slice(lo, hi)
-            bank = stress_t[(c, g)][h]
+        def t_pair(j, g, k):
+            t_stress(j, g, k, 0)
+            t_stress(j + 1, g, k, 1)
+
+        def v_mul(j, g):
+            s0 = 2 * P * (j // 2)
+            if j % 2 == 0:
+                pnl[(s0, g)] = work.tile([P, 2 * P, 4], BF16, name="pnl", align_bytes=64)
+            u0 = 0 if j < J else s0
+            cols = slice(j * P - u0, j * P - u0 + P)
             nc.vector.tensor_tensor(
-                out=pnl[(c, g)][:, cols, :].rearrange("p s (u e) -> p s u e", u=2),
-                in0=units[(c, g)][:, :, cols].rearrange("p (u e) s -> p s u e", u=2),
-                in1=bank[:].rearrange("p u j s -> p u (j s)")[:, :, lo - 256 * h : hi - 256 * h]
-                .bitcast(BF16)
-                .rearrange("p u (s e) -> p s u e", e=2),
+                out=pnl[(s0, g)][:, P * (j % 2) : P * (j % 2 + 1), :].rearrange("p s (u e) -> p s u e", u=2),
+                in0=units[(u0, g)][:, :, cols].rearrange("p (u e) s -> p s u e", u=2),
+                in1=st_bank[(j, g)].bitcast(BF16).rearrange("p u (s e) -> p s u e", e=2),
                 op=ALU.mult,
             )
 
-        def v_quant(c, g, h):
-            cols = slice(256 * h, 256 * (h + 1))
+        def v_quant(s0, g, lo=0, hi=2 * P):
+            if lo == 0:
+                pnl_codes[(s0, g)] = work.tile([P, 2 * P], U32, name="pnl_codes", align_bytes=64, bufs=8)
+                pnl_sc[(s0, g)] = work.tile([P, 2 * P], U8, name="pnl_sc", align_bytes=64, bufs=8)
             nc.vector.quantize_mx(
-                out=pnl_codes[(c, g)][:, cols].bitcast(E5),
-                scales=pnl_sc[(c, g)][:, cols],
-                in_=pnl[(c, g)][:, cols, :].rearrange("p s t -> p (s t)"),
+                out=pnl_codes[(s0, g)][:, lo:hi].bitcast(E5),
+                scales=pnl_sc[(s0, g)][:, lo:hi],
+                in_=pnl[(s0, g)][:, lo:hi, :].rearrange("p s t -> p (s t)"),
             )
 
-        def mx2_pass(c, j, g, acc):
-            cols = slice(P * j, P * (j + 1))
+        def mx2_pass(j, g):
+            acc_out[j] = banks[2 + j % 2] if j < S // P - 2 else banks[7 - 2 * (j % 2)]
+            s0 = 2 * P * (j // 2)
+            cols = slice(P * (j % 2), P * (j % 2 + 1))
             nc.tensor.matmul_mx(
-                out=acc[:],
-                lhsT=pnl_codes[(c, g)][:, cols].bitcast(E5),
-                lhsT_scale=pnl_sc[(c, g)][:, cols],
+                out=acc_out[j][:],
+                lhsT=pnl_codes[(s0, g)][:, cols].bitcast(E5),
+                lhsT_scale=pnl_sc[(s0, g)][:, cols],
                 rhs=h_codes[:, g, :].bitcast(E4),
                 rhs_scale=h_sc[:, g, :],
                 start=(g == 0),
                 stop=(g == G - 1),
             )
 
-        def mx2(c, j):
-            acc = psum.tile([P, B], F32, name="out_ps", bufs=2)
+        def mx2(j):
             for g in range(G):
-                mx2_pass(c, j, g, acc)
-            return (c, j, acc)
+                mx2_pass(j, g)
 
-        def v_out(item):
-            c, j, acc = item
+        def v_out(j):
             res = work.tile([P, B], F32, name="res", bufs=5)
-            nc.vector.tensor_tensor(out=res[:], in0=acc[:], in1=hg[c][:, j, :], op=ALU.add)
-            s0 = SC * c + P * j
-            nc.sync.dma_start(out=out[s0 : s0 + P, :], in_=res[:])
+            nc.vector.tensor_tensor(out=res[:], in0=acc_out[j][:], in1=hg[j // J][:, j % J, :], op=ALU.add)
+            nc.sync.dma_start(out=out[P * j : P * (j + 1), :], in_=res[:])
 
-        def store(c, j, res):
-            s0 = SC * c + P * j
-            nc.sync.dma_start(out=out[s0 : s0 + P, :], in_=res[:])
-
-        def s_evac(item):
-            raw = work.tile([P, B], F32, name="res_raw", bufs=4)
-            nc.scalar.copy(out=raw[:], in_=item[2][:])
-            return raw
-
-        def v_add(item, raw):
-            res = work.tile([P, B], F32, name="res", bufs=5)
-            nc.vector.tensor_tensor(out=res[:], in0=raw[:], in1=hg[item[0]][:, item[1], :], op=ALU.add)
-            store(item[0], item[1], res)
-
-        def g_add(item, raw):
-            res = work.tile([P, B], F32, name="res_g", bufs=4)
-            for k in range(0, B, 256):
-                cols = slice(k, k + 256)
-                nc.gpsimd.tensor_tensor(out=res[:, cols], in0=raw[:, cols], in1=hg[item[0]][:, item[1], cols], op=ALU.add)
-            return (item[0], item[1], res)
-
-        def v_hold(g):
-            nc.vector.tensor_copy(out=h_grp[:, g], in_=h_raw[:, g].rearrange("p j w -> p w j"))
+        def v_hold(g, h):
+            cols = slice(256 * h, 256 * (h + 1))
+            nc.vector.tensor_copy(
+                out=h_grp[g][:, cols, :].rearrange("p (c i) t -> p c t i", i=4),
+                in_=h_raw[g][:, :, cols].rearrange("p t (c i) -> p c t i", i=4),
+            )
 
         def v_hold_q(g):
             nc.vector.quantize_mx(
-                out=h_codes[:, g].bitcast(E4), scales=h_sc[:, g], in_=h_grp[:, g].rearrange("p w j -> p (w j)")
+                out=h_codes[:, g].bitcast(E4), scales=h_sc[:, g], in_=h_grp[g][:].rearrange("p w j -> p (w j)")
             )
 
         with tc.manual_schedule():
-            nc.vector.memset(ca_raw[:].bitcast(I32), 0)
-            for c in range(C):
-                zero_gs(c)
-            warm = keep.tile([P, 1], F32, name="warm")
-            nc.vector.memset(warm[:], 0.0)
-            nc.scalar.activation(out=warm[:], in_=warm[:], func=ACT.Identity, scale=1.0)
+            nc.scalar.dma_start(out=ca_raw[:, :, 0:4], in_=carry.rearrange("(g p t) -> p g t", g=G, t=4))
+            nc.vector.memset(gs_first[:].rearrange("p a n -> p (a n)").bitcast(I32), 0)
+            nc.vector.memset(gs_rest[:].rearrange("p a n -> p (a n)").bitcast(I32), 0)
+            nc.scalar.activation(out=ca[:], in_=ca_raw[:, :, 0:4], func=ACT.Identity, scale=1.0)
             load_d(0)
-            nc.sync.dma_start(out=ca_raw[0:G, :], in_=carry.rearrange("(g k) -> g k", g=G))
-            load_gs(0)
             load_d(1)
-            load_g(0)
-            for i in range(2, 8):
-                load_d(i)
+            load_gs(gs_first, 0, SC)
+            load_g(0, 0, 1)
+            load_g(0, 1, A)
+            load_d(2)
+            load_h(0)
+            load_d(3)
+            load_h(1)
+            load_d(4)
             load_st(0)
-            load_gs(1)
-            load_g(1)
+            load_d(5)
             load_st(1)
-            nc.sync.dma_start(out=h_raw[:], in_=hold.rearrange("(g p j) w -> p g j w", g=G, j=4))
-            load_hg(0)
-            load_gs(2)
-            load_g(2)
+            load_d(6)
+            load_d(7)
             load_st(2)
-            load_hg(1)
-            load_gs(3)
-            load_g(3)
+            load_gs(gs_rest, SC, S)
+            load_g(1, 0, A)
             load_st(3)
-            load_hg(2)
-            load_hg(3)
+            load_hg(0)
+            for c in range(2, C):
+                load_st(2 * c)
+                load_g(c, 0, A)
+                load_st(2 * c + 1)
+                load_hg(c - 1)
+            load_hg(C - 1)
 
-            def t_d(i):
+            for i in range(2):
                 t_delta(i)
-                s_delta(i)
-                v_delta(i)
-
-            t_d(0)
-            t_d(1)
-            t_carry()
-            mx1(0, 0)
-            t_d(2)
-            t_d(3)
-            mx1(0, 1)
-            mx1(0, 2)
-            t_d(4)
-            t_d(5)
-            mx1(0, 3)
-            t_stress(0, 0, "out_ps", 2)
-            mx1(0, 4)
-            v_mul(0, 0, 0, 256)
-            t_d(6)
-            v_mul(0, 0, 256, 512)
-            mx1(0, 5)
-            t_d(7)
-            v_quant(0, 0, 0)
-            v_quant(0, 0, 1)
-            mx1(0, 6)
-            reorder(1, 0, 0)
-            v_hold(0)
-            reorder(1, 0, 1)
-            mx1(0, 7)
-            reorder(1, 1, 0)
-            t_stress(0, 1, "tr", 4)
-            reorder(1, 1, 1)
-
-            for c in range(1, C):
-                for i in range(4):
-                    mx1(c, i)
-                    if c + 1 < C and i in (1, 3):
-                        reorder(c + 1, 0, i // 2)
-                v_mul(c - 1, 1, 0, 256)
-                v_mul(c - 1, 1, 256, 512)
-                v_quant(c - 1, 1, 0)
-                if c == 1:
-                    v_hold(1)
-                    v_quant(c - 1, 1, 1)
+                c_delta(i, False)
+                q_delta(i, 0, 1)
+                q_delta(i, 1, 3)
+            for i in range(7):
+                mx1(0, SC, i, [0, 1])
+                if i == 4:
+                    reorder(0, 1)
+                if i + 2 < 8:
+                    t_delta(i + 2)
+                if i in (3, 4):
+                    t_pair(2 * (i - 3), 0, 2 + (i - 3))
+                if i in (4, 5):
+                    v_mul(2 * (i - 4), 0)
+                if i + 2 < 8:
+                    c_delta(i + 2, i < 4)
+                if i == 0:
+                    v_hold(0, 0)
+                    v_hold(0, 1)
+                if i == 1:
                     v_hold_q(0)
+                    v_hold(1, 0)
+                if i == 2:
+                    v_hold(1, 1)
+                if i == 3:
                     v_hold_q(1)
-                else:
-                    v_quant(c - 1, 1, 1)
-                t_stress(c, 0, "tr", 4)
-                t_stress(c, 1, "tr", 4)
-                outs = []
-                if c == 2:
-                    outs.append(mx2(c - 1, 0))
-                    outs.append(mx2(c - 1, 1))
-                for i in range(4, 8):
-                    mx1(c, i)
-                    if c == 2 and i in (5, 6):
-                        outs.append(mx2(c - 1, i - 3))
-                    if c + 1 < C and i in (5, 7):
-                        reorder(c + 1, 1, (i - 5) // 2)
-                if c == 1:
-                    outs = [mx2(c - 1, j) for j in range(J)]
-                v_mul(c, 0, 0, 256)
-                if c == 2:
-                    v_out(outs.pop(0))
-                v_mul(c, 0, 256, 512)
-                if c == 2:
-                    v_out(outs.pop(0))
-                v_quant(c, 0, 0)
-                if c < 3:
-                    v_out(outs.pop(0))
-                v_quant(c, 0, 1)
-                while outs:
-                    v_out(outs.pop(0))
-            c = C - 1
-            held = []
-            for j in range(J):
-                item = mx2(c - 1, j)
-                held.append(g_add(item, s_evac(item)))
-            accs = []
-            for j in range(J):
-                if j < 2:
-                    acc = psum.tile([P, B], F32, name="out_ps", bufs=2)
-                else:
-                    acc = psum.tile([P, B], F32, name="tr", bufs=4)
-                accs.append((c, j, acc))
-            for j in (2, 3, 0, 1):
-                mx2_pass(c, j, 0, accs[j][2])
-            v_mul(c, 1, 0, 128)
-            v_mul(c, 1, 128, 256)
-            v_mul(c, 1, 256, 384)
-            v_quant(c, 1, 0)
-            v_mul(c, 1, 384, 512)
-            store(*held[0])
-            store(*held[1])
-            store(*held[2])
-            for j in range(J):
-                mx2_pass(c, j, 1, accs[j][2])
-                if j == 1:
-                    v_quant(c, 1, 1)
-                v_out(accs[j])
-                if j == 1:
-                    store(*held[3])
+                if i == 4:
+                    v_mul(1, 0)
+                if i == 5:
+                    v_quant(0, 0)
+                if i + 2 < 8:
+                    q_delta(i + 2, 0, 1)
+                    q_delta(i + 2, 1, 3)
+            v_mul(3, 0)
+            reorder(2, 1)
+
+            steps = [(0, 1), (2, 1)] + [(j, g) for j in range(J, S // P, 2) for g in range(G)]
+            three = [4, 1, 0]
+
+            def t_run(k):
+                for m in range(k, min(k + 3, len(steps))):
+                    t_pair(steps[m][0], steps[m][1], 5 + m % 3)
+
+            unit_turn[0] = 0
+            mx1(SC, 2 * P, 0, three)
+            mx1(SC, 2 * P, 1, three)
+            reorder(4, 0)
+            mx1(0, SC, 7, three)
+            v_quant(2 * P, 0)
+            t_run(0)
+            reorder(4, 1)
+            reorder(6, 0)
+            mx1(SC, 2 * P, 2, three)
+            mx1(SC, 2 * P, 3, three)
+            v_mul(0, 1)
+            v_mul(1, 1)
+            v_mul(2, 1)
+            v_quant(0, 1)
+            v_mul(3, 1)
+            ready = [0, 1, 2, 3]
+            pending = []
+            for k in range(3, len(steps)):
+                j, g = steps[k]
+                jb, gb = steps[k - 1]
+                count = 2 if len(ready) > 2 or k == len(steps) - 1 else 1
+                take = ready[:count]
+                ready = ready[count:]
+                for t in range(4):
+                    mx1(P * j, 2 * P, 4 * g + t, three)
+                    if t == 1 and k < len(steps) - 2:
+                        reorder(*steps[k + 2])
+                    if k == 4 and t == 1:
+                        v_out(pending.pop(0))
+                        t_run(3)
+                    if t == (1 if k == 4 else 0):
+                        v_mul(jb, gb)
+                        if k == 3:
+                            v_quant(2 * P, 1)
+                        while pending:
+                            v_out(pending.pop(0))
+                        v_mul(jb + 1, gb)
+                    if take and (t == 3 or t == (2 if k == 3 else 1)):
+                        mx2(take[0])
+                        pending.append(take.pop(0))
+                        if t < 3:
+                            v_out(pending.pop(0))
+                            v_quant(P * jb, gb)
+                if gb == G - 1:
+                    ready.extend([jb, jb + 1])
+                if k % 3 == 0 and k > 3:
+                    t_run(k)
+            j, g = steps[-1]
+            mx2_pass(j, 0)
+            mx2_pass(j + 1, 0)
+            v_mul(j, g)
+            v_out(pending.pop(0))
+            v_quant(P * j, g, 0, P)
+            mx2_pass(j, g)
+            v_mul(j + 1, g)
+            v_quant(P * j, g, P, 2 * P)
+            mx2_pass(j + 1, g)
+            v_out(j)
+            v_out(j + 1)

@@ -155,13 +155,13 @@ def tile_scenario_book_pnl_e3_kernel(tc, g_words, g_scales, delta, carry, stress
             nc.scalar.copy(out=st_re[(j, g)][:], in_=words[:, g])
 
         def t_stress(j, g, k, half):
-            dst = banks[k][:, 256 * half : 256 * (half + 1)].rearrange("p (u s) -> p u s", u=2)
+            dst = banks[k][:, 256 * half : 256 * (half + 1)]
             for u in range(2):
                 if (j - j % 2, g) in st_re:
                     words = st_re[(j - j % 2, g)][:, j % 2, u, :]
                 else:
                     words = st[j // 2][:, j % 2, :].bitcast(F32)[:, 256 * g + u : 256 * (g + 1) : 2]
-                nc.tensor.transpose(dst[:, u, :], words, ident[:])
+                nc.tensor.transpose(dst.rearrange("p (c u i) -> p u c i", u=2, i=4)[:, u], words, ident[:])
             st_bank[(j, g)] = dst
 
         def t_pair(j, g, k):
@@ -175,9 +175,9 @@ def tile_scenario_book_pnl_e3_kernel(tc, g_words, g_scales, delta, carry, stress
             u0 = 0 if j < J else s0
             cols = slice(j * P - u0, j * P - u0 + P)
             nc.vector.tensor_tensor(
-                out=pnl[(s0, g)][:, P * (j % 2) : P * (j % 2 + 1), :].rearrange("p s (u e) -> p s u e", u=2),
-                in0=units[(u0, g)][:, :, cols].rearrange("p (u e) s -> p s u e", u=2),
-                in1=st_bank[(j, g)].bitcast(BF16).rearrange("p u (s e) -> p s u e", e=2),
+                out=pnl[(s0, g)][:, P * (j % 2) : P * (j % 2 + 1), :].rearrange("p (c i) (u e) -> p c u e i", i=4, u=2),
+                in0=units[(u0, g)][:, :, cols].rearrange("p (u e) (c i) -> p c u e i", i=4, u=2),
+                in1=st_bank[(j, g)].bitcast(BF16).rearrange("p (c u i e) -> p c u e i", u=2, i=4, e=2),
                 op=ALU.mult,
             )
 

@@ -64,6 +64,7 @@ def tile_scenario_book_pnl_e3_kernel(tc, g_words, g_scales, delta, carry, stress
         pnl_codes = {}
         pnl_sc = {}
         d_grp = {}
+        d_re = {}
         acc_out = {}
         unit_turn = [0]
 
@@ -102,11 +103,21 @@ def tile_scenario_book_pnl_e3_kernel(tc, g_words, g_scales, delta, carry, stress
 
         def t_delta(i):
             one, two = d_banks(i)
-            words = d_raw[i][:].bitcast(F32)
             for a in range(A):
                 for u in range(2):
                     dst = one[:, u, :] if a == 0 else two[:, a - 1, u, :]
-                    nc.tensor.transpose(dst, words[:, 256 * a + u : 256 * (a + 1) : 2], ident[:])
+                    if i in d_re:
+                        words = d_re[i][:, a, u, :]
+                    else:
+                        words = d_raw[i][:].bitcast(F32)[:, 256 * a + u : 256 * (a + 1) : 2]
+                    nc.tensor.transpose(dst, words, ident[:])
+
+        def r_delta(i):
+            d_re[i] = work.tile([P, A, 2, P], F32, name="d_re", bufs=3)
+            nc.vector.tensor_copy(
+                out=d_re[i][:].rearrange("p a u (v m) -> p v a u m", v=2),
+                in_=d_raw[i][:].bitcast(F32).rearrange("p (a v m u) -> p v a u m", a=A, v=2, u=2),
+            )
 
         def c_delta(i, first_on_scalar):
             one, two = d_banks(i)
@@ -130,8 +141,19 @@ def tile_scenario_book_pnl_e3_kernel(tc, g_words, g_scales, delta, carry, stress
             )
 
         def mx1(s0, n, i, pool_banks):
-            c, lo = s0 // SC, s0 % SC
             acc = unit_bank(pool_banks)[:, 0:n]
+            mx1_passes(s0, n, i, acc)
+            s_unit(s0, n, i, acc)
+
+        def mx1_two(s0, i, pool_banks):
+            bank = unit_bank(pool_banks)
+            for m in range(2):
+                mx1_passes(s0, P, i + m, bank[:, P * m : P * (m + 1)])
+            for m in range(2):
+                s_unit(s0, P, i + m, bank[:, P * m : P * (m + 1)])
+
+        def mx1_passes(s0, n, i, acc):
+            c, lo = s0 // SC, s0 % SC
             for a in range(A):
                 nc.tensor.matmul_mx(
                     out=acc,
@@ -142,6 +164,8 @@ def tile_scenario_book_pnl_e3_kernel(tc, g_words, g_scales, delta, carry, stress
                     start=(a == 0),
                     stop=(a == A - 1),
                 )
+
+        def s_unit(s0, n, i, acc):
             g, t = i // 4, i % 4
             if t == 0:
                 units[(s0, g)] = work.tile([P, 4, n], F32, name="unit")
@@ -149,10 +173,10 @@ def tile_scenario_book_pnl_e3_kernel(tc, g_words, g_scales, delta, carry, stress
                 out=units[(s0, g)][:, t, :], in_=acc, func=ACT.Identity, bias=ca[:, g, t : t + 1], scale=1.0
             )
 
-        def reorder(j, g):
+        def reorder(j, g, copy=nc.scalar.copy):
             st_re[(j, g)] = work.tile([P, 2, 2, P], F32, name="st_re", bufs=6)
             words = st[j // 2][:].bitcast(F32).rearrange("p j (g m u) -> p g j u m", g=G, u=2)
-            nc.scalar.copy(out=st_re[(j, g)][:], in_=words[:, g])
+            copy(out=st_re[(j, g)][:], in_=words[:, g])
 
         def t_stress(j, g, k, half):
             dst = banks[k][:, 256 * half : 256 * (half + 1)]
@@ -170,9 +194,9 @@ def tile_scenario_book_pnl_e3_kernel(tc, g_words, g_scales, delta, carry, stress
 
         def v_mul(j, g):
             s0 = 2 * P * (j // 2)
-            if j % 2 == 0:
-                pnl[(s0, g)] = work.tile([P, 2 * P, 4], BF16, name="pnl", align_bytes=64)
-            u0 = 0 if j < J else s0
+            if (s0, g) not in pnl:
+                pnl[(s0, g)] = work.tile([P, 2 * P, 4], BF16, name="pnl", align_bytes=64, bufs=4)
+            u0 = 0 if j < J else s0 if j < S // P - 2 else P * j
             cols = slice(j * P - u0, j * P - u0 + P)
             nc.vector.tensor_tensor(
                 out=pnl[(s0, g)][:, P * (j % 2) : P * (j % 2 + 1), :].rearrange("p (c i) (u e) -> p c u e i", i=4, u=2),
@@ -183,8 +207,8 @@ def tile_scenario_book_pnl_e3_kernel(tc, g_words, g_scales, delta, carry, stress
 
         def v_quant(s0, g, lo=0, hi=2 * P):
             if lo == 0:
-                pnl_codes[(s0, g)] = work.tile([P, 2 * P], U32, name="pnl_codes", align_bytes=64, bufs=8)
-                pnl_sc[(s0, g)] = work.tile([P, 2 * P], U8, name="pnl_sc", align_bytes=64, bufs=8)
+                pnl_codes[(s0, g)] = work.tile([P, 2 * P], U32, name="pnl_codes", align_bytes=64, bufs=10)
+                pnl_sc[(s0, g)] = work.tile([P, 2 * P], U8, name="pnl_sc", align_bytes=64, bufs=10)
             nc.vector.quantize_mx(
                 out=pnl_codes[(s0, g)][:, lo:hi].bitcast(E5),
                 scales=pnl_sc[(s0, g)][:, lo:hi],
@@ -192,7 +216,7 @@ def tile_scenario_book_pnl_e3_kernel(tc, g_words, g_scales, delta, carry, stress
             )
 
         def mx2_pass(j, g):
-            acc_out[j] = banks[2 + j % 2] if j < S // P - 2 else banks[7 - 2 * (j % 2)]
+            acc_out[j] = banks[2 + j % 2]
             s0 = 2 * P * (j // 2)
             cols = slice(P * (j % 2), P * (j % 2 + 1))
             nc.tensor.matmul_mx(
@@ -210,7 +234,7 @@ def tile_scenario_book_pnl_e3_kernel(tc, g_words, g_scales, delta, carry, stress
                 mx2_pass(j, g)
 
         def v_out(j):
-            res = work.tile([P, B], F32, name="res", bufs=5)
+            res = work.tile([P, B], F32, name="res", bufs=6)
             nc.vector.tensor_tensor(out=res[:], in0=acc_out[j][:], in1=hg[j // J][:, j % J, :], op=ALU.add)
             nc.sync.dma_start(out=out[P * j : P * (j + 1), :], in_=res[:])
 
@@ -237,18 +261,18 @@ def tile_scenario_book_pnl_e3_kernel(tc, g_words, g_scales, delta, carry, stress
             load_g(0, 0, 1)
             load_g(0, 1, A)
             load_d(2)
-            load_h(0)
             load_d(3)
-            load_h(1)
             load_d(4)
-            load_st(0)
+            load_h(0)
             load_d(5)
-            load_st(1)
+            load_st(0)
             load_d(6)
+            load_h(1)
             load_d(7)
-            load_st(2)
+            load_st(1)
             load_gs(gs_rest, SC, S)
             load_g(1, 0, A)
+            load_st(2)
             load_st(3)
             load_hg(0)
             for c in range(2, C):
@@ -258,6 +282,7 @@ def tile_scenario_book_pnl_e3_kernel(tc, g_words, g_scales, delta, carry, stress
                 load_hg(c - 1)
             load_hg(C - 1)
 
+            on_vector = nc.vector.tensor_copy
             for i in range(2):
                 t_delta(i)
                 c_delta(i, False)
@@ -265,100 +290,153 @@ def tile_scenario_book_pnl_e3_kernel(tc, g_words, g_scales, delta, carry, stress
                 q_delta(i, 1, 3)
             for i in range(7):
                 mx1(0, SC, i, [0, 1])
-                if i == 4:
-                    reorder(0, 1)
                 if i + 2 < 8:
                     t_delta(i + 2)
-                if i in (3, 4):
-                    t_pair(2 * (i - 3), 0, 2 + (i - 3))
                 if i in (4, 5):
-                    v_mul(2 * (i - 4), 0)
-                if i + 2 < 8:
-                    c_delta(i + 2, i < 4)
-                if i == 0:
-                    v_hold(0, 0)
-                    v_hold(0, 1)
+                    t_pair(2 * (i - 4), 0, 2 + (i - 4))
+                if i + 3 < 8:
+                    r_delta(i + 3)
                 if i == 1:
-                    v_hold_q(0)
-                    v_hold(1, 0)
+                    v_hold(0, 0)
                 if i == 2:
-                    v_hold(1, 1)
+                    v_hold(0, 1)
                 if i == 3:
-                    v_hold_q(1)
+                    reorder(0, 0, on_vector)
                 if i == 4:
-                    v_mul(1, 0)
+                    reorder(2, 0, on_vector)
                 if i == 5:
-                    v_quant(0, 0)
+                    v_mul(0, 0)
+                    v_mul(1, 0)
                 if i + 2 < 8:
+                    c_delta(i + 2, True)
                     q_delta(i + 2, 0, 1)
+                if i == 3:
+                    v_hold(1, 0)
+                if i == 4:
+                    v_hold(1, 1)
+                if i + 2 < 8:
                     q_delta(i + 2, 1, 3)
+                if i == 5:
+                    reorder(0, 1)
+            reorder(2, 1, on_vector)
+            v_mul(2, 0)
+            v_quant(0, 0)
             v_mul(3, 0)
-            reorder(2, 1)
 
             steps = [(0, 1), (2, 1)] + [(j, g) for j in range(J, S // P, 2) for g in range(G)]
-            three = [4, 1, 0]
+            three = [0, 4, 1]
 
             def t_run(k):
                 for m in range(k, min(k + 3, len(steps))):
                     t_pair(steps[m][0], steps[m][1], 5 + m % 3)
 
-            unit_turn[0] = 0
-            mx1(SC, 2 * P, 0, three)
-            mx1(SC, 2 * P, 1, three)
+            mx1(SC, 2 * P, 0, [4])
+            mx1(SC, 2 * P, 1, [5])
             reorder(4, 0)
-            mx1(0, SC, 7, three)
+            mx1(0, SC, 7, [1])
+            unit_turn[0] = 0
             v_quant(2 * P, 0)
             t_run(0)
             reorder(4, 1)
             reorder(6, 0)
             mx1(SC, 2 * P, 2, three)
             mx1(SC, 2 * P, 3, three)
-            v_mul(0, 1)
-            v_mul(1, 1)
-            v_mul(2, 1)
+            for j in range(J):
+                v_mul(j, 1)
+            for t in range(4):
+                mx1(SC, 2 * P, 4 + t, three)
+            v_mul(4, 0)
+            v_mul(5, 0)
+            mx1(SC + 2 * P, 2 * P, 0, three)
+            reorder(6, 1)
+            mx1(SC + 2 * P, 2 * P, 1, three)
+            t_run(3)
+            reorder(8, 0)
+            v_hold_q(0)
             v_quant(0, 1)
-            v_mul(3, 1)
-            ready = [0, 1, 2, 3]
+            v_hold_q(1)
+            mx1(SC + 2 * P, 2 * P, 2, three)
+            mx1(SC + 2 * P, 2 * P, 3, three)
+            v_mul(4, 1)
+            v_quant(2 * P, 1)
+            v_mul(5, 1)
+            v_quant(SC, 0)
+            v_quant(SC, 1)
+            ready = [0, 1, 2, 3, 4, 5]
             pending = []
-            for k in range(3, len(steps)):
+            for k in range(5, len(steps) - 2):
                 j, g = steps[k]
                 jb, gb = steps[k - 1]
-                count = 2 if len(ready) > 2 or k == len(steps) - 1 else 1
+                count = 2 if len(ready) > 2 or k == len(steps) - 3 else 1
                 take = ready[:count]
                 ready = ready[count:]
                 for t in range(4):
                     mx1(P * j, 2 * P, 4 * g + t, three)
-                    if t == 1 and k < len(steps) - 2:
+                    if t == 1:
                         reorder(*steps[k + 2])
-                    if k == 4 and t == 1:
-                        v_out(pending.pop(0))
-                        t_run(3)
-                    if t == (1 if k == 4 else 0):
+                    if t == 0:
                         v_mul(jb, gb)
-                        if k == 3:
-                            v_quant(2 * P, 1)
                         while pending:
                             v_out(pending.pop(0))
                         v_mul(jb + 1, gb)
-                    if take and (t == 3 or t == (2 if k == 3 else 1)):
+                    if take and t in (1, 3):
                         mx2(take[0])
                         pending.append(take.pop(0))
-                        if t < 3:
+                        if t == 1:
                             v_out(pending.pop(0))
                             v_quant(P * jb, gb)
                 if gb == G - 1:
                     ready.extend([jb, jb + 1])
-                if k % 3 == 0 and k > 3:
+                if k % 3 == 0:
                     t_run(k)
-            j, g = steps[-1]
-            mx2_pass(j, 0)
-            mx2_pass(j + 1, 0)
-            v_mul(j, g)
+
+            ja, jz = S // P - 2, S // P - 1
+            for g in range(G):
+                t_stress(ja, g, 5, g)
+            for g in range(G):
+                t_stress(jz, g, 6, g)
+            mx1_two(P * ja, 0, three)
+            v_mul(ja - 2, 1)
             v_out(pending.pop(0))
-            v_quant(P * j, g, 0, P)
-            mx2_pass(j, g)
-            v_mul(j + 1, g)
-            v_quant(P * j, g, P, 2 * P)
-            mx2_pass(j + 1, g)
-            v_out(j)
-            v_out(j + 1)
+            v_mul(ja - 1, 1)
+            mx1_two(P * ja, 2, three)
+            mx1_two(P * ja, 4, three)
+            v_quant(P * (ja - 2), 1)
+            v_mul(ja, 0)
+            mx1_two(P * ja, 6, three)
+            mx2(ja - 2)
+            mx2(ja - 1)
+            v_quant(P * ja, 0, 0, P)
+            v_mul(ja, 1)
+            v_out(ja - 2)
+            v_quant(P * ja, 1, 0, P)
+            v_out(ja - 1)
+            mx1_two(P * jz, 0, three)
+            mx1_two(P * jz, 2, three)
+            v_mul(jz, 0)
+            mx1_two(P * jz, 4, three)
+            mx1(P * jz, P, 6, [7])
+            mx1(P * jz, P, 7, [5])
+            mx2(ja)
+            v_mul(jz, 1)
+            v_quant(P * ja, 0, P, 2 * P)
+            v_quant(P * ja, 1, P, 2 * P)
+            v_out(ja)
+            for g in range(G):
+                for h in range(2):
+                    nc.tensor.matmul_mx(
+                        out=banks[3 + 4 * h][:, 0 : B // 2],
+                        lhsT=pnl_codes[(P * ja, g)][:, P : 2 * P].bitcast(E5),
+                        lhsT_scale=pnl_sc[(P * ja, g)][:, P : 2 * P],
+                        rhs=h_codes[:, g, B // 2 * h : B // 2 * (h + 1)].bitcast(E4),
+                        rhs_scale=h_sc[:, g, B // 2 * h : B // 2 * (h + 1)],
+                        start=(g == 0),
+                        stop=(g == G - 1),
+                    )
+            for h in range(2):
+                cols = slice(B // 2 * h, B // 2 * (h + 1))
+                res = work.tile([P, B // 2], F32, name="res", bufs=6)
+                nc.vector.tensor_tensor(
+                    out=res[:], in0=banks[3 + 4 * h][:, 0 : B // 2], in1=hg[C - 1][:, J - 1, cols], op=ALU.add
+                )
+                nc.sync.dma_start(out=out[P * jz : P * (jz + 1), cols], in_=res[:])

@@ -36,11 +36,12 @@ def tile_scenario_book_pnl_e3_kernel(tc, g_words, g_scales, delta, carry, stress
         banks = [psum.tile([P, 512], F32, name="bank%d" % k) for k in range(8)]
 
         d_raw = [keep.tile([P, F], BF16, name="d_raw%d" % i) for i in range(8)]
-        gw = [keep.tile([P, A, SC], U32, name="gw%d" % c, align_bytes=64) for c in range(C)]
+        gw_cuts = [0, SC, SC + 2 * P, 2 * SC, 3 * SC, S]
+        gw = [keep.tile([P, A, gw_cuts[k + 1] - gw_cuts[k]], U32, name="gw%d" % k, align_bytes=64) for k in range(5)]
         st = [keep.tile([P, 2, I], BF16, name="st%d" % k) for k in range(S // (2 * P))]
         hg = [keep.tile([P, J, B], BF16, name="hg%d" % c) for c in range(C)]
-        gs_first = keep.tile([P, A, SC], U8, name="gs_first", align_bytes=64)
-        gs_rest = keep.tile([P, A, S - SC], U8, name="gs_rest", align_bytes=64)
+        gs_cuts = [0, SC, 2 * SC, S]
+        gs = [keep.tile([P, A, gs_cuts[k + 1] - gs_cuts[k]], U8, name="gs%d" % k, align_bytes=64) for k in range(3)]
         h_raw = [keep.tile([P, 4, B], BF16, name="h_raw%d" % g) for g in range(G)]
         h_grp = [keep.tile([P, B, 4], BF16, name="h_grp%d" % g, align_bytes=64) for g in range(G)]
         h_codes = keep.tile([P, G, B], U32, name="h_codes", align_bytes=64)
@@ -71,9 +72,9 @@ def tile_scenario_book_pnl_e3_kernel(tc, g_words, g_scales, delta, carry, stress
         def load_d(i):
             nc.sync.dma_start(out=d_raw[i][:], in_=d_view[i // 4, i % 4])
 
-        def load_g(c, lo, hi):
+        def load_g(k, lo=0, hi=A):
             nc.sync.dma_start(
-                out=gw[c][:, lo:hi].bitcast(I32), in_=gw_view[:, lo:hi, 2048 * c : 2048 * (c + 1)].bitcast(I32)
+                out=gw[k][:, lo:hi].bitcast(I32), in_=gw_view[:, lo:hi, 4 * gw_cuts[k] : 4 * gw_cuts[k + 1]].bitcast(I32)
             )
 
         def load_st(k):
@@ -85,10 +86,11 @@ def tile_scenario_book_pnl_e3_kernel(tc, g_words, g_scales, delta, carry, stress
         def load_h(g):
             nc.sync.dma_start(out=h_raw[g][:], in_=h_view[g])
 
-        def load_gs(plane, lo, hi):
+        def load_gs(k):
             for q in range(4):
                 nc.sync.dma_start(
-                    out=plane[32 * q : 32 * q + 4].bitcast(I32), in_=gs_view[4 * q : 4 * q + 4, :, lo // 4 : hi // 4]
+                    out=gs[k][32 * q : 32 * q + 4].bitcast(I32),
+                    in_=gs_view[4 * q : 4 * q + 4, :, gs_cuts[k] // 4 : gs_cuts[k + 1] // 4],
                 )
 
         def unit_bank(pool_banks):
@@ -153,14 +155,16 @@ def tile_scenario_book_pnl_e3_kernel(tc, g_words, g_scales, delta, carry, stress
                 s_unit(s0, P, i + m, bank[:, P * m : P * (m + 1)])
 
         def mx1_passes(s0, n, i, acc):
-            c, lo = s0 // SC, s0 % SC
+            kw = max(k for k in range(5) if gw_cuts[k] <= s0)
+            ks = max(k for k in range(3) if gs_cuts[k] <= s0)
+            w0, c0 = s0 - gw_cuts[kw], s0 - gs_cuts[ks]
             for a in range(A):
                 nc.tensor.matmul_mx(
                     out=acc,
                     lhsT=d_codes[i][:, a, :].bitcast(E4),
                     lhsT_scale=d_sc[i][:, a, :],
-                    rhs=gw[c][:, a, lo : lo + n].bitcast(E5),
-                    rhs_scale=gs_first[:, a, s0 : s0 + n] if c == 0 else gs_rest[:, a, s0 - SC : s0 - SC + n],
+                    rhs=gw[kw][:, a, w0 : w0 + n].bitcast(E5),
+                    rhs_scale=gs[ks][:, a, c0 : c0 + n],
                     start=(a == 0),
                     stop=(a == A - 1),
                 )
@@ -168,7 +172,10 @@ def tile_scenario_book_pnl_e3_kernel(tc, g_words, g_scales, delta, carry, stress
         def s_unit(s0, n, i, acc):
             g, t = i // 4, i % 4
             if t == 0:
-                units[(s0, g)] = work.tile([P, 4, n], F32, name="unit")
+                if n == SC:
+                    units[(s0, g)] = work.tile([P, 4, n], F32, name="unit_wide", bufs=2)
+                else:
+                    units[(s0, g)] = work.tile([P, 4, n], F32, name="unit", bufs=4)
             nc.scalar.activation(
                 out=units[(s0, g)][:, t, :], in_=acc, func=ACT.Identity, bias=ca[:, g, t : t + 1], scale=1.0
             )
@@ -237,6 +244,8 @@ def tile_scenario_book_pnl_e3_kernel(tc, g_words, g_scales, delta, carry, stress
             res = work.tile([P, B], F32, name="res", bufs=6)
             nc.vector.tensor_tensor(out=res[:], in0=acc_out[j][:], in1=hg[j // J][:, j % J, :], op=ALU.add)
             nc.sync.dma_start(out=out[P * j : P * (j + 1), :], in_=res[:])
+            if j in (1, 5):
+                load_hg(2 + j // 4)
 
         def v_hold(g, h):
             cols = slice(256 * h, 256 * (h + 1))
@@ -252,12 +261,12 @@ def tile_scenario_book_pnl_e3_kernel(tc, g_words, g_scales, delta, carry, stress
 
         with tc.manual_schedule():
             nc.scalar.dma_start(out=ca_raw[:, :, 0:4], in_=carry.rearrange("(g p t) -> p g t", g=G, t=4))
-            nc.vector.memset(gs_first[:].rearrange("p a n -> p (a n)").bitcast(I32), 0)
-            nc.vector.memset(gs_rest[:].rearrange("p a n -> p (a n)").bitcast(I32), 0)
+            for k in range(3):
+                nc.vector.memset(gs[k][:].rearrange("p a n -> p (a n)").bitcast(I32), 0)
             nc.scalar.activation(out=ca[:], in_=ca_raw[:, :, 0:4], func=ACT.Identity, scale=1.0)
             load_d(0)
             load_d(1)
-            load_gs(gs_first, 0, SC)
+            load_gs(0)
             load_g(0, 0, 1)
             load_g(0, 1, A)
             load_d(2)
@@ -267,20 +276,23 @@ def tile_scenario_book_pnl_e3_kernel(tc, g_words, g_scales, delta, carry, stress
             load_d(5)
             load_st(0)
             load_d(6)
-            load_h(1)
             load_d(7)
             load_st(1)
-            load_gs(gs_rest, SC, S)
-            load_g(1, 0, A)
+            load_gs(1)
+            load_g(1)
+            load_h(1)
             load_st(2)
+            load_g(2)
             load_st(3)
+            load_gs(2)
+            load_st(4)
             load_hg(0)
-            for c in range(2, C):
-                load_st(2 * c)
-                load_g(c, 0, A)
-                load_st(2 * c + 1)
-                load_hg(c - 1)
-            load_hg(C - 1)
+            load_g(3)
+            load_st(5)
+            load_hg(1)
+            load_st(6)
+            load_g(4)
+            load_st(7)
 
             on_vector = nc.vector.tensor_copy
             for i in range(2):
@@ -311,9 +323,7 @@ def tile_scenario_book_pnl_e3_kernel(tc, g_words, g_scales, delta, carry, stress
                     c_delta(i + 2, True)
                     q_delta(i + 2, 0, 1)
                 if i == 3:
-                    v_hold(1, 0)
-                if i == 4:
-                    v_hold(1, 1)
+                    v_hold_q(0)
                 if i + 2 < 8:
                     q_delta(i + 2, 1, 3)
                 if i == 5:
@@ -331,31 +341,35 @@ def tile_scenario_book_pnl_e3_kernel(tc, g_words, g_scales, delta, carry, stress
                     t_pair(steps[m][0], steps[m][1], 5 + m % 3)
 
             mx1(SC, 2 * P, 0, [4])
-            mx1(SC, 2 * P, 1, [5])
+            mx1(SC, 2 * P, 1, [2])
             reorder(4, 0)
             mx1(0, SC, 7, [1])
             unit_turn[0] = 0
+            v_hold(1, 0)
             v_quant(2 * P, 0)
+            v_hold(1, 1)
             t_run(0)
             reorder(4, 1)
             reorder(6, 0)
-            mx1(SC, 2 * P, 2, three)
-            mx1(SC, 2 * P, 3, three)
+            five = [0, 4, 2, 3, 1]
+            mx1(SC, 2 * P, 2, five)
+            mx1(SC, 2 * P, 3, five)
             for j in range(J):
                 v_mul(j, 1)
             for t in range(4):
-                mx1(SC, 2 * P, 4 + t, three)
+                mx1(SC, 2 * P, 4 + t, five)
+                if t == 1:
+                    reorder(6, 1)
             v_mul(4, 0)
             v_mul(5, 0)
-            mx1(SC + 2 * P, 2 * P, 0, three)
-            reorder(6, 1)
-            mx1(SC + 2 * P, 2 * P, 1, three)
-            t_run(3)
+            mx1(SC + 2 * P, 2 * P, 0, five)
+            mx1(SC + 2 * P, 2 * P, 1, five)
             reorder(8, 0)
-            v_hold_q(0)
+            mx1(SC + 2 * P, 2 * P, 2, five)
+            t_run(3)
             v_quant(0, 1)
             v_hold_q(1)
-            mx1(SC + 2 * P, 2 * P, 2, three)
+            unit_turn[0] = 0
             mx1(SC + 2 * P, 2 * P, 3, three)
             v_mul(4, 1)
             v_quant(2 * P, 1)

@@ -147,12 +147,12 @@ def tile_scenario_book_pnl_e3_kernel(tc, g_words, g_scales, delta, carry, stress
             mx1_passes(s0, n, i, acc)
             s_unit(s0, n, i, acc)
 
-        def mx1_two(s0, i, pool_banks):
+        def mx1_two(s0, i, pool_banks, n=P):
             bank = unit_bank(pool_banks)
             for m in range(2):
-                mx1_passes(s0, P, i + m, bank[:, P * m : P * (m + 1)])
+                mx1_passes(s0, n, i + m, bank[:, n * m : n * (m + 1)])
             for m in range(2):
-                s_unit(s0, P, i + m, bank[:, P * m : P * (m + 1)])
+                s_unit(s0, n, i + m, bank[:, n * m : n * (m + 1)])
 
         def mx1_passes(s0, n, i, acc):
             kw = max(k for k in range(5) if gw_cuts[k] <= s0)
@@ -193,43 +193,47 @@ def tile_scenario_book_pnl_e3_kernel(tc, g_words, g_scales, delta, carry, stress
                 else:
                     words = st[j // 2][:, j % 2, :].bitcast(F32)[:, 256 * g + u : 256 * (g + 1) : 2]
                 nc.tensor.transpose(dst.rearrange("p (c u i) -> p u c i", u=2, i=4)[:, u], words, ident[:])
-            st_bank[(j, g)] = dst
+            st_bank[(j, g)] = (k, half)
 
         def t_pair(j, g, k):
             t_stress(j, g, k, 0)
             t_stress(j + 1, g, k, 1)
 
-        def v_mul(j, g):
-            s0 = 2 * P * (j // 2)
-            if (s0, g) not in pnl:
-                pnl[(s0, g)] = work.tile([P, 2 * P, 4], BF16, name="pnl", align_bytes=64, bufs=4)
-            u0 = 0 if j < J else s0 if j < S // P - 2 else P * j
-            cols = slice(j * P - u0, j * P - u0 + P)
+        def v_mul(j, g, blocks=2):
+            n = P * blocks
+            if g == 0:
+                pnl[j] = work.tile([P, G, n, 4], BF16, name="pnl", align_bytes=64, bufs=3)
+            u0 = 0 if j < J else P * j
+            cols = slice(j * P - u0, j * P - u0 + n)
+            k, half = st_bank[(j, g)]
             nc.vector.tensor_tensor(
-                out=pnl[(s0, g)][:, P * (j % 2) : P * (j % 2 + 1), :].rearrange("p (c i) (u e) -> p c u e i", i=4, u=2),
+                out=pnl[j][:, g].rearrange("p (c i) (u e) -> p c u e i", i=4, u=2),
                 in0=units[(u0, g)][:, :, cols].rearrange("p (u e) (c i) -> p c u e i", i=4, u=2),
-                in1=st_bank[(j, g)].bitcast(BF16).rearrange("p (c u i e) -> p c u e i", u=2, i=4, e=2),
+                in1=banks[k][:, 256 * half : 256 * (half + blocks)]
+                .bitcast(BF16)
+                .rearrange("p (c u i e) -> p c u e i", u=2, i=4, e=2),
                 op=ALU.mult,
             )
 
-        def v_quant(s0, g, lo=0, hi=2 * P):
+        def v_quant(j, lo=0, hi=G):
+            n = pnl[j].shape[2]
             if lo == 0:
-                pnl_codes[(s0, g)] = work.tile([P, 2 * P], U32, name="pnl_codes", align_bytes=64, bufs=10)
-                pnl_sc[(s0, g)] = work.tile([P, 2 * P], U8, name="pnl_sc", align_bytes=64, bufs=10)
+                pnl_codes[j] = work.tile([P, G, n], U32, name="pnl_codes", align_bytes=64, bufs=5)
+                pnl_sc[j] = work.tile([P, G, n], U8, name="pnl_sc", align_bytes=64, bufs=5)
             nc.vector.quantize_mx(
-                out=pnl_codes[(s0, g)][:, lo:hi].bitcast(E5),
-                scales=pnl_sc[(s0, g)][:, lo:hi],
-                in_=pnl[(s0, g)][:, lo:hi, :].rearrange("p s t -> p (s t)"),
+                out=pnl_codes[j][:, lo:hi].rearrange("p g s -> p (g s)").bitcast(E5),
+                scales=pnl_sc[j][:, lo:hi].rearrange("p g s -> p (g s)"),
+                in_=pnl[j][:, lo:hi].rearrange("p g s t -> p (g s t)"),
             )
 
         def mx2_pass(j, g):
             acc_out[j] = banks[2 + j % 2]
-            s0 = 2 * P * (j // 2)
-            cols = slice(P * (j % 2), P * (j % 2 + 1))
+            j0 = j if j in pnl_codes else j - 1
+            cols = slice(P * (j - j0), P * (j - j0 + 1))
             nc.tensor.matmul_mx(
                 out=acc_out[j][:],
-                lhsT=pnl_codes[(s0, g)][:, cols].bitcast(E5),
-                lhsT_scale=pnl_sc[(s0, g)][:, cols],
+                lhsT=pnl_codes[j0][:, g, cols].bitcast(E5),
+                lhsT_scale=pnl_sc[j0][:, g, cols],
                 rhs=h_codes[:, g, :].bitcast(E4),
                 rhs_scale=h_sc[:, g, :],
                 start=(g == 0),
@@ -247,11 +251,15 @@ def tile_scenario_book_pnl_e3_kernel(tc, g_words, g_scales, delta, carry, stress
             if j in (1, 5):
                 load_hg(2 + j // 4)
 
-        def v_hold(g, h):
-            cols = slice(256 * h, 256 * (h + 1))
-            nc.vector.tensor_copy(
-                out=h_grp[g][:, cols, :].rearrange("p (c i) t -> p c t i", i=4),
-                in_=h_raw[g][:, :, cols].rearrange("p t (c i) -> p c t i", i=4),
+        def g_hold(g, h):
+            cols = slice(P * h, P * (h + 1))
+            nc.gpsimd.tensor_scalar(
+                out=h_grp[g][:, cols, :],
+                in0=h_raw[g][:, :, cols].rearrange("p t w -> p w t"),
+                scalar1=1.0,
+                scalar2=0.0,
+                op0=ALU.mult,
+                op1=ALU.add,
             )
 
         def v_hold_q(g):
@@ -272,7 +280,6 @@ def tile_scenario_book_pnl_e3_kernel(tc, g_words, g_scales, delta, carry, stress
             load_d(2)
             load_d(3)
             load_d(4)
-            load_h(0)
             load_d(5)
             load_st(0)
             load_d(6)
@@ -280,10 +287,11 @@ def tile_scenario_book_pnl_e3_kernel(tc, g_words, g_scales, delta, carry, stress
             load_st(1)
             load_gs(1)
             load_g(1)
-            load_h(1)
             load_st(2)
             load_g(2)
             load_st(3)
+            load_h(0)
+            load_h(1)
             load_gs(2)
             load_st(4)
             load_hg(0)
@@ -306,32 +314,23 @@ def tile_scenario_book_pnl_e3_kernel(tc, g_words, g_scales, delta, carry, stress
                     t_delta(i + 2)
                 if i in (4, 5):
                     t_pair(2 * (i - 4), 0, 2 + (i - 4))
-                if i + 3 < 8:
-                    r_delta(i + 3)
-                if i == 1:
-                    v_hold(0, 0)
-                if i == 2:
-                    v_hold(0, 1)
-                if i == 3:
-                    reorder(0, 0, on_vector)
-                if i == 4:
-                    reorder(2, 0, on_vector)
-                if i == 5:
-                    v_mul(0, 0)
-                    v_mul(1, 0)
+                if i == 0:
+                    r_delta(3)
                 if i + 2 < 8:
-                    c_delta(i + 2, True)
+                    c_delta(i + 2, False)
+                    if i + 4 < 8:
+                        r_delta(i + 4)
+                    else:
+                        reorder(2 * (i - 4), 1, on_vector)
                     q_delta(i + 2, 0, 1)
-                if i == 3:
-                    v_hold_q(0)
-                if i + 2 < 8:
-                    q_delta(i + 2, 1, 3)
-                if i == 5:
-                    reorder(0, 1)
-            reorder(2, 1, on_vector)
+                    q_delta(i + 2, 1, A)
+                if i in (2, 3, 5):
+                    reorder({2: 0, 3: 2, 5: 4}[i], 0)
+            for g in range(G):
+                for h in range(4):
+                    g_hold(g, h)
+            v_mul(0, 0)
             v_mul(2, 0)
-            v_quant(0, 0)
-            v_mul(3, 0)
 
             steps = [(0, 1), (2, 1)] + [(j, g) for j in range(J, S // P, 2) for g in range(G)]
             three = [0, 4, 1]
@@ -340,48 +339,41 @@ def tile_scenario_book_pnl_e3_kernel(tc, g_words, g_scales, delta, carry, stress
                 for m in range(k, min(k + 3, len(steps))):
                     t_pair(steps[m][0], steps[m][1], 5 + m % 3)
 
-            mx1(SC, 2 * P, 0, [4])
-            mx1(SC, 2 * P, 1, [2])
-            reorder(4, 0)
+            mx1_two(SC, 0, [4], 2 * P)
             mx1(0, SC, 7, [1])
             unit_turn[0] = 0
-            v_hold(1, 0)
-            v_quant(2 * P, 0)
-            v_hold(1, 1)
             t_run(0)
             reorder(4, 1)
             reorder(6, 0)
-            five = [0, 4, 2, 3, 1]
+            five = [0, 4, 1, 2, 3]
             mx1(SC, 2 * P, 2, five)
             mx1(SC, 2 * P, 3, five)
-            for j in range(J):
-                v_mul(j, 1)
+            v_mul(0, 1)
+            v_mul(2, 1)
             for t in range(4):
                 mx1(SC, 2 * P, 4 + t, five)
                 if t == 1:
                     reorder(6, 1)
             v_mul(4, 0)
-            v_mul(5, 0)
             mx1(SC + 2 * P, 2 * P, 0, five)
             mx1(SC + 2 * P, 2 * P, 1, five)
             reorder(8, 0)
             mx1(SC + 2 * P, 2 * P, 2, five)
             t_run(3)
-            v_quant(0, 1)
+            v_hold_q(0)
+            v_quant(0)
             v_hold_q(1)
             unit_turn[0] = 0
             mx1(SC + 2 * P, 2 * P, 3, three)
             v_mul(4, 1)
-            v_quant(2 * P, 1)
-            v_mul(5, 1)
-            v_quant(SC, 0)
-            v_quant(SC, 1)
-            ready = [0, 1, 2, 3, 4, 5]
+            v_quant(2)
+            ready = [0, 1, 2, 3]
             pending = []
+            to_quant = [4]
             for k in range(5, len(steps) - 2):
                 j, g = steps[k]
                 jb, gb = steps[k - 1]
-                count = 2 if len(ready) > 2 or k == len(steps) - 3 else 1
+                count = 1 if k < 7 else 2
                 take = ready[:count]
                 ready = ready[count:]
                 for t in range(4):
@@ -389,18 +381,19 @@ def tile_scenario_book_pnl_e3_kernel(tc, g_words, g_scales, delta, carry, stress
                     if t == 1:
                         reorder(*steps[k + 2])
                     if t == 0:
-                        v_mul(jb, gb)
                         while pending:
                             v_out(pending.pop(0))
-                        v_mul(jb + 1, gb)
+                        v_mul(jb, gb)
                     if take and t in (1, 3):
                         mx2(take[0])
                         pending.append(take.pop(0))
                         if t == 1:
                             v_out(pending.pop(0))
-                            v_quant(P * jb, gb)
-                if gb == G - 1:
-                    ready.extend([jb, jb + 1])
+                            if gb == G - 1:
+                                to_quant.append(jb)
+                            if to_quant and k > 5:
+                                ready.extend([to_quant[0], to_quant[0] + 1])
+                                v_quant(to_quant.pop(0))
                 if k % 3 == 0:
                     t_run(k)
 
@@ -411,37 +404,35 @@ def tile_scenario_book_pnl_e3_kernel(tc, g_words, g_scales, delta, carry, stress
                 t_stress(jz, g, 6, g)
             mx1_two(P * ja, 0, three)
             v_mul(ja - 2, 1)
+            v_quant(ja - 2)
             v_out(pending.pop(0))
-            v_mul(ja - 1, 1)
             mx1_two(P * ja, 2, three)
             mx1_two(P * ja, 4, three)
-            v_quant(P * (ja - 2), 1)
-            v_mul(ja, 0)
+            v_mul(ja, 0, 1)
             mx1_two(P * ja, 6, three)
             mx2(ja - 2)
             mx2(ja - 1)
-            v_quant(P * ja, 0, 0, P)
-            v_mul(ja, 1)
+            v_mul(ja, 1, 1)
             v_out(ja - 2)
-            v_quant(P * ja, 1, 0, P)
+            v_quant(ja)
             v_out(ja - 1)
             mx1_two(P * jz, 0, three)
             mx1_two(P * jz, 2, three)
-            v_mul(jz, 0)
+            v_mul(jz, 0, 1)
             mx1_two(P * jz, 4, three)
             mx1(P * jz, P, 6, [7])
             mx1(P * jz, P, 7, [5])
             mx2(ja)
-            v_mul(jz, 1)
-            v_quant(P * ja, 0, P, 2 * P)
-            v_quant(P * ja, 1, P, 2 * P)
+            v_mul(jz, 1, 1)
+            v_quant(jz, 0, 1)
+            v_quant(jz, 1, G)
             v_out(ja)
             for g in range(G):
                 for h in range(2):
                     nc.tensor.matmul_mx(
                         out=banks[3 + 4 * h][:, 0 : B // 2],
-                        lhsT=pnl_codes[(P * ja, g)][:, P : 2 * P].bitcast(E5),
-                        lhsT_scale=pnl_sc[(P * ja, g)][:, P : 2 * P],
+                        lhsT=pnl_codes[jz][:, g].bitcast(E5),
+                        lhsT_scale=pnl_sc[jz][:, g],
                         rhs=h_codes[:, g, B // 2 * h : B // 2 * (h + 1)].bitcast(E4),
                         rhs_scale=h_sc[:, g, B // 2 * h : B // 2 * (h + 1)],
                         start=(g == 0),

@@ -251,15 +251,11 @@ def tile_scenario_book_pnl_e3_kernel(tc, g_words, g_scales, delta, carry, stress
             if j in (1, 5):
                 load_hg(2 + j // 4)
 
-        def g_hold(g, h):
-            cols = slice(P * h, P * (h + 1))
-            nc.gpsimd.tensor_scalar(
-                out=h_grp[g][:, cols, :],
-                in0=h_raw[g][:, :, cols].rearrange("p t w -> p w t"),
-                scalar1=1.0,
-                scalar2=0.0,
-                op0=ALU.mult,
-                op1=ALU.add,
+        def v_hold(g, h):
+            cols = slice(256 * h, 256 * (h + 1))
+            nc.vector.tensor_copy(
+                out=h_grp[g][:, cols, :].rearrange("p (c i) t -> p c t i", i=4),
+                in_=h_raw[g][:, :, cols].rearrange("p t (c i) -> p c t i", i=4),
             )
 
         def v_hold_q(g):
@@ -280,18 +276,18 @@ def tile_scenario_book_pnl_e3_kernel(tc, g_words, g_scales, delta, carry, stress
             load_d(2)
             load_d(3)
             load_d(4)
+            load_h(0)
             load_d(5)
             load_st(0)
             load_d(6)
             load_d(7)
+            load_h(1)
             load_st(1)
             load_gs(1)
             load_g(1)
             load_st(2)
             load_g(2)
             load_st(3)
-            load_h(0)
-            load_h(1)
             load_gs(2)
             load_st(4)
             load_hg(0)
@@ -318,17 +314,16 @@ def tile_scenario_book_pnl_e3_kernel(tc, g_words, g_scales, delta, carry, stress
                     r_delta(3)
                 if i + 2 < 8:
                     c_delta(i + 2, False)
-                    if i + 4 < 8:
+                    if i in (0, 3):
                         r_delta(i + 4)
                     else:
+                        v_hold(i // 4, (i - 1) % 3)
+                    if i + 4 >= 8:
                         reorder(2 * (i - 4), 1, on_vector)
                     q_delta(i + 2, 0, 1)
                     q_delta(i + 2, 1, A)
                 if i in (2, 3, 5):
                     reorder({2: 0, 3: 2, 5: 4}[i], 0)
-            for g in range(G):
-                for h in range(4):
-                    g_hold(g, h)
             v_mul(0, 0)
             v_mul(2, 0)
 

@@ -69,8 +69,8 @@ def tile_scenario_book_pnl_e3_kernel(tc, g_words, g_scales, delta, carry, stress
         acc_out = {}
         unit_turn = [0]
 
-        def load_d(i):
-            nc.sync.dma_start(out=d_raw[i][:], in_=d_view[i // 4, i % 4])
+        def load_d(i, lo=0, hi=F):
+            nc.sync.dma_start(out=d_raw[i][:, lo:hi], in_=d_view[i // 4, i % 4][:, lo:hi])
 
         def load_g(k, lo=0, hi=A):
             nc.sync.dma_start(
@@ -268,11 +268,13 @@ def tile_scenario_book_pnl_e3_kernel(tc, g_words, g_scales, delta, carry, stress
             for k in range(3):
                 nc.vector.memset(gs[k][:].rearrange("p a n -> p (a n)").bitcast(I32), 0)
             nc.scalar.activation(out=ca[:], in_=ca_raw[:, :, 0:4], func=ACT.Identity, scale=1.0)
-            load_d(0)
+            load_d(0, 0, 512)
+            load_d(0, 512, F)
             load_d(1)
             load_gs(0)
             load_g(0, 0, 1)
-            load_g(0, 1, A)
+            load_g(0, 1, 2)
+            load_g(0, 2, 3)
             load_d(2)
             load_d(3)
             load_d(4)
@@ -281,11 +283,11 @@ def tile_scenario_book_pnl_e3_kernel(tc, g_words, g_scales, delta, carry, stress
             load_st(0)
             load_d(6)
             load_d(7)
-            load_h(1)
             load_st(1)
             load_gs(1)
             load_g(1)
             load_st(2)
+            load_h(1)
             load_g(2)
             load_st(3)
             load_gs(2)
@@ -310,22 +312,23 @@ def tile_scenario_book_pnl_e3_kernel(tc, g_words, g_scales, delta, carry, stress
                     t_delta(i + 2)
                 if i in (4, 5):
                     t_pair(2 * (i - 4), 0, 2 + (i - 4))
-                if i == 0:
-                    r_delta(3)
                 if i + 2 < 8:
                     c_delta(i + 2, False)
-                    if i in (0, 3):
-                        r_delta(i + 4)
-                    else:
-                        v_hold(i // 4, (i - 1) % 3)
+                    if i in (1, 2):
+                        v_hold(0, i - 1)
+                    if i == 3:
+                        v_hold_q(0)
                     if i + 4 >= 8:
                         reorder(2 * (i - 4), 1, on_vector)
                     q_delta(i + 2, 0, 1)
                     q_delta(i + 2, 1, A)
-                if i in (2, 3, 5):
-                    reorder({2: 0, 3: 2, 5: 4}[i], 0)
+                if i == 3:
+                    r_delta(7)
+                if i in (3, 4, 5):
+                    reorder(2 * (i - 3), 0)
             v_mul(0, 0)
             v_mul(2, 0)
+            v_hold(1, 0)
 
             steps = [(0, 1), (2, 1)] + [(j, g) for j in range(J, S // P, 2) for g in range(G)]
             three = [0, 4, 1]
@@ -355,7 +358,7 @@ def tile_scenario_book_pnl_e3_kernel(tc, g_words, g_scales, delta, carry, stress
             reorder(8, 0)
             mx1(SC + 2 * P, 2 * P, 2, five)
             t_run(3)
-            v_hold_q(0)
+            v_hold(1, 1)
             v_quant(0)
             v_hold_q(1)
             unit_turn[0] = 0

@@ -35,7 +35,8 @@ def tile_scenario_book_pnl_e3_kernel(tc, g_words, g_scales, delta, carry, stress
         make_identity(nc, ident[:])
         banks = [psum.tile([P, 512], F32, name="bank%d" % k) for k in range(8)]
 
-        d_raw = [keep.tile([P, F], BF16, name="d_raw%d" % i) for i in range(8)]
+        d_raw = [work.tile([P, F], BF16, name="d_words", bufs=4) for i in range(4)]
+        d_raw = d_raw + [keep.tile([P, F], BF16, name="d_raw%d" % i) for i in range(4, 8)]
         gw_cuts = [0, SC, SC + 2 * P, 2 * SC, 3 * SC, S]
         gw = [keep.tile([P, A, gw_cuts[k + 1] - gw_cuts[k]], U32, name="gw%d" % k, align_bytes=64) for k in range(5)]
         st = [keep.tile([P, 2, I], BF16, name="st%d" % k) for k in range(S // (2 * P))]
@@ -69,8 +70,8 @@ def tile_scenario_book_pnl_e3_kernel(tc, g_words, g_scales, delta, carry, stress
         acc_out = {}
         unit_turn = [0]
 
-        def load_d(i, lo=0, hi=F):
-            nc.sync.dma_start(out=d_raw[i][:, lo:hi], in_=d_view[i // 4, i % 4][:, lo:hi])
+        def load_d(i):
+            nc.sync.dma_start(out=d_raw[i][:], in_=d_view[i // 4, i % 4])
 
         def load_g(k, lo=0, hi=A):
             nc.sync.dma_start(
@@ -115,7 +116,7 @@ def tile_scenario_book_pnl_e3_kernel(tc, g_words, g_scales, delta, carry, stress
                     nc.tensor.transpose(dst, words, ident[:])
 
         def r_delta(i):
-            d_re[i] = work.tile([P, A, 2, P], F32, name="d_re", bufs=3)
+            d_re[i] = work.tile([P, A, 2, P], F32, name="d_words", bufs=4)
             nc.vector.tensor_copy(
                 out=d_re[i][:].rearrange("p a u (v m) -> p v a u m", v=2),
                 in_=d_raw[i][:].bitcast(F32).rearrange("p (a v m u) -> p v a u m", a=A, v=2, u=2),
@@ -154,11 +155,11 @@ def tile_scenario_book_pnl_e3_kernel(tc, g_words, g_scales, delta, carry, stress
             for m in range(2):
                 s_unit(s0, n, i + m, bank[:, n * m : n * (m + 1)])
 
-        def mx1_passes(s0, n, i, acc):
+        def mx1_passes(s0, n, i, acc, passes=range(A)):
             kw = max(k for k in range(5) if gw_cuts[k] <= s0)
             ks = max(k for k in range(3) if gs_cuts[k] <= s0)
             w0, c0 = s0 - gw_cuts[kw], s0 - gs_cuts[ks]
-            for a in range(A):
+            for a in passes:
                 nc.tensor.matmul_mx(
                     out=acc,
                     lhsT=d_codes[i][:, a, :].bitcast(E4),
@@ -202,7 +203,7 @@ def tile_scenario_book_pnl_e3_kernel(tc, g_words, g_scales, delta, carry, stress
         def v_mul(j, g, blocks=2):
             n = P * blocks
             if g == 0:
-                pnl[j] = work.tile([P, G, n, 4], BF16, name="pnl", align_bytes=64, bufs=3)
+                pnl[j] = work.tile([P, G, n, 4], BF16, name="pnl", align_bytes=64, bufs=4)
             u0 = 0 if j < J else P * j
             cols = slice(j * P - u0, j * P - u0 + n)
             k, half = st_bank[(j, g)]
@@ -268,28 +269,27 @@ def tile_scenario_book_pnl_e3_kernel(tc, g_words, g_scales, delta, carry, stress
             for k in range(3):
                 nc.vector.memset(gs[k][:].rearrange("p a n -> p (a n)").bitcast(I32), 0)
             nc.scalar.activation(out=ca[:], in_=ca_raw[:, :, 0:4], func=ACT.Identity, scale=1.0)
-            load_d(0, 0, 512)
-            load_d(0, 512, F)
+            load_d(0)
             load_d(1)
+            load_d(2)
+            load_d(3)
             load_gs(0)
             load_g(0, 0, 1)
             load_g(0, 1, 2)
             load_g(0, 2, 3)
-            load_d(2)
-            load_d(3)
             load_d(4)
-            load_h(0)
             load_d(5)
-            load_st(0)
             load_d(6)
             load_d(7)
+            load_st(0)
+            load_h(0)
             load_st(1)
+            load_st(2)
             load_gs(1)
             load_g(1)
-            load_st(2)
             load_h(1)
-            load_g(2)
             load_st(3)
+            load_g(2)
             load_gs(2)
             load_st(4)
             load_hg(0)
@@ -301,34 +301,54 @@ def tile_scenario_book_pnl_e3_kernel(tc, g_words, g_scales, delta, carry, stress
             load_st(7)
 
             on_vector = nc.vector.tensor_copy
-            for i in range(2):
-                t_delta(i)
+
+            def cq_delta(i):
                 c_delta(i, False)
+                if i not in (0, 4):
+                    q_delta(i - 1, 1, A)
                 q_delta(i, 0, 1)
-                q_delta(i, 1, 3)
-            for i in range(7):
-                mx1(0, SC, i, [0, 1])
-                if i + 2 < 8:
-                    t_delta(i + 2)
-                if i in (4, 5):
-                    t_pair(2 * (i - 4), 0, 2 + (i - 4))
-                if i + 2 < 8:
-                    c_delta(i + 2, False)
-                    if i in (1, 2):
-                        v_hold(0, i - 1)
-                    if i == 3:
-                        v_hold_q(0)
-                    if i + 4 >= 8:
-                        reorder(2 * (i - 4), 1, on_vector)
-                    q_delta(i + 2, 0, 1)
-                    q_delta(i + 2, 1, A)
-                if i == 3:
-                    r_delta(7)
-                if i in (3, 4, 5):
-                    reorder(2 * (i - 3), 0)
+
+            for i in range(4):
+                t_delta(i)
+                cq_delta(i)
+            q_delta(3, 1, A)
+            for a in range(A - 1):
+                for i in range(4):
+                    mx1_passes(0, SC, i, banks[i][:], [a])
+            mx1_passes(0, SC, 0, banks[0][:], [A - 1])
+            s_unit(0, SC, 0, banks[0][:])
+            for i in range(4, 7):
+                r_delta(i)
+            t_delta(4)
+            t_delta(5)
+            for i in range(1, 4):
+                mx1_passes(0, SC, i, banks[i][:], [A - 1])
+            cq_delta(4)
+            r_delta(7)
+            cq_delta(5)
+            s_unit(0, SC, 1, banks[1][:])
+            t_delta(6)
+            t_delta(7)
+            s_unit(0, SC, 2, banks[2][:])
+            reorder(0, 0, on_vector)
+            cq_delta(6)
+            s_unit(0, SC, 3, banks[3][:])
+            mx1(0, SC, 4, [0])
+            reorder(2, 0, on_vector)
+            cq_delta(7)
+            mx1(0, SC, 5, [1])
+            t_pair(0, 0, 2)
+            t_pair(2, 0, 3)
+            q_delta(7, 1, A)
+            reorder(0, 1)
+            reorder(2, 1)
+            mx1(0, SC, 6, [0])
+            mx1(0, SC, 7, [1])
             v_mul(0, 0)
+            reorder(4, 0, on_vector)
+            v_hold(0, 0)
             v_mul(2, 0)
-            v_hold(1, 0)
+            v_hold(0, 1)
 
             steps = [(0, 1), (2, 1)] + [(j, g) for j in range(J, S // P, 2) for g in range(G)]
             three = [0, 4, 1]
@@ -337,15 +357,14 @@ def tile_scenario_book_pnl_e3_kernel(tc, g_words, g_scales, delta, carry, stress
                 for m in range(k, min(k + 3, len(steps))):
                     t_pair(steps[m][0], steps[m][1], 5 + m % 3)
 
-            mx1_two(SC, 0, [4], 2 * P)
-            mx1(0, SC, 7, [1])
             unit_turn[0] = 0
             t_run(0)
             reorder(4, 1)
-            reorder(6, 0)
-            five = [0, 4, 1, 2, 3]
-            mx1(SC, 2 * P, 2, five)
-            mx1(SC, 2 * P, 3, five)
+            five = [4, 0, 1, 2, 3]
+            for t in range(4):
+                mx1(SC, 2 * P, t, five)
+                if t == 1:
+                    reorder(6, 0)
             v_mul(0, 1)
             v_mul(2, 1)
             for t in range(4):
@@ -358,16 +377,17 @@ def tile_scenario_book_pnl_e3_kernel(tc, g_words, g_scales, delta, carry, stress
             reorder(8, 0)
             mx1(SC + 2 * P, 2 * P, 2, five)
             t_run(3)
+            v_hold(1, 0)
+            v_hold_q(0)
             v_hold(1, 1)
             v_quant(0)
             v_hold_q(1)
             unit_turn[0] = 0
             mx1(SC + 2 * P, 2 * P, 3, three)
             v_mul(4, 1)
-            v_quant(2)
-            ready = [0, 1, 2, 3]
+            ready = [0, 1]
             pending = []
-            to_quant = [4]
+            to_quant = [2, 4]
             for k in range(5, len(steps) - 2):
                 j, g = steps[k]
                 jb, gb = steps[k - 1]

@@ -275,10 +275,10 @@ def tile_scenario_book_pnl_e3_kernel(tc, g_words, g_scales, delta, carry, stress
             load_d(3)
             load_gs(0)
             load_g(0, 0, 1)
-            load_g(0, 1, 2)
-            load_g(0, 2, 3)
             load_d(4)
+            load_g(0, 1, 2)
             load_d(5)
+            load_g(0, 2, 3)
             load_d(6)
             load_d(7)
             load_st(0)
@@ -304,7 +304,7 @@ def tile_scenario_book_pnl_e3_kernel(tc, g_words, g_scales, delta, carry, stress
 
             def cq_delta(i):
                 c_delta(i, False)
-                if i not in (0, 4):
+                if i > 0:
                     q_delta(i - 1, 1, A)
                 q_delta(i, 0, 1)
 
@@ -317,29 +317,32 @@ def tile_scenario_book_pnl_e3_kernel(tc, g_words, g_scales, delta, carry, stress
                     mx1_passes(0, SC, i, banks[i][:], [a])
             mx1_passes(0, SC, 0, banks[0][:], [A - 1])
             s_unit(0, SC, 0, banks[0][:])
-            for i in range(4, 7):
+            for i in range(4, 6):
                 r_delta(i)
             t_delta(4)
             t_delta(5)
             for i in range(1, 4):
                 mx1_passes(0, SC, i, banks[i][:], [A - 1])
-            cq_delta(4)
-            r_delta(7)
-            cq_delta(5)
+            for i in range(4, 6):
+                c_delta(i, False)
+                r_delta(i + 2)
+            q_delta(4, 0, A)
             s_unit(0, SC, 1, banks[1][:])
             t_delta(6)
             t_delta(7)
             s_unit(0, SC, 2, banks[2][:])
+            q_delta(5, 0, A)
+            c_delta(6, False)
             reorder(0, 0, on_vector)
-            cq_delta(6)
             s_unit(0, SC, 3, banks[3][:])
+            c_delta(7, False)
             mx1(0, SC, 4, [0])
             reorder(2, 0, on_vector)
-            cq_delta(7)
+            q_delta(6, 0, A)
             mx1(0, SC, 5, [1])
             t_pair(0, 0, 2)
             t_pair(2, 0, 3)
-            q_delta(7, 1, A)
+            q_delta(7, 0, A)
             reorder(0, 1)
             reorder(2, 1)
             mx1(0, SC, 6, [0])
@@ -351,7 +354,7 @@ def tile_scenario_book_pnl_e3_kernel(tc, g_words, g_scales, delta, carry, stress
             v_hold(0, 1)
 
             steps = [(0, 1), (2, 1)] + [(j, g) for j in range(J, S // P, 2) for g in range(G)]
-            three = [0, 4, 1]
+            three = [1, 0, 4]
 
             def t_run(k):
                 for m in range(k, min(k + 3, len(steps))):
@@ -399,10 +402,13 @@ def tile_scenario_book_pnl_e3_kernel(tc, g_words, g_scales, delta, carry, stress
                     if t == 1:
                         reorder(*steps[k + 2])
                     if t == 0:
+                        if k == 6:
+                            v_mul(jb, gb)
                         while pending:
                             v_out(pending.pop(0))
-                        v_mul(jb, gb)
-                    if take and t in (1, 3):
+                        if k != 6:
+                            v_mul(jb, gb)
+                    if take and (t == 3 or (t == 1 and k > 5)):
                         mx2(take[0])
                         pending.append(take.pop(0))
                         if t == 1:

@@ -22,6 +22,8 @@ G = I // 512
 SC = 512
 C = S // SC
 J = SC // P
+UNIT_BUFS = 4
+PNL_BUFS = 4
 
 
 def tile_scenario_book_pnl_e3_kernel(tc, g_words, g_scales, delta, carry, stress, hold, hedge, out):
@@ -35,12 +37,11 @@ def tile_scenario_book_pnl_e3_kernel(tc, g_words, g_scales, delta, carry, stress
         make_identity(nc, ident[:])
         banks = [psum.tile([P, 512], F32, name="bank%d" % k) for k in range(8)]
 
-        d_raw = [work.tile([P, F], BF16, name="d_words", bufs=4) for i in range(4)]
-        d_raw = d_raw + [keep.tile([P, F], BF16, name="d_raw%d" % i) for i in range(4, 8)]
-        gw_cuts = [0, SC, SC + 2 * P, 2 * SC, 3 * SC, S]
-        gw = [keep.tile([P, A, gw_cuts[k + 1] - gw_cuts[k]], U32, name="gw%d" % k, align_bytes=64) for k in range(5)]
+
+        d_raw = [work.tile([P, F], BF16, name="d_words", bufs=8) for i in range(8)]
+        gw = [keep.tile([P, A, SC], U32, name="gw%d" % c, align_bytes=64) for c in range(C)]
         st = [keep.tile([P, 2, I], BF16, name="st%d" % k) for k in range(S // (2 * P))]
-        hg = [keep.tile([P, J, B], BF16, name="hg%d" % c) for c in range(C)]
+        hg = {}
         gs_cuts = [0, SC, 2 * SC, S]
         gs = [keep.tile([P, A, gs_cuts[k + 1] - gs_cuts[k]], U8, name="gs%d" % k, align_bytes=64) for k in range(3)]
         h_raw = [keep.tile([P, 4, B], BF16, name="h_raw%d" % g) for g in range(G)]
@@ -68,20 +69,21 @@ def tile_scenario_book_pnl_e3_kernel(tc, g_words, g_scales, delta, carry, stress
         d_grp = {}
         d_re = {}
         acc_out = {}
-        unit_turn = [0]
+        turn = [0]
 
         def load_d(i):
             nc.sync.dma_start(out=d_raw[i][:], in_=d_view[i // 4, i % 4])
 
-        def load_g(k, lo=0, hi=A):
+        def load_g(c, lo=0, hi=A):
             nc.sync.dma_start(
-                out=gw[k][:, lo:hi].bitcast(I32), in_=gw_view[:, lo:hi, 4 * gw_cuts[k] : 4 * gw_cuts[k + 1]].bitcast(I32)
+                out=gw[c][:, lo:hi].bitcast(I32), in_=gw_view[:, lo:hi, 4 * SC * c : 4 * SC * (c + 1)].bitcast(I32)
             )
 
         def load_st(k):
             nc.sync.dma_start(out=st[k][:], in_=st_view[k])
 
         def load_hg(c):
+            hg[c] = work.tile([P, J, B], BF16, name="hg", bufs=3)
             nc.sync.dma_start(out=hg[c][:], in_=hg_view[c])
 
         def load_h(g):
@@ -94,9 +96,9 @@ def tile_scenario_book_pnl_e3_kernel(tc, g_words, g_scales, delta, carry, stress
                     in_=gs_view[4 * q : 4 * q + 4, :, gs_cuts[k] // 4 : gs_cuts[k + 1] // 4],
                 )
 
-        def unit_bank(pool_banks):
-            k = pool_banks[unit_turn[0] % len(pool_banks)]
-            unit_turn[0] = unit_turn[0] + 1
+        def next_bank(ring):
+            k = ring[turn[0] % len(ring)]
+            turn[0] = turn[0] + 1
             return banks[k]
 
         def d_banks(i):
@@ -116,23 +118,27 @@ def tile_scenario_book_pnl_e3_kernel(tc, g_words, g_scales, delta, carry, stress
                     nc.tensor.transpose(dst, words, ident[:])
 
         def r_delta(i):
-            d_re[i] = work.tile([P, A, 2, P], F32, name="d_words", bufs=4)
+            d_re[i] = work.tile([P, A, 2, P], F32, name="d_words", bufs=8)
             nc.vector.tensor_copy(
                 out=d_re[i][:].rearrange("p a u (v m) -> p v a u m", v=2),
                 in_=d_raw[i][:].bitcast(F32).rearrange("p (a v m u) -> p v a u m", a=A, v=2, u=2),
             )
 
-        def c_delta(i, first_on_scalar):
+        def c_first(i, copy):
             one, two = d_banks(i)
-            grp = work.tile([P, A, P, 4], BF16, name="d_grp", align_bytes=64)
-            d_grp[i] = grp
-            first_copy = nc.scalar.copy if first_on_scalar else nc.vector.tensor_copy
-            first_copy(
-                out=grp[:, 0].rearrange("p m t -> p (m t)").bitcast(F32).rearrange("p (m u) -> p m u", u=2),
+            d_grp[i] = work.tile([P, A, P, 4], BF16, name="d_grp", align_bytes=64)
+            copy(
+                out=d_grp[i][:, 0].rearrange("p m t -> p (m t)").bitcast(F32).rearrange("p (m u) -> p m u", u=2),
                 in_=one.rearrange("p u m -> p m u"),
             )
-            nc.scalar.copy(
-                out=grp[:, 1:3].rearrange("p a m t -> p a (m t)").bitcast(F32).rearrange("p a (m u) -> p a m u", u=2),
+
+        def c_rest(i, copy):
+            one, two = d_banks(i)
+            copy(
+                out=d_grp[i][:, 1:3]
+                .rearrange("p a m t -> p a (m t)")
+                .bitcast(F32)
+                .rearrange("p a (m u) -> p a m u", u=2),
                 in_=two.rearrange("p a u m -> p a m u"),
             )
 
@@ -143,28 +149,28 @@ def tile_scenario_book_pnl_e3_kernel(tc, g_words, g_scales, delta, carry, stress
                 in_=d_grp[i][:, lo:hi].rearrange("p a m t -> p (a m t)"),
             )
 
-        def mx1(s0, n, i, pool_banks):
-            acc = unit_bank(pool_banks)[:, 0:n]
+        def mx1(s0, n, i, ring):
+            acc = next_bank(ring)[:, 0:n]
             mx1_passes(s0, n, i, acc)
             s_unit(s0, n, i, acc)
 
-        def mx1_two(s0, i, pool_banks, n=P):
-            bank = unit_bank(pool_banks)
+        def mx1_two(s0, n, i, ring):
+            bank = next_bank(ring)
             for m in range(2):
                 mx1_passes(s0, n, i + m, bank[:, n * m : n * (m + 1)])
             for m in range(2):
                 s_unit(s0, n, i + m, bank[:, n * m : n * (m + 1)])
 
         def mx1_passes(s0, n, i, acc, passes=range(A)):
-            kw = max(k for k in range(5) if gw_cuts[k] <= s0)
-            ks = max(k for k in range(3) if gs_cuts[k] <= s0)
-            w0, c0 = s0 - gw_cuts[kw], s0 - gs_cuts[ks]
+            c = s0 // SC
+            ks = min(c, 2)
+            w0, c0 = s0 - SC * c, s0 - gs_cuts[ks]
             for a in passes:
                 nc.tensor.matmul_mx(
                     out=acc,
                     lhsT=d_codes[i][:, a, :].bitcast(E4),
                     lhsT_scale=d_sc[i][:, a, :],
-                    rhs=gw[kw][:, a, w0 : w0 + n].bitcast(E5),
+                    rhs=gw[c][:, a, w0 : w0 + n].bitcast(E5),
                     rhs_scale=gs[ks][:, a, c0 : c0 + n],
                     start=(a == 0),
                     stop=(a == A - 1),
@@ -173,43 +179,36 @@ def tile_scenario_book_pnl_e3_kernel(tc, g_words, g_scales, delta, carry, stress
         def s_unit(s0, n, i, acc):
             g, t = i // 4, i % 4
             if t == 0:
-                if n == SC:
-                    units[(s0, g)] = work.tile([P, 4, n], F32, name="unit_wide", bufs=2)
-                else:
-                    units[(s0, g)] = work.tile([P, 4, n], F32, name="unit", bufs=4)
+                tile = work.tile([P, 4, n], F32, name="unit", bufs=UNIT_BUFS)
+                for j in range(s0 // P, (s0 + n) // P):
+                    units[(j, g)] = (tile, P * j - s0)
             nc.scalar.activation(
-                out=units[(s0, g)][:, t, :], in_=acc, func=ACT.Identity, bias=ca[:, g, t : t + 1], scale=1.0
+                out=units[(s0 // P, g)][0][:, t, :], in_=acc, func=ACT.Identity, bias=ca[:, g, t : t + 1], scale=1.0
             )
 
-        def reorder(j, g, copy=nc.scalar.copy):
-            st_re[(j, g)] = work.tile([P, 2, 2, P], F32, name="st_re", bufs=6)
+        def reorder(j, g, copy):
+            st_re[(j, g)] = work.tile([P, 2, 2, P], F32, name="st_re", bufs=8)
             words = st[j // 2][:].bitcast(F32).rearrange("p j (g m u) -> p g j u m", g=G, u=2)
             copy(out=st_re[(j, g)][:], in_=words[:, g])
 
-        def t_stress(j, g, k, half):
-            dst = banks[k][:, 256 * half : 256 * (half + 1)]
-            for u in range(2):
-                if (j - j % 2, g) in st_re:
-                    words = st_re[(j - j % 2, g)][:, j % 2, u, :]
-                else:
-                    words = st[j // 2][:, j % 2, :].bitcast(F32)[:, 256 * g + u : 256 * (g + 1) : 2]
-                nc.tensor.transpose(dst.rearrange("p (c u i) -> p u c i", u=2, i=4)[:, u], words, ident[:])
-            st_bank[(j, g)] = (k, half)
-
         def t_pair(j, g, k):
-            t_stress(j, g, k, 0)
-            t_stress(j + 1, g, k, 1)
+            for half in range(2):
+                dst = banks[k][:, 256 * half : 256 * (half + 1)]
+                for u in range(2):
+                    nc.tensor.transpose(
+                        dst.rearrange("p (c u i) -> p u c i", u=2, i=4)[:, u], st_re[(j, g)][:, half, u, :], ident[:]
+                    )
+                st_bank[(j + half, g)] = (k, half)
 
         def v_mul(j, g, blocks=2):
             n = P * blocks
-            if g == 0:
-                pnl[j] = work.tile([P, G, n, 4], BF16, name="pnl", align_bytes=64, bufs=4)
-            u0 = 0 if j < J else P * j
-            cols = slice(j * P - u0, j * P - u0 + n)
+            if j not in pnl:
+                pnl[j] = work.tile([P, G, n, 4], BF16, name="pnl", align_bytes=64, bufs=PNL_BUFS)
+            tile, c0 = units[(j, g)]
             k, half = st_bank[(j, g)]
             nc.vector.tensor_tensor(
                 out=pnl[j][:, g].rearrange("p (c i) (u e) -> p c u e i", i=4, u=2),
-                in0=units[(u0, g)][:, :, cols].rearrange("p (u e) (c i) -> p c u e i", i=4, u=2),
+                in0=tile[:, :, c0 : c0 + n].rearrange("p (u e) (c i) -> p c u e i", i=4, u=2),
                 in1=banks[k][:, 256 * half : 256 * (half + blocks)]
                 .bitcast(BF16)
                 .rearrange("p (c u i e) -> p c u e i", u=2, i=4, e=2),
@@ -218,43 +217,41 @@ def tile_scenario_book_pnl_e3_kernel(tc, g_words, g_scales, delta, carry, stress
 
         def v_quant(j, lo=0, hi=G):
             n = pnl[j].shape[2]
-            if lo == 0:
-                pnl_codes[j] = work.tile([P, G, n], U32, name="pnl_codes", align_bytes=64, bufs=5)
-                pnl_sc[j] = work.tile([P, G, n], U8, name="pnl_sc", align_bytes=64, bufs=5)
+            if j not in pnl_codes:
+                pnl_codes[j] = work.tile([P, G, n], U32, name="pnl_codes", align_bytes=64, bufs=4)
+                pnl_sc[j] = work.tile([P, G, n], U8, name="pnl_sc", align_bytes=64, bufs=4)
             nc.vector.quantize_mx(
                 out=pnl_codes[j][:, lo:hi].rearrange("p g s -> p (g s)").bitcast(E5),
                 scales=pnl_sc[j][:, lo:hi].rearrange("p g s -> p (g s)"),
                 in_=pnl[j][:, lo:hi].rearrange("p g s t -> p (g s t)"),
             )
 
-        def mx2_pass(j, g):
-            acc_out[j] = banks[2 + j % 2]
+        def mx2_pass(j, g, acc, b0=0, n=B):
             j0 = j if j in pnl_codes else j - 1
             cols = slice(P * (j - j0), P * (j - j0 + 1))
             nc.tensor.matmul_mx(
-                out=acc_out[j][:],
+                out=acc,
                 lhsT=pnl_codes[j0][:, g, cols].bitcast(E5),
                 lhsT_scale=pnl_sc[j0][:, g, cols],
-                rhs=h_codes[:, g, :].bitcast(E4),
-                rhs_scale=h_sc[:, g, :],
+                rhs=h_codes[:, g, b0 : b0 + n].bitcast(E4),
+                rhs_scale=h_sc[:, g, b0 : b0 + n],
                 start=(g == 0),
                 stop=(g == G - 1),
             )
 
-        def mx2(j):
+        def mx2(j, ring):
+            acc_out[j] = next_bank(ring)
             for g in range(G):
-                mx2_pass(j, g)
+                mx2_pass(j, g, acc_out[j][:])
 
         def v_out(j):
             res = work.tile([P, B], F32, name="res", bufs=6)
             nc.vector.tensor_tensor(out=res[:], in0=acc_out[j][:], in1=hg[j // J][:, j % J, :], op=ALU.add)
             nc.sync.dma_start(out=out[P * j : P * (j + 1), :], in_=res[:])
-            if j in (1, 5):
-                load_hg(2 + j // 4)
 
-        def v_hold(g, h):
+        def i_hold(g, h, copy):
             cols = slice(256 * h, 256 * (h + 1))
-            nc.vector.tensor_copy(
+            copy(
                 out=h_grp[g][:, cols, :].rearrange("p (c i) t -> p c t i", i=4),
                 in_=h_raw[g][:, :, cols].rearrange("p t (c i) -> p c t i", i=4),
             )
@@ -264,208 +261,224 @@ def tile_scenario_book_pnl_e3_kernel(tc, g_words, g_scales, delta, carry, stress
                 out=h_codes[:, g].bitcast(E4), scales=h_sc[:, g], in_=h_grp[g][:].rearrange("p w j -> p (w j)")
             )
 
+        on_vector = nc.vector.tensor_copy
+        on_scalar = nc.scalar.copy
+
         with tc.manual_schedule():
             nc.scalar.dma_start(out=ca_raw[:, :, 0:4], in_=carry.rearrange("(g p t) -> p g t", g=G, t=4))
             for k in range(3):
                 nc.vector.memset(gs[k][:].rearrange("p a n -> p (a n)").bitcast(I32), 0)
             nc.scalar.activation(out=ca[:], in_=ca_raw[:, :, 0:4], func=ACT.Identity, scale=1.0)
-            load_d(0)
-            load_d(1)
-            load_d(2)
-            load_d(3)
+            for i in range(4):
+                load_d(i)
             load_gs(0)
             load_g(0, 0, 1)
-            load_d(4)
             load_g(0, 1, 2)
-            load_d(5)
+            load_d(4)
             load_g(0, 2, 3)
+            load_d(5)
             load_d(6)
             load_d(7)
             load_st(0)
-            load_h(0)
             load_st(1)
-            load_st(2)
             load_gs(1)
             load_g(1)
-            load_h(1)
+            load_st(2)
+            load_h(0)
             load_st(3)
-            load_g(2)
+            load_h(1)
             load_gs(2)
+            load_g(2)
             load_st(4)
-            load_hg(0)
-            load_g(3)
             load_st(5)
-            load_hg(1)
+            load_hg(0)
             load_st(6)
-            load_g(4)
+            load_hg(1)
+            load_g(3)
             load_st(7)
-
-            on_vector = nc.vector.tensor_copy
-
-            def cq_delta(i):
-                c_delta(i, False)
-                if i > 0:
-                    q_delta(i - 1, 1, A)
-                q_delta(i, 0, 1)
+            load_hg(2)
 
             for i in range(4):
                 t_delta(i)
-                cq_delta(i)
+                c_first(i, on_vector)
+                c_rest(i, on_scalar)
+                if i > 0:
+                    q_delta(i - 1, 1, A)
+                q_delta(i, 0, 1)
             q_delta(3, 1, A)
             for a in range(A - 1):
                 for i in range(4):
                     mx1_passes(0, SC, i, banks[i][:], [a])
             mx1_passes(0, SC, 0, banks[0][:], [A - 1])
             s_unit(0, SC, 0, banks[0][:])
-            for i in range(4, 6):
-                r_delta(i)
+            r_delta(4)
+            r_delta(5)
             t_delta(4)
             t_delta(5)
             for i in range(1, 4):
                 mx1_passes(0, SC, i, banks[i][:], [A - 1])
-            for i in range(4, 6):
-                c_delta(i, False)
-                r_delta(i + 2)
+            c_first(4, on_vector)
+            c_rest(4, on_scalar)
+            r_delta(6)
+            c_first(5, on_vector)
+            c_rest(5, on_scalar)
+            r_delta(7)
             q_delta(4, 0, A)
             s_unit(0, SC, 1, banks[1][:])
             t_delta(6)
             t_delta(7)
             s_unit(0, SC, 2, banks[2][:])
-            q_delta(5, 0, A)
-            c_delta(6, False)
-            reorder(0, 0, on_vector)
             s_unit(0, SC, 3, banks[3][:])
-            c_delta(7, False)
-            mx1(0, SC, 4, [0])
+            reorder(0, 0, on_vector)
+            q_delta(5, 0, A)
+            c_first(6, on_vector)
+            c_rest(6, on_scalar)
             reorder(2, 0, on_vector)
+            c_first(7, on_vector)
+            c_rest(7, on_scalar)
+            reorder(0, 1, on_vector)
+            mx1(0, SC, 4, [0])
             q_delta(6, 0, A)
             mx1(0, SC, 5, [1])
             t_pair(0, 0, 2)
             t_pair(2, 0, 3)
+            t_pair(0, 1, 4)
             q_delta(7, 0, A)
-            reorder(0, 1)
-            reorder(2, 1)
-            mx1(0, SC, 6, [0])
-            mx1(0, SC, 7, [1])
             v_mul(0, 0)
-            reorder(4, 0, on_vector)
-            v_hold(0, 0)
             v_mul(2, 0)
-            v_hold(0, 1)
+            ring = [6, 7, 0, 1]
+            turn[0] = 0
+            stress_banks = [2, 3, 4, 5]
+            pieces = [(0, 0), (2, 0), (0, 1), (2, 1), (4, 0), (6, 0), (4, 1), (6, 1)]
+            pieces = pieces + [(j, g) for j in range(8, 16, 2) for g in range(G)]
 
-            steps = [(0, 1), (2, 1)] + [(j, g) for j in range(J, S // P, 2) for g in range(G)]
-            three = [1, 0, 4]
+            def t_run(order):
+                for m in order:
+                    t_pair(pieces[m][0], pieces[m][1], stress_banks[m % 4])
 
-            def t_run(k):
-                for m in range(k, min(k + 3, len(steps))):
-                    t_pair(steps[m][0], steps[m][1], 5 + m % 3)
+            def r_piece(m, copy):
+                reorder(pieces[m][0], pieces[m][1], copy)
 
-            unit_turn[0] = 0
-            t_run(0)
-            reorder(4, 1)
-            five = [4, 0, 1, 2, 3]
-            for t in range(4):
-                mx1(SC, 2 * P, t, five)
-                if t == 1:
-                    reorder(6, 0)
+            def step(j, g):
+                mx1_two(P * j, 2 * P, 4 * g, ring)
+                mx1_two(P * j, 2 * P, 4 * g + 2, ring)
+
+            r_piece(3, on_scalar)
+            mx1(0, SC, 6, ring)
+            r_piece(4, on_scalar)
+            mx1(0, SC, 7, ring)
+            i_hold(0, 0, on_vector)
+            r_piece(5, on_vector)
             v_mul(0, 1)
+            mx1(SC, SC, 0, ring)
+            mx1(SC, SC, 1, ring)
+            t_run([3, 4, 5])
             v_mul(2, 1)
-            for t in range(4):
-                mx1(SC, 2 * P, 4 + t, five)
-                if t == 1:
-                    reorder(6, 1)
-            v_mul(4, 0)
-            mx1(SC + 2 * P, 2 * P, 0, five)
-            mx1(SC + 2 * P, 2 * P, 1, five)
-            reorder(8, 0)
-            mx1(SC + 2 * P, 2 * P, 2, five)
-            t_run(3)
-            v_hold(1, 0)
-            v_hold_q(0)
-            v_hold(1, 1)
+            i_hold(1, 0, on_scalar)
+            mx1(SC, SC, 2, ring)
+            mx1(SC, SC, 3, ring)
+            r_piece(6, on_scalar)
+            i_hold(0, 1, on_vector)
             v_quant(0)
+            v_hold_q(0)
+            v_mul(4, 0)
+            mx1(SC, SC, 4, ring)
+            r_piece(7, on_scalar)
+            mx1(SC, SC, 5, ring)
+            r_piece(8, on_scalar)
+            v_quant(2)
+            i_hold(1, 1, on_vector)
+            v_mul(6, 0)
             v_hold_q(1)
-            unit_turn[0] = 0
-            mx1(SC + 2 * P, 2 * P, 3, three)
+            mx1(SC, SC, 6, ring)
+            mx1(SC, SC, 7, ring)
+            t_run([6, 7, 8])
+            r_piece(9, on_scalar)
+            r_piece(10, on_scalar)
+            step(8, 0)
+            r_piece(11, on_scalar)
             v_mul(4, 1)
-            ready = [0, 1]
-            pending = []
-            to_quant = [2, 4]
-            for k in range(5, len(steps) - 2):
-                j, g = steps[k]
-                jb, gb = steps[k - 1]
-                count = 1 if k < 7 else 2
-                take = ready[:count]
-                ready = ready[count:]
-                for t in range(4):
-                    mx1(P * j, 2 * P, 4 * g + t, three)
-                    if t == 1:
-                        reorder(*steps[k + 2])
-                    if t == 0:
-                        if k == 6:
-                            v_mul(jb, gb)
-                        while pending:
-                            v_out(pending.pop(0))
-                        if k != 6:
-                            v_mul(jb, gb)
-                    if take and (t == 3 or (t == 1 and k > 5)):
-                        mx2(take[0])
-                        pending.append(take.pop(0))
-                        if t == 1:
-                            v_out(pending.pop(0))
-                            if gb == G - 1:
-                                to_quant.append(jb)
-                            if to_quant and k > 5:
-                                ready.extend([to_quant[0], to_quant[0] + 1])
-                                v_quant(to_quant.pop(0))
-                if k % 3 == 0:
-                    t_run(k)
-
-            ja, jz = S // P - 2, S // P - 1
-            for g in range(G):
-                t_stress(ja, g, 5, g)
-            for g in range(G):
-                t_stress(jz, g, 6, g)
-            mx1_two(P * ja, 0, three)
-            v_mul(ja - 2, 1)
-            v_quant(ja - 2)
-            v_out(pending.pop(0))
-            mx1_two(P * ja, 2, three)
-            mx1_two(P * ja, 4, three)
-            v_mul(ja, 0, 1)
-            mx1_two(P * ja, 6, three)
-            mx2(ja - 2)
-            mx2(ja - 1)
-            v_mul(ja, 1, 1)
-            v_out(ja - 2)
-            v_quant(ja)
-            v_out(ja - 1)
-            mx1_two(P * jz, 0, three)
-            mx1_two(P * jz, 2, three)
+            mx2(0, ring)
+            mx2(1, ring)
+            v_mul(6, 1)
+            v_out(0)
+            v_quant(4)
+            v_out(1)
+            step(8, 1)
+            mx2(2, ring)
+            t_run([9, 10, 11])
+            mx2(3, ring)
+            r_piece(12, on_scalar)
+            v_mul(8, 0)
+            v_out(2)
+            v_quant(6)
+            v_out(3)
+            load_hg(3)
+            step(10, 0)
+            mx2(4, ring)
+            mx2(5, ring)
+            r_piece(13, on_scalar)
+            v_mul(8, 1)
+            v_out(4)
+            v_mul(10, 0)
+            v_out(5)
+            step(10, 1)
+            mx2(6, ring)
+            t_run([12, 13])
+            mx2(7, ring)
+            r_piece(14, on_scalar)
+            r_piece(15, on_scalar)
+            v_quant(8)
+            v_out(6)
+            v_mul(10, 1)
+            v_out(7)
+            step(12, 0)
+            step(12, 1)
+            mx2(8, ring)
+            mx2(9, ring)
+            t_run([14, 15])
+            v_quant(10)
+            v_mul(12, 0)
+            v_mul(12, 1)
+            v_out(8)
+            v_quant(12)
+            v_out(9)
+            ja, jy, jz = S // P - 4, S // P - 2, S // P - 1
+            mx1_two(P * jy, P, 0, ring)
+            mx1_two(P * jy, P, 2, ring)
+            mx2(10, [2])
+            mx1_two(P * jy, P, 4, [3])
+            mx1_two(P * jy, P, 6, ring)
+            v_mul(jy, 0, 1)
+            v_out(10)
+            mx2(11, ring)
+            mx1_two(P * jz, P, 0, ring)
+            mx1_two(P * jz, P, 2, ring)
+            v_mul(jy, 1, 1)
+            v_out(11)
+            v_quant(jy)
             v_mul(jz, 0, 1)
-            mx1_two(P * jz, 4, three)
-            mx1(P * jz, P, 6, [7])
-            mx1(P * jz, P, 7, [5])
-            mx2(ja)
-            v_mul(jz, 1, 1)
-            v_quant(jz, 0, 1)
-            v_quant(jz, 1, G)
+            mx2(ja, [3])
+            mx1_two(P * jz, P, 4, [2])
+            mx1(P * jz, P, 6, ring)
+            turn[0] = turn[0] + 1
+            mx1(P * jz, P, 7, ring)
+            mx2(ja + 1, ring)
+            mx2(jy, [4])
             v_out(ja)
+            v_quant(jz, 0, 1)
+            v_mul(jz, 1, 1)
+            v_quant(jz, 1, G)
+            v_out(ja + 1)
+            v_out(jy)
+            last_banks = [banks[2], banks[3]]
             for g in range(G):
                 for h in range(2):
-                    nc.tensor.matmul_mx(
-                        out=banks[3 + 4 * h][:, 0 : B // 2],
-                        lhsT=pnl_codes[jz][:, g].bitcast(E5),
-                        lhsT_scale=pnl_sc[jz][:, g],
-                        rhs=h_codes[:, g, B // 2 * h : B // 2 * (h + 1)].bitcast(E4),
-                        rhs_scale=h_sc[:, g, B // 2 * h : B // 2 * (h + 1)],
-                        start=(g == 0),
-                        stop=(g == G - 1),
-                    )
+                    mx2_pass(jz, g, last_banks[h][:, 0 : B // 2], B // 2 * h, B // 2)
             for h in range(2):
                 cols = slice(B // 2 * h, B // 2 * (h + 1))
                 res = work.tile([P, B // 2], F32, name="res", bufs=6)
                 nc.vector.tensor_tensor(
-                    out=res[:], in0=banks[3 + 4 * h][:, 0 : B // 2], in1=hg[C - 1][:, J - 1, cols], op=ALU.add
+                    out=res[:], in0=last_banks[h][:, 0 : B // 2], in1=hg[C - 1][:, J - 1, cols], op=ALU.add
                 )
                 nc.sync.dma_start(out=out[P * jz : P * (jz + 1), cols], in_=res[:])

@@ -22,6 +22,7 @@ G = I // 512
 SC = 512
 C = S // SC
 J = SC // P
+PIECES = S // (2 * P)
 UNIT_BUFS = 4
 PNL_BUFS = 4
 
@@ -38,17 +39,20 @@ def tile_scenario_book_pnl_e3_kernel(tc, g_words, g_scales, delta, carry, stress
         banks = [psum.tile([P, 512], F32, name="bank%d" % k) for k in range(8)]
 
 
-        d_raw = [work.tile([P, F], BF16, name="d_words", bufs=8) for i in range(8)]
+        d_raw = [work.tile([P, F], BF16, name="d_words", bufs=4) for i in range(4)]
+        d_two = keep.tile([P, 2 * F], BF16, name="d_two")
+        d_raw = d_raw + [d_two[:, 0:F], d_two[:, F : 2 * F]]
+        d_raw = d_raw + [keep.tile([P, F], BF16, name="d_raw%d" % i) for i in range(6, 8)]
         gw = [keep.tile([P, A, SC], U32, name="gw%d" % c, align_bytes=64) for c in range(C)]
         st = [keep.tile([P, 2, I], BF16, name="st%d" % k) for k in range(S // (2 * P))]
         hg = {}
-        gs_cuts = [0, SC, 2 * SC, S]
-        gs = [keep.tile([P, A, gs_cuts[k + 1] - gs_cuts[k]], U8, name="gs%d" % k, align_bytes=64) for k in range(3)]
+        gs_cuts = [0, SC, 2 * SC, 3 * SC, S]
+        gs = [keep.tile([P, A, gs_cuts[k + 1] - gs_cuts[k]], U8, name="gs%d" % k, align_bytes=64) for k in range(C)]
         h_raw = [keep.tile([P, 4, B], BF16, name="h_raw%d" % g) for g in range(G)]
         h_grp = [keep.tile([P, B, 4], BF16, name="h_grp%d" % g, align_bytes=64) for g in range(G)]
         h_codes = keep.tile([P, G, B], U32, name="h_codes", align_bytes=64)
         h_sc = keep.tile([P, G, B], U8, name="h_sc", align_bytes=64)
-        ca_raw = keep.tile([P, G, 16], BF16, name="ca_raw")
+        ca_raw = keep.tile([P, 512], BF16, name="ca_raw")
         ca = keep.tile([P, G, 4], F32, name="ca")
         d_codes = [keep.tile([P, A, P], U32, name="d_codes%d" % i, align_bytes=64) for i in range(8)]
         d_sc = [keep.tile([P, A, P], U8, name="d_sc%d" % i, align_bytes=64) for i in range(8)]
@@ -56,8 +60,14 @@ def tile_scenario_book_pnl_e3_kernel(tc, g_words, g_scales, delta, carry, stress
         d_view = delta.rearrange("(g m t) k -> g t m k", g=G, t=4)
         gw_view = g_words.rearrange("g p n t -> p g (n t)")
         gs_view = g_scales.bitcast(I32).rearrange("a r n -> r a n")
-        st_view = stress.rearrange("(k j p) i -> k p j i", j=2, p=P)
-        hg_view = hedge.rearrange("(c j p) b -> c p j b", c=C, p=P)
+        d_two_view = delta.rearrange("(g m k t) f -> g k m (t f)", g=G, k=2, t=2)
+
+        def rows(array, k):
+            piece = array[2 * P * k : 2 * P * (k + 1), :]
+            if k < PIECES - 1:
+                return piece.rearrange("(p j) w -> p j w", j=2)
+            return piece.rearrange("(j p) w -> p j w", j=2)
+
         h_view = hold.rearrange("(g p j) w -> g p j w", g=G, j=4)
 
         units = {}
@@ -74,26 +84,29 @@ def tile_scenario_book_pnl_e3_kernel(tc, g_words, g_scales, delta, carry, stress
         def load_d(i):
             nc.sync.dma_start(out=d_raw[i][:], in_=d_view[i // 4, i % 4])
 
+        def load_d_two():
+            nc.sync.dma_start(out=d_two[:], in_=d_two_view[1, 0])
+
         def load_g(c, lo=0, hi=A):
             nc.sync.dma_start(
                 out=gw[c][:, lo:hi].bitcast(I32), in_=gw_view[:, lo:hi, 4 * SC * c : 4 * SC * (c + 1)].bitcast(I32)
             )
 
         def load_st(k):
-            nc.sync.dma_start(out=st[k][:], in_=st_view[k])
+            nc.sync.dma_start(out=st[k][:], in_=rows(stress, k))
 
-        def load_hg(c):
-            hg[c] = work.tile([P, J, B], BF16, name="hg", bufs=3)
-            nc.sync.dma_start(out=hg[c][:], in_=hg_view[c])
+        def load_hg(k):
+            hg[k] = work.tile([P, 2, B], BF16, name="hg", bufs=6)
+            nc.sync.dma_start(out=hg[k][:], in_=rows(hedge, k))
 
         def load_h(g):
             nc.sync.dma_start(out=h_raw[g][:], in_=h_view[g])
 
         def load_gs(k):
-            for q in range(4):
+            for r in range(4):
                 nc.sync.dma_start(
-                    out=gs[k][32 * q : 32 * q + 4].bitcast(I32),
-                    in_=gs_view[4 * q : 4 * q + 4, :, gs_cuts[k] // 4 : gs_cuts[k + 1] // 4],
+                    out=gs[k][r:P:32].bitcast(I32),
+                    in_=gs_view[r:16:4, :, gs_cuts[k] // 4 : gs_cuts[k + 1] // 4],
                 )
 
         def next_bank(ring):
@@ -118,7 +131,7 @@ def tile_scenario_book_pnl_e3_kernel(tc, g_words, g_scales, delta, carry, stress
                     nc.tensor.transpose(dst, words, ident[:])
 
         def r_delta(i):
-            d_re[i] = work.tile([P, A, 2, P], F32, name="d_words", bufs=8)
+            d_re[i] = work.tile([P, A, 2, P], F32, name="d_words", bufs=4)
             nc.vector.tensor_copy(
                 out=d_re[i][:].rearrange("p a u (v m) -> p v a u m", v=2),
                 in_=d_raw[i][:].bitcast(F32).rearrange("p (a v m u) -> p v a u m", a=A, v=2, u=2),
@@ -163,7 +176,7 @@ def tile_scenario_book_pnl_e3_kernel(tc, g_words, g_scales, delta, carry, stress
 
         def mx1_passes(s0, n, i, acc, passes=range(A)):
             c = s0 // SC
-            ks = min(c, 2)
+            ks = c
             w0, c0 = s0 - SC * c, s0 - gs_cuts[ks]
             for a in passes:
                 nc.tensor.matmul_mx(
@@ -182,9 +195,11 @@ def tile_scenario_book_pnl_e3_kernel(tc, g_words, g_scales, delta, carry, stress
                 tile = work.tile([P, 4, n], F32, name="unit", bufs=UNIT_BUFS)
                 for j in range(s0 // P, (s0 + n) // P):
                     units[(j, g)] = (tile, P * j - s0)
-            nc.scalar.activation(
-                out=units[(s0 // P, g)][0][:, t, :], in_=acc, func=ACT.Identity, bias=ca[:, g, t : t + 1], scale=1.0
-            )
+            dst = units[(s0 // P, g)][0][:, t, :]
+            if s0 < S - 2 * P:
+                dst = dst.rearrange("p (k j m) -> p k j m", j=2, m=P)
+                acc = acc.rearrange("p (k m j) -> p k j m", j=2, m=P)
+            nc.scalar.activation(out=dst, in_=acc, func=ACT.Identity, bias=ca[:, g, t : t + 1], scale=1.0)
 
         def reorder(j, g, copy):
             st_re[(j, g)] = work.tile([P, 2, 2, P], F32, name="st_re", bufs=8)
@@ -246,8 +261,8 @@ def tile_scenario_book_pnl_e3_kernel(tc, g_words, g_scales, delta, carry, stress
 
         def v_out(j):
             res = work.tile([P, B], F32, name="res", bufs=6)
-            nc.vector.tensor_tensor(out=res[:], in0=acc_out[j][:], in1=hg[j // J][:, j % J, :], op=ALU.add)
-            nc.sync.dma_start(out=out[P * j : P * (j + 1), :], in_=res[:])
+            nc.vector.tensor_tensor(out=res[:], in0=acc_out[j][:], in1=hg[j // 2][:, j % 2, :], op=ALU.add)
+            nc.sync.dma_start(out=rows(out, j // 2)[:, j % 2], in_=res[:])
 
         def i_hold(g, h, copy):
             cols = slice(256 * h, 256 * (h + 1))
@@ -265,18 +280,17 @@ def tile_scenario_book_pnl_e3_kernel(tc, g_words, g_scales, delta, carry, stress
         on_scalar = nc.scalar.copy
 
         with tc.manual_schedule():
-            nc.scalar.dma_start(out=ca_raw[:, :, 0:4], in_=carry.rearrange("(g p t) -> p g t", g=G, t=4))
-            for k in range(3):
+            nc.vector.memset(ca_raw[:], 0)
+            for k in range(C):
                 nc.vector.memset(gs[k][:].rearrange("p a n -> p (a n)").bitcast(I32), 0)
-            nc.scalar.activation(out=ca[:], in_=ca_raw[:, :, 0:4], func=ACT.Identity, scale=1.0)
             for i in range(4):
                 load_d(i)
+            nc.sync.dma_start(out=ca_raw[0:G, :], in_=carry.rearrange("(g w) -> g w", g=G))
             load_gs(0)
             load_g(0, 0, 1)
             load_g(0, 1, 2)
-            load_d(4)
+            load_d_two()
             load_g(0, 2, 3)
-            load_d(5)
             load_d(6)
             load_d(7)
             load_st(0)
@@ -284,19 +298,23 @@ def tile_scenario_book_pnl_e3_kernel(tc, g_words, g_scales, delta, carry, stress
             load_gs(1)
             load_g(1)
             load_st(2)
-            load_h(0)
             load_st(3)
+            load_h(0)
             load_h(1)
             load_gs(2)
             load_g(2)
             load_st(4)
             load_st(5)
             load_hg(0)
-            load_st(6)
             load_hg(1)
-            load_g(3)
-            load_st(7)
+            load_st(6)
             load_hg(2)
+            load_gs(3)
+            load_g(3)
+            load_hg(3)
+            load_st(7)
+            load_hg(4)
+            load_hg(5)
 
             for i in range(4):
                 t_delta(i)
@@ -305,25 +323,34 @@ def tile_scenario_book_pnl_e3_kernel(tc, g_words, g_scales, delta, carry, stress
                 if i > 0:
                     q_delta(i - 1, 1, A)
                 q_delta(i, 0, 1)
+            for u in range(2):
+                nc.tensor.transpose(
+                    banks[4][:, P * (2 + u) : P * (3 + u)], ca_raw[:].bitcast(F32)[:, u:256:2], ident[:]
+                )
+            nc.scalar.activation(
+                out=ca[:].rearrange("p g (u e) -> p u g e", u=2),
+                in_=banks[4][:, 2 * P : 4 * P].bitcast(BF16).rearrange("p (u r e) -> p u r e", u=2, e=2)[:, :, 0:G, :],
+                func=ACT.Identity,
+                scale=1.0,
+            )
             q_delta(3, 1, A)
             for a in range(A - 1):
                 for i in range(4):
                     mx1_passes(0, SC, i, banks[i][:], [a])
-            mx1_passes(0, SC, 0, banks[0][:], [A - 1])
-            s_unit(0, SC, 0, banks[0][:])
             r_delta(4)
             r_delta(5)
             t_delta(4)
             t_delta(5)
-            for i in range(1, 4):
+            for i in range(4):
                 mx1_passes(0, SC, i, banks[i][:], [A - 1])
             c_first(4, on_vector)
             c_rest(4, on_scalar)
-            r_delta(6)
             c_first(5, on_vector)
             c_rest(5, on_scalar)
+            r_delta(6)
             r_delta(7)
             q_delta(4, 0, A)
+            s_unit(0, SC, 0, banks[0][:])
             s_unit(0, SC, 1, banks[1][:])
             t_delta(6)
             t_delta(7)
@@ -367,7 +394,6 @@ def tile_scenario_book_pnl_e3_kernel(tc, g_words, g_scales, delta, carry, stress
             mx1(0, SC, 6, ring)
             r_piece(4, on_scalar)
             mx1(0, SC, 7, ring)
-            i_hold(0, 0, on_vector)
             r_piece(5, on_vector)
             v_mul(0, 1)
             mx1(SC, SC, 0, ring)
@@ -378,6 +404,7 @@ def tile_scenario_book_pnl_e3_kernel(tc, g_words, g_scales, delta, carry, stress
             mx1(SC, SC, 2, ring)
             mx1(SC, SC, 3, ring)
             r_piece(6, on_scalar)
+            i_hold(0, 0, on_vector)
             i_hold(0, 1, on_vector)
             v_quant(0)
             v_hold_q(0)
@@ -385,18 +412,17 @@ def tile_scenario_book_pnl_e3_kernel(tc, g_words, g_scales, delta, carry, stress
             mx1(SC, SC, 4, ring)
             r_piece(7, on_scalar)
             mx1(SC, SC, 5, ring)
-            r_piece(8, on_scalar)
-            v_quant(2)
             i_hold(1, 1, on_vector)
-            v_mul(6, 0)
+            v_quant(2)
             v_hold_q(1)
+            v_mul(6, 0)
             mx1(SC, SC, 6, ring)
             mx1(SC, SC, 7, ring)
-            t_run([6, 7, 8])
+            t_run([6, 7])
+            r_piece(8, on_scalar)
             r_piece(9, on_scalar)
-            r_piece(10, on_scalar)
             step(8, 0)
-            r_piece(11, on_scalar)
+            r_piece(10, on_scalar)
             v_mul(4, 1)
             mx2(0, ring)
             mx2(1, ring)
@@ -404,16 +430,19 @@ def tile_scenario_book_pnl_e3_kernel(tc, g_words, g_scales, delta, carry, stress
             v_out(0)
             v_quant(4)
             v_out(1)
-            step(8, 1)
+            mx1_two(8 * P, 2 * P, 4, ring)
+            t_run([8, 9, 10])
+            mx1_two(8 * P, 2 * P, 6, ring)
             mx2(2, ring)
-            t_run([9, 10, 11])
             mx2(3, ring)
+            r_piece(11, on_scalar)
             r_piece(12, on_scalar)
             v_mul(8, 0)
             v_out(2)
             v_quant(6)
             v_out(3)
-            load_hg(3)
+            load_hg(6)
+            load_hg(7)
             step(10, 0)
             mx2(4, ring)
             mx2(5, ring)
@@ -422,9 +451,10 @@ def tile_scenario_book_pnl_e3_kernel(tc, g_words, g_scales, delta, carry, stress
             v_out(4)
             v_mul(10, 0)
             v_out(5)
-            step(10, 1)
+            mx1_two(10 * P, 2 * P, 4, ring)
+            t_run([11, 12, 13])
+            mx1_two(10 * P, 2 * P, 6, ring)
             mx2(6, ring)
-            t_run([12, 13])
             mx2(7, ring)
             r_piece(14, on_scalar)
             r_piece(15, on_scalar)
@@ -444,34 +474,33 @@ def tile_scenario_book_pnl_e3_kernel(tc, g_words, g_scales, delta, carry, stress
             v_quant(12)
             v_out(9)
             ja, jy, jz = S // P - 4, S // P - 2, S // P - 1
-            mx1_two(P * jy, P, 0, ring)
-            mx1_two(P * jy, P, 2, ring)
+            mx1_two(P * jy, P, 0, [6])
+            mx1_two(P * jy, P, 2, [7])
             mx2(10, [2])
             mx1_two(P * jy, P, 4, [3])
-            mx1_two(P * jy, P, 6, ring)
+            mx1_two(P * jy, P, 6, [0])
             v_mul(jy, 0, 1)
             v_out(10)
-            mx2(11, ring)
-            mx1_two(P * jz, P, 0, ring)
-            mx1_two(P * jz, P, 2, ring)
+            mx2(11, [1])
+            mx1_two(P * jz, P, 0, [6])
+            mx1_two(P * jz, P, 2, [7])
             v_mul(jy, 1, 1)
             v_out(11)
             v_quant(jy)
             v_mul(jz, 0, 1)
             mx2(ja, [3])
+            mx2(ja + 1, [0])
             mx1_two(P * jz, P, 4, [2])
-            mx1(P * jz, P, 6, ring)
-            turn[0] = turn[0] + 1
-            mx1(P * jz, P, 7, ring)
-            mx2(ja + 1, ring)
-            mx2(jy, [4])
+            mx1(P * jz, P, 6, [6])
+            mx1(P * jz, P, 7, [7])
+            mx2(jy, [1])
             v_out(ja)
             v_quant(jz, 0, 1)
+            v_out(ja + 1)
             v_mul(jz, 1, 1)
             v_quant(jz, 1, G)
-            v_out(ja + 1)
             v_out(jy)
-            last_banks = [banks[2], banks[3]]
+            last_banks = [banks[4], banks[3]]
             for g in range(G):
                 for h in range(2):
                     mx2_pass(jz, g, last_banks[h][:, 0 : B // 2], B // 2 * h, B // 2)
@@ -479,6 +508,6 @@ def tile_scenario_book_pnl_e3_kernel(tc, g_words, g_scales, delta, carry, stress
                 cols = slice(B // 2 * h, B // 2 * (h + 1))
                 res = work.tile([P, B // 2], F32, name="res", bufs=6)
                 nc.vector.tensor_tensor(
-                    out=res[:], in0=last_banks[h][:, 0 : B // 2], in1=hg[C - 1][:, J - 1, cols], op=ALU.add
+                    out=res[:], in0=last_banks[h][:, 0 : B // 2], in1=hg[PIECES - 1][:, 1, cols], op=ALU.add
                 )
                 nc.sync.dma_start(out=out[P * jz : P * (jz + 1), cols], in_=res[:])

@@ -25,6 +25,7 @@ J = SC // P
 PIECES = S // (2 * P)
 UNIT_BUFS = 4
 PNL_BUFS = 4
+BOTH = slice(0, G)
 
 
 def tile_scenario_book_pnl_e3_kernel(tc, g_words, g_scales, delta, carry, stress, hold, hedge, out):
@@ -201,17 +202,18 @@ def tile_scenario_book_pnl_e3_kernel(tc, g_words, g_scales, delta, carry, stress
                 acc = acc.rearrange("p (k m j) -> p k j m", j=2, m=P)
             nc.scalar.activation(out=dst, in_=acc, func=ACT.Identity, bias=ca[:, g, t : t + 1], scale=1.0)
 
-        def reorder(j, g, copy):
-            st_re[(j, g)] = work.tile([P, 2, 2, P], F32, name="st_re", bufs=8)
-            words = st[j // 2][:].bitcast(F32).rearrange("p j (g m u) -> p g j u m", g=G, u=2)
-            copy(out=st_re[(j, g)][:], in_=words[:, g])
+        def reorder(j, groups, copy):
+            if j not in st_re:
+                st_re[j] = work.tile([P, 2, G, 2, P], F32, name="st_re", bufs=4)
+            words = st[j // 2][:].bitcast(F32).rearrange("p j (g m u) -> p j g u m", g=G, u=2)
+            copy(out=st_re[j][:, :, groups], in_=words[:, :, groups])
 
         def t_pair(j, g, k):
             for half in range(2):
                 dst = banks[k][:, 256 * half : 256 * (half + 1)]
                 for u in range(2):
                     nc.tensor.transpose(
-                        dst.rearrange("p (c u i) -> p u c i", u=2, i=4)[:, u], st_re[(j, g)][:, half, u, :], ident[:]
+                        dst.rearrange("p (c u i) -> p u c i", u=2, i=4)[:, u], st_re[j][:, half, g, u, :], ident[:]
                     )
                 st_bank[(j + half, g)] = (k, half)
 
@@ -264,8 +266,7 @@ def tile_scenario_book_pnl_e3_kernel(tc, g_words, g_scales, delta, carry, stress
             nc.vector.tensor_tensor(out=res[:], in0=acc_out[j][:], in1=hg[j // 2][:, j % 2, :], op=ALU.add)
             nc.sync.dma_start(out=rows(out, j // 2)[:, j % 2], in_=res[:])
 
-        def i_hold(g, h, copy):
-            cols = slice(256 * h, 256 * (h + 1))
+        def i_hold(g, cols, copy):
             copy(
                 out=h_grp[g][:, cols, :].rearrange("p (c i) t -> p c t i", i=4),
                 in_=h_raw[g][:, :, cols].rearrange("p t (c i) -> p c t i", i=4),
@@ -356,14 +357,13 @@ def tile_scenario_book_pnl_e3_kernel(tc, g_words, g_scales, delta, carry, stress
             t_delta(7)
             s_unit(0, SC, 2, banks[2][:])
             s_unit(0, SC, 3, banks[3][:])
-            reorder(0, 0, on_vector)
+            reorder(0, BOTH, on_vector)
             q_delta(5, 0, A)
             c_first(6, on_vector)
             c_rest(6, on_scalar)
-            reorder(2, 0, on_vector)
+            reorder(2, slice(0, 1), on_vector)
             c_first(7, on_vector)
             c_rest(7, on_scalar)
-            reorder(0, 1, on_vector)
             mx1(0, SC, 4, [0])
             q_delta(6, 0, A)
             mx1(0, SC, 5, [1])
@@ -383,90 +383,78 @@ def tile_scenario_book_pnl_e3_kernel(tc, g_words, g_scales, delta, carry, stress
                 for m in order:
                     t_pair(pieces[m][0], pieces[m][1], stress_banks[m % 4])
 
-            def r_piece(m, copy):
-                reorder(pieces[m][0], pieces[m][1], copy)
-
             def step(j, g):
                 mx1_two(P * j, 2 * P, 4 * g, ring)
                 mx1_two(P * j, 2 * P, 4 * g + 2, ring)
 
-            r_piece(3, on_scalar)
+            reorder(2, slice(1, 2), on_scalar)
             mx1(0, SC, 6, ring)
-            r_piece(4, on_scalar)
             mx1(0, SC, 7, ring)
-            r_piece(5, on_vector)
+            reorder(4, BOTH, on_vector)
             v_mul(0, 1)
             mx1(SC, SC, 0, ring)
+            reorder(6, BOTH, on_scalar)
             mx1(SC, SC, 1, ring)
-            t_run([3, 4, 5])
-            v_mul(2, 1)
-            i_hold(1, 0, on_scalar)
             mx1(SC, SC, 2, ring)
-            mx1(SC, SC, 3, ring)
-            r_piece(6, on_scalar)
-            i_hold(0, 0, on_vector)
-            i_hold(0, 1, on_vector)
-            v_quant(0)
+            t_run([3, 4, 5])
+            i_hold(0, slice(0, B), on_vector)
+            v_mul(2, 1)
             v_hold_q(0)
+            mx1(SC, SC, 3, ring)
+            i_hold(1, slice(0, B // 2), on_scalar)
+            v_quant(0)
             v_mul(4, 0)
             mx1(SC, SC, 4, ring)
-            r_piece(7, on_scalar)
             mx1(SC, SC, 5, ring)
-            i_hold(1, 1, on_vector)
+            i_hold(1, slice(B // 2, B), on_scalar)
             v_quant(2)
-            v_hold_q(1)
             v_mul(6, 0)
+            v_hold_q(1)
             mx1(SC, SC, 6, ring)
             mx1(SC, SC, 7, ring)
             t_run([6, 7])
-            r_piece(8, on_scalar)
-            r_piece(9, on_scalar)
             step(8, 0)
-            r_piece(10, on_scalar)
+            reorder(8, BOTH, on_scalar)
             v_mul(4, 1)
             mx2(0, ring)
             mx2(1, ring)
-            v_mul(6, 1)
             v_out(0)
-            v_quant(4)
+            v_mul(6, 1)
             v_out(1)
-            mx1_two(8 * P, 2 * P, 4, ring)
-            t_run([8, 9, 10])
-            mx1_two(8 * P, 2 * P, 6, ring)
+            v_quant(4)
+            step(8, 1)
+            reorder(10, BOTH, on_scalar)
+            t_run([8, 9])
             mx2(2, ring)
             mx2(3, ring)
-            r_piece(11, on_scalar)
-            r_piece(12, on_scalar)
             v_mul(8, 0)
             v_out(2)
             v_quant(6)
             v_out(3)
             load_hg(6)
             load_hg(7)
+            reorder(12, BOTH, on_scalar)
             step(10, 0)
             mx2(4, ring)
+            t_run([10, 11, 12])
             mx2(5, ring)
-            r_piece(13, on_scalar)
             v_mul(8, 1)
             v_out(4)
             v_mul(10, 0)
             v_out(5)
-            mx1_two(10 * P, 2 * P, 4, ring)
-            t_run([11, 12, 13])
-            mx1_two(10 * P, 2 * P, 6, ring)
+            reorder(14, BOTH, on_scalar)
+            step(10, 1)
             mx2(6, ring)
             mx2(7, ring)
-            r_piece(14, on_scalar)
-            r_piece(15, on_scalar)
             v_quant(8)
             v_out(6)
             v_mul(10, 1)
             v_out(7)
             step(12, 0)
             step(12, 1)
+            t_run([13, 14, 15])
             mx2(8, ring)
             mx2(9, ring)
-            t_run([14, 15])
             v_quant(10)
             v_mul(12, 0)
             v_mul(12, 1)

@@ -41,9 +41,7 @@ def tile_scenario_book_pnl_e3_kernel(tc, g_words, g_scales, delta, carry, stress
 
 
         d_raw = [work.tile([P, F], BF16, name="d_words", bufs=4) for i in range(4)]
-        d_two = keep.tile([P, 2 * F], BF16, name="d_two")
-        d_raw = d_raw + [d_two[:, 0:F], d_two[:, F : 2 * F]]
-        d_raw = d_raw + [keep.tile([P, F], BF16, name="d_raw%d" % i) for i in range(6, 8)]
+        d_raw = d_raw + [keep.tile([P, F], BF16, name="d_raw%d" % i) for i in range(4, 8)]
         gw = [keep.tile([P, A, SC], U32, name="gw%d" % c, align_bytes=64) for c in range(C)]
         st = [keep.tile([P, 2, I], BF16, name="st%d" % k) for k in range(S // (2 * P))]
         hg = {}
@@ -61,7 +59,6 @@ def tile_scenario_book_pnl_e3_kernel(tc, g_words, g_scales, delta, carry, stress
         d_view = delta.rearrange("(g m t) k -> g t m k", g=G, t=4)
         gw_view = g_words.rearrange("g p n t -> p g (n t)")
         gs_view = g_scales.bitcast(I32).rearrange("a r n -> r a n")
-        d_two_view = delta.rearrange("(g m k t) f -> g k m (t f)", g=G, k=2, t=2)
 
         def rows(array, k):
             piece = array[2 * P * k : 2 * P * (k + 1), :]
@@ -84,9 +81,6 @@ def tile_scenario_book_pnl_e3_kernel(tc, g_words, g_scales, delta, carry, stress
 
         def load_d(i):
             nc.sync.dma_start(out=d_raw[i][:], in_=d_view[i // 4, i % 4])
-
-        def load_d_two():
-            nc.sync.dma_start(out=d_two[:], in_=d_two_view[1, 0])
 
         def load_g(c, lo=0, hi=A):
             nc.sync.dma_start(
@@ -208,8 +202,8 @@ def tile_scenario_book_pnl_e3_kernel(tc, g_words, g_scales, delta, carry, stress
             words = st[j // 2][:].bitcast(F32).rearrange("p j (g m u) -> p j g u m", g=G, u=2)
             copy(out=st_re[j][:, :, groups], in_=words[:, :, groups])
 
-        def t_pair(j, g, k):
-            for half in range(2):
+        def t_pair(j, g, k, halves=range(2)):
+            for half in halves:
                 dst = banks[k][:, 256 * half : 256 * (half + 1)]
                 for u in range(2):
                     nc.tensor.transpose(
@@ -277,6 +271,16 @@ def tile_scenario_book_pnl_e3_kernel(tc, g_words, g_scales, delta, carry, stress
                 out=h_codes[:, g].bitcast(E4), scales=h_sc[:, g], in_=h_grp[g][:].rearrange("p w j -> p (w j)")
             )
 
+        def turn_carry():
+            for u in range(2):
+                nc.tensor.transpose(banks[3][:, P * u : P * (u + 1)], ca_raw[:].bitcast(F32)[:, u:256:2], ident[:])
+            nc.scalar.activation(
+                out=ca[:].rearrange("p g (u e) -> p u g e", u=2),
+                in_=banks[3][:, 0 : 2 * P].bitcast(BF16).rearrange("p (u r e) -> p u r e", u=2, e=2)[:, :, 0:G, :],
+                func=ACT.Identity,
+                scale=1.0,
+            )
+
         on_vector = nc.vector.tensor_copy
         on_scalar = nc.scalar.copy
 
@@ -284,13 +288,16 @@ def tile_scenario_book_pnl_e3_kernel(tc, g_words, g_scales, delta, carry, stress
             nc.vector.memset(ca_raw[:], 0)
             for k in range(C):
                 nc.vector.memset(gs[k][:].rearrange("p a n -> p (a n)").bitcast(I32), 0)
-            for i in range(4):
-                load_d(i)
+            load_d(0)
+            load_d(1)
             nc.sync.dma_start(out=ca_raw[0:G, :], in_=carry.rearrange("(g w) -> g w", g=G))
+            load_d(2)
+            load_d(3)
             load_gs(0)
             load_g(0, 0, 1)
             load_g(0, 1, 2)
-            load_d_two()
+            load_d(4)
+            load_d(5)
             load_g(0, 2, 3)
             load_d(6)
             load_d(7)
@@ -302,9 +309,9 @@ def tile_scenario_book_pnl_e3_kernel(tc, g_words, g_scales, delta, carry, stress
             load_st(3)
             load_h(0)
             load_h(1)
+            load_st(4)
             load_gs(2)
             load_g(2)
-            load_st(4)
             load_st(5)
             load_hg(0)
             load_hg(1)
@@ -321,19 +328,11 @@ def tile_scenario_book_pnl_e3_kernel(tc, g_words, g_scales, delta, carry, stress
                 t_delta(i)
                 c_first(i, on_vector)
                 c_rest(i, on_scalar)
+                if i == 1:
+                    turn_carry()
                 if i > 0:
                     q_delta(i - 1, 1, A)
                 q_delta(i, 0, 1)
-            for u in range(2):
-                nc.tensor.transpose(
-                    banks[4][:, P * (2 + u) : P * (3 + u)], ca_raw[:].bitcast(F32)[:, u:256:2], ident[:]
-                )
-            nc.scalar.activation(
-                out=ca[:].rearrange("p g (u e) -> p u g e", u=2),
-                in_=banks[4][:, 2 * P : 4 * P].bitcast(BF16).rearrange("p (u r e) -> p u r e", u=2, e=2)[:, :, 0:G, :],
-                func=ACT.Identity,
-                scale=1.0,
-            )
             q_delta(3, 1, A)
             for a in range(A - 1):
                 for i in range(4):
@@ -357,8 +356,8 @@ def tile_scenario_book_pnl_e3_kernel(tc, g_words, g_scales, delta, carry, stress
             t_delta(7)
             s_unit(0, SC, 2, banks[2][:])
             s_unit(0, SC, 3, banks[3][:])
-            reorder(0, BOTH, on_vector)
             q_delta(5, 0, A)
+            reorder(0, BOTH, on_vector)
             c_first(6, on_vector)
             c_rest(6, on_scalar)
             reorder(2, slice(0, 1), on_vector)
@@ -397,24 +396,27 @@ def tile_scenario_book_pnl_e3_kernel(tc, g_words, g_scales, delta, carry, stress
             mx1(SC, SC, 1, ring)
             mx1(SC, SC, 2, ring)
             t_run([3, 4, 5])
+            t_pair(4, 1, stress_banks[2], [0])
             i_hold(0, slice(0, B), on_vector)
             v_mul(2, 1)
             v_hold_q(0)
-            mx1(SC, SC, 3, ring)
             i_hold(1, slice(0, B // 2), on_scalar)
+            mx1(SC, SC, 3, ring)
             v_quant(0)
             v_mul(4, 0)
             mx1(SC, SC, 4, ring)
-            mx1(SC, SC, 5, ring)
             i_hold(1, slice(B // 2, B), on_scalar)
-            v_quant(2)
+            mx1(SC, SC, 5, ring)
+            reorder(8, BOTH, on_vector)
             v_mul(6, 0)
+            v_quant(2)
             v_hold_q(1)
             mx1(SC, SC, 6, ring)
             mx1(SC, SC, 7, ring)
-            t_run([6, 7])
-            step(8, 0)
-            reorder(8, BOTH, on_scalar)
+            mx1_two(8 * P, 2 * P, 0, ring)
+            t_pair(4, 1, stress_banks[2], [1])
+            t_run([7, 8, 9])
+            mx1_two(8 * P, 2 * P, 2, ring)
             v_mul(4, 1)
             mx2(0, ring)
             mx2(1, ring)
@@ -424,7 +426,6 @@ def tile_scenario_book_pnl_e3_kernel(tc, g_words, g_scales, delta, carry, stress
             v_quant(4)
             step(8, 1)
             reorder(10, BOTH, on_scalar)
-            t_run([8, 9])
             mx2(2, ring)
             mx2(3, ring)
             v_mul(8, 0)

@@ -23,9 +23,11 @@ SC = 512
 C = S // SC
 J = SC // P
 PIECES = S // (2 * P)
-UNIT_BUFS = 4
+UNIT_BUFS = 3
 PNL_BUFS = 4
 BOTH = slice(0, G)
+ON_VECTOR = (10, 11, 12)
+PLAIN_ORDER = (5, 6, 7)
 
 
 def tile_scenario_book_pnl_e3_kernel(tc, g_words, g_scales, delta, carry, stress, hold, hedge, out):
@@ -43,7 +45,10 @@ def tile_scenario_book_pnl_e3_kernel(tc, g_words, g_scales, delta, carry, stress
         d_raw = [work.tile([P, F], BF16, name="d_words", bufs=4) for i in range(4)]
         d_raw = d_raw + [keep.tile([P, F], BF16, name="d_raw%d" % i) for i in range(4, 8)]
         gw = [keep.tile([P, A, SC], U32, name="gw%d" % c, align_bytes=64) for c in range(C)]
-        st = [keep.tile([P, 2, I], BF16, name="st%d" % k) for k in range(S // (2 * P))]
+        st = {k: keep.tile([P, 2, I], BF16, name="st%d" % k) for k in (0, 1, 2, 3, 4, 7)}
+        st[6] = keep.tile([P, 2, I // 2], BF16, name="st_half")
+        st_quad = {m: keep.tile([P, 8, P], BF16, name="st_quad%d" % m) for m in ON_VECTOR}
+        st_turned = {}
         hg = {}
         gs_cuts = [0, SC, 2 * SC, 3 * SC, S]
         gs = [keep.tile([P, A, gs_cuts[k + 1] - gs_cuts[k]], U8, name="gs%d" % k, align_bytes=64) for k in range(C)]
@@ -62,7 +67,7 @@ def tile_scenario_book_pnl_e3_kernel(tc, g_words, g_scales, delta, carry, stress
 
         def rows(array, k):
             piece = array[2 * P * k : 2 * P * (k + 1), :]
-            if k < PIECES - 1:
+            if k not in PLAIN_ORDER:
                 return piece.rearrange("(p j) w -> p j w", j=2)
             return piece.rearrange("(j p) w -> p j w", j=2)
 
@@ -78,6 +83,11 @@ def tile_scenario_book_pnl_e3_kernel(tc, g_words, g_scales, delta, carry, stress
         d_re = {}
         acc_out = {}
         turn = [0]
+        ring = [6, 7, 0, 1]
+        stress_banks = [2, 3, 4, 5]
+        pieces = [(0, 0), (2, 0), (0, 1), (2, 1), (4, 0), (6, 0), (4, 1), (6, 1)]
+        pieces = pieces + [(j, g) for j in range(8, 16, 2) for g in range(G)]
+        on_tensor = [pieces[m] for m in range(len(pieces)) if m not in ON_VECTOR]
 
         def load_d(i):
             nc.sync.dma_start(out=d_raw[i][:], in_=d_view[i // 4, i % 4])
@@ -89,6 +99,17 @@ def tile_scenario_book_pnl_e3_kernel(tc, g_words, g_scales, delta, carry, stress
 
         def load_st(k):
             nc.sync.dma_start(out=st[k][:], in_=rows(stress, k))
+
+        def load_st_half():
+            nc.sync.dma_start(out=st[6][:], in_=rows(stress, 6)[:, :, I // 2 : I])
+
+        def load_st_quad(m):
+            j, g = pieces[m]
+            blocks = stress[P * j : P * (j + 2), :].rearrange("(b r) i -> r b i", r=32)
+            for q in (0, 2, 1, 3):
+                nc.sync.dma_start(
+                    out=st_quad[m][32 * q : 32 * (q + 1)], in_=blocks[:, :, 512 * g + P * q : 512 * g + P * (q + 1)]
+                )
 
         def load_hg(k):
             hg[k] = work.tile([P, 2, B], BF16, name="hg", bufs=6)
@@ -191,7 +212,7 @@ def tile_scenario_book_pnl_e3_kernel(tc, g_words, g_scales, delta, carry, stress
                 for j in range(s0 // P, (s0 + n) // P):
                     units[(j, g)] = (tile, P * j - s0)
             dst = units[(s0 // P, g)][0][:, t, :]
-            if s0 < S - 2 * P:
+            if s0 // (2 * P) not in PLAIN_ORDER:
                 dst = dst.rearrange("p (k j m) -> p k j m", j=2, m=P)
                 acc = acc.rearrange("p (k m j) -> p k j m", j=2, m=P)
             nc.scalar.activation(out=dst, in_=acc, func=ACT.Identity, bias=ca[:, g, t : t + 1], scale=1.0)
@@ -202,13 +223,30 @@ def tile_scenario_book_pnl_e3_kernel(tc, g_words, g_scales, delta, carry, stress
             words = st[j // 2][:].bitcast(F32).rearrange("p j (g m u) -> p j g u m", g=G, u=2)
             copy(out=st_re[j][:, :, groups], in_=words[:, :, groups])
 
-        def t_pair(j, g, k, halves=range(2)):
-            for half in halves:
+        def reorder_half():
+            st_re[12] = work.tile([P, 2, G, 2, P], F32, name="st_re", bufs=4)
+            words = st[6][:].bitcast(F32).rearrange("p j (m u) -> p j u m", u=2)
+            nc.scalar.copy(out=st_re[12][:, :, 1], in_=words)
+
+        def reorder_quad(m):
+            st_re[("quad", m)] = work.tile([P, 2, 8, 32], F32, name="quad_re", bufs=2, align_bytes=64)
+            words = st_quad[m][:].bitcast(F32).rearrange("p b (w u) -> p u b w", u=2)
+            nc.scalar.copy(out=st_re[("quad", m)][:], in_=words)
+
+        def v_turn(m):
+            st_turned[pieces[m]] = work.tile([P, 512], F32, name="quad_turned", bufs=3, align_bytes=64)
+            nc.vector.transpose(
+                out=st_turned[pieces[m]][:], in_=st_re[("quad", m)][:].rearrange("p u b w -> p (u b w)")
+            )
+
+        def t_run(lo, hi):
+            for m in range(lo, hi):
+                j, g = on_tensor[m // 4]
+                k, half, u = stress_banks[m // 4 % 4], m // 2 % 2, m % 2
                 dst = banks[k][:, 256 * half : 256 * (half + 1)]
-                for u in range(2):
-                    nc.tensor.transpose(
-                        dst.rearrange("p (c u i) -> p u c i", u=2, i=4)[:, u], st_re[j][:, half, g, u, :], ident[:]
-                    )
+                nc.tensor.transpose(
+                    dst.rearrange("p (c u i) -> p u c i", u=2, i=4)[:, u], st_re[j][:, half, g, u, :], ident[:]
+                )
                 st_bank[(j + half, g)] = (k, half)
 
         def v_mul(j, g, blocks=2):
@@ -216,6 +254,14 @@ def tile_scenario_book_pnl_e3_kernel(tc, g_words, g_scales, delta, carry, stress
             if j not in pnl:
                 pnl[j] = work.tile([P, G, n, 4], BF16, name="pnl", align_bytes=64, bufs=PNL_BUFS)
             tile, c0 = units[(j, g)]
+            if (j, g) in st_turned:
+                nc.vector.tensor_tensor(
+                    out=pnl[j][:, g].rearrange("p s (u e) -> p s u e", u=2),
+                    in0=tile[:, :, c0 : c0 + n].rearrange("p (u e) s -> p s u e", u=2),
+                    in1=st_turned[(j, g)][:].bitcast(BF16).rearrange("p (u s e) -> p s u e", u=2, e=2),
+                    op=ALU.mult,
+                )
+                return
             k, half = st_bank[(j, g)]
             nc.vector.tensor_tensor(
                 out=pnl[j][:, g].rearrange("p (c i) (u e) -> p c u e i", i=4, u=2),
@@ -303,26 +349,27 @@ def tile_scenario_book_pnl_e3_kernel(tc, g_words, g_scales, delta, carry, stress
             load_d(7)
             load_st(0)
             load_st(1)
+            load_h(0)
             load_gs(1)
-            load_g(1)
+            load_g(1, 0, 1)
+            load_g(1, 1, A)
             load_st(2)
             load_st(3)
-            load_h(0)
             load_h(1)
             load_st(4)
             load_gs(2)
             load_g(2)
-            load_st(5)
+            load_st_quad(10)
+            load_st_half()
             load_hg(0)
+            load_st(7)
+            load_st_quad(11)
             load_hg(1)
-            load_st(6)
-            load_hg(2)
+            load_st_quad(12)
             load_gs(3)
             load_g(3)
+            load_hg(2)
             load_hg(3)
-            load_st(7)
-            load_hg(4)
-            load_hg(5)
 
             for i in range(4):
                 t_delta(i)
@@ -360,136 +407,134 @@ def tile_scenario_book_pnl_e3_kernel(tc, g_words, g_scales, delta, carry, stress
             reorder(0, BOTH, on_vector)
             c_first(6, on_vector)
             c_rest(6, on_scalar)
-            reorder(2, slice(0, 1), on_vector)
+            reorder(2, BOTH, on_vector)
             c_first(7, on_vector)
             c_rest(7, on_scalar)
             mx1(0, SC, 4, [0])
             q_delta(6, 0, A)
             mx1(0, SC, 5, [1])
-            t_pair(0, 0, 2)
-            t_pair(2, 0, 3)
-            t_pair(0, 1, 4)
+            t_run(0, 13)
             q_delta(7, 0, A)
             v_mul(0, 0)
             v_mul(2, 0)
-            ring = [6, 7, 0, 1]
             turn[0] = 0
-            stress_banks = [2, 3, 4, 5]
-            pieces = [(0, 0), (2, 0), (0, 1), (2, 1), (4, 0), (6, 0), (4, 1), (6, 1)]
-            pieces = pieces + [(j, g) for j in range(8, 16, 2) for g in range(G)]
-
-            def t_run(order):
-                for m in order:
-                    t_pair(pieces[m][0], pieces[m][1], stress_banks[m % 4])
 
             def step(j, g):
                 mx1_two(P * j, 2 * P, 4 * g, ring)
                 mx1_two(P * j, 2 * P, 4 * g + 2, ring)
 
-            reorder(2, slice(1, 2), on_scalar)
+            i_hold(0, slice(0, B // 2), on_scalar)
             mx1(0, SC, 6, ring)
             mx1(0, SC, 7, ring)
+            i_hold(0, slice(B // 2, B), on_vector)
             reorder(4, BOTH, on_vector)
             v_mul(0, 1)
+            v_hold_q(0)
             mx1(SC, SC, 0, ring)
-            reorder(6, BOTH, on_scalar)
+            reorder(6, slice(0, 1), on_scalar)
             mx1(SC, SC, 1, ring)
             mx1(SC, SC, 2, ring)
-            t_run([3, 4, 5])
-            t_pair(4, 1, stress_banks[2], [0])
-            i_hold(0, slice(0, B), on_vector)
+            reorder(6, slice(1, 2), on_scalar)
+            t_run(13, 26)
             v_mul(2, 1)
-            v_hold_q(0)
             i_hold(1, slice(0, B // 2), on_scalar)
-            mx1(SC, SC, 3, ring)
+            i_hold(1, slice(B // 2, B), on_vector)
             v_quant(0)
+            v_hold_q(1)
+            mx1(SC, SC, 3, ring)
             v_mul(4, 0)
             mx1(SC, SC, 4, ring)
-            i_hold(1, slice(B // 2, B), on_scalar)
+            reorder(8, BOTH, on_scalar)
             mx1(SC, SC, 5, ring)
-            reorder(8, BOTH, on_vector)
             v_mul(6, 0)
             v_quant(2)
-            v_hold_q(1)
             mx1(SC, SC, 6, ring)
             mx1(SC, SC, 7, ring)
             mx1_two(8 * P, 2 * P, 0, ring)
-            t_pair(4, 1, stress_banks[2], [1])
-            t_run([7, 8, 9])
+            t_run(26, 39)
+            reorder_quad(10)
+            reorder_half()
             mx1_two(8 * P, 2 * P, 2, ring)
+            reorder(14, BOTH, on_scalar)
             v_mul(4, 1)
             mx2(0, ring)
             mx2(1, ring)
-            v_out(0)
             v_mul(6, 1)
+            v_turn(10)
+            v_out(0)
             v_out(1)
             v_quant(4)
             step(8, 1)
-            reorder(10, BOTH, on_scalar)
+            reorder_quad(11)
+            reorder_quad(12)
             mx2(2, ring)
             mx2(3, ring)
             v_mul(8, 0)
             v_out(2)
             v_quant(6)
             v_out(3)
-            load_hg(6)
-            load_hg(7)
-            reorder(12, BOTH, on_scalar)
-            step(10, 0)
+            load_hg(4)
+            load_hg(5)
+            mx1_two(10 * P, 2 * P, 0, ring)
+            t_run(39, 52)
+            mx1_two(10 * P, 2 * P, 2, ring)
             mx2(4, ring)
-            t_run([10, 11, 12])
             mx2(5, ring)
             v_mul(8, 1)
+            v_turn(11)
+            v_turn(12)
+            v_quant(8)
             v_out(4)
             v_mul(10, 0)
             v_out(5)
-            reorder(14, BOTH, on_scalar)
+            load_hg(6)
+            load_hg(7)
             step(10, 1)
-            mx2(6, ring)
-            mx2(7, ring)
-            v_quant(8)
+            mx2(6, [3])
+            mx2(7, [6])
             v_out(6)
             v_mul(10, 1)
             v_out(7)
-            step(12, 0)
-            step(12, 1)
-            t_run([13, 14, 15])
-            mx2(8, ring)
-            mx2(9, ring)
+            mx1_two(12 * P, 2 * P, 0, [0])
+            mx1_two(12 * P, 2 * P, 2, [1])
+            mx1_two(12 * P, 2 * P, 4, [7])
+            mx1_two(12 * P, 2 * P, 6, [3])
             v_quant(10)
             v_mul(12, 0)
+            mx2(8, [0])
+            mx2(9, [6])
             v_mul(12, 1)
             v_out(8)
             v_quant(12)
             v_out(9)
             ja, jy, jz = S // P - 4, S // P - 2, S // P - 1
-            mx1_two(P * jy, P, 0, [6])
+            mx1_two(P * jy, P, 0, [1])
             mx1_two(P * jy, P, 2, [7])
-            mx2(10, [2])
-            mx1_two(P * jy, P, 4, [3])
-            mx1_two(P * jy, P, 6, [0])
+            mx2(10, [3])
+            mx1_two(P * jy, P, 4, [1])
+            mx1_two(P * jy, P, 6, [7])
             v_mul(jy, 0, 1)
             v_out(10)
-            mx2(11, [1])
-            mx1_two(P * jz, P, 0, [6])
+            mx2(11, [4])
+            mx1_two(P * jz, P, 0, [1])
             mx1_two(P * jz, P, 2, [7])
             v_mul(jy, 1, 1)
             v_out(11)
             v_quant(jy)
             v_mul(jz, 0, 1)
-            mx2(ja, [3])
-            mx2(ja + 1, [0])
-            mx1_two(P * jz, P, 4, [2])
-            mx1(P * jz, P, 6, [6])
-            mx1(P * jz, P, 7, [7])
-            mx2(jy, [1])
+            mx2(ja, [0])
+            mx2(ja + 1, [6])
+            mx1_two(P * jz, P, 4, [1])
+            mx1(P * jz, P, 6, [7])
+            mx1(P * jz, P, 7, [3])
+            mx2(jy, [4])
             v_out(ja)
             v_quant(jz, 0, 1)
-            v_out(ja + 1)
             v_mul(jz, 1, 1)
+            v_out(ja + 1)
             v_quant(jz, 1, G)
             v_out(jy)
-            last_banks = [banks[4], banks[3]]
+            last_banks = [banks[5], banks[0]]
             for g in range(G):
                 for h in range(2):
                     mx2_pass(jz, g, last_banks[h][:, 0 : B // 2], B // 2 * h, B // 2)

@@ -21,13 +21,12 @@ A = F // 512
 G = I // 512
 SC = 512
 C = S // SC
-J = SC // P
-PIECES = S // (2 * P)
-UNIT_BUFS = 3
-PNL_BUFS = 4
-BOTH = slice(0, G)
-ON_VECTOR = (10, 11, 12)
-PLAIN_ORDER = (5, 6, 7)
+PC = 2 * P
+PIECES = S // PC
+LAST = PIECES - 1
+TURNED = 6
+PLAIN = (TURNED, LAST)
+EARLY = 4
 
 
 def tile_scenario_book_pnl_e3_kernel(tc, g_words, g_scales, delta, carry, stress, hold, hedge, out):
@@ -41,17 +40,12 @@ def tile_scenario_book_pnl_e3_kernel(tc, g_words, g_scales, delta, carry, stress
         make_identity(nc, ident[:])
         banks = [psum.tile([P, 512], F32, name="bank%d" % k) for k in range(8)]
 
-
-        d_raw = [work.tile([P, F], BF16, name="d_words", bufs=4) for i in range(4)]
-        d_raw = d_raw + [keep.tile([P, F], BF16, name="d_raw%d" % i) for i in range(4, 8)]
+        d_raw = [work.tile([P, F], BF16, name="d_words", bufs=EARLY) for i in range(EARLY)]
+        d_raw = d_raw + [keep.tile([P, F], BF16, name="d_raw%d" % i) for i in range(EARLY, 8)]
         gw = [keep.tile([P, A, SC], U32, name="gw%d" % c, align_bytes=64) for c in range(C)]
-        st = {k: keep.tile([P, 2, I], BF16, name="st%d" % k) for k in (0, 1, 2, 3, 4, 7)}
-        st[6] = keep.tile([P, 2, I // 2], BF16, name="st_half")
-        st_quad = {m: keep.tile([P, 8, P], BF16, name="st_quad%d" % m) for m in ON_VECTOR}
-        st_turned = {}
-        hg = {}
-        gs_cuts = [0, SC, 2 * SC, 3 * SC, S]
-        gs = [keep.tile([P, A, gs_cuts[k + 1] - gs_cuts[k]], U8, name="gs%d" % k, align_bytes=64) for k in range(C)]
+        gs = [keep.tile([P, A, SC], U8, name="gs%d" % c, align_bytes=64) for c in range(C)]
+        st = {k: keep.tile([P, 2, I], BF16, name="st%d" % k) for k in range(PIECES) if k != TURNED}
+        st_quad = [keep.tile([P, 8, P], BF16, name="st_quad%d" % g) for g in range(G)]
         h_raw = [keep.tile([P, 4, B], BF16, name="h_raw%d" % g) for g in range(G)]
         h_grp = [keep.tile([P, B, 4], BF16, name="h_grp%d" % g, align_bytes=64) for g in range(G)]
         h_codes = keep.tile([P, G, B], U32, name="h_codes", align_bytes=64)
@@ -64,30 +58,27 @@ def tile_scenario_book_pnl_e3_kernel(tc, g_words, g_scales, delta, carry, stress
         d_view = delta.rearrange("(g m t) k -> g t m k", g=G, t=4)
         gw_view = g_words.rearrange("g p n t -> p g (n t)")
         gs_view = g_scales.bitcast(I32).rearrange("a r n -> r a n")
-
-        def rows(array, k):
-            piece = array[2 * P * k : 2 * P * (k + 1), :]
-            if k not in PLAIN_ORDER:
-                return piece.rearrange("(p j) w -> p j w", j=2)
-            return piece.rearrange("(j p) w -> p j w", j=2)
-
         h_view = hold.rearrange("(g p j) w -> g p j w", g=G, j=4)
 
+        def rows(array, k):
+            piece = array[PC * k : PC * (k + 1), :]
+            if k in PLAIN:
+                return piece.rearrange("(j p) w -> p j w", j=2)
+            return piece.rearrange("(p j) w -> p j w", j=2)
+
+        hg = {}
         units = {}
         st_re = {}
-        st_bank = {}
+        st_words = {}
+        st_turned = {}
         pnl = {}
         pnl_codes = {}
         pnl_sc = {}
         d_grp = {}
         d_re = {}
-        acc_out = {}
-        turn = [0]
-        ring = [6, 7, 0, 1]
-        stress_banks = [2, 3, 4, 5]
-        pieces = [(0, 0), (2, 0), (0, 1), (2, 1), (4, 0), (6, 0), (4, 1), (6, 1)]
-        pieces = pieces + [(j, g) for j in range(8, 16, 2) for g in range(G)]
-        on_tensor = [pieces[m] for m in range(len(pieces)) if m not in ON_VECTOR]
+        d_banks = {}
+        book = {}
+        res = {}
 
         def load_d(i):
             nc.sync.dma_start(out=d_raw[i][:], in_=d_view[i // 4, i % 4])
@@ -97,18 +88,20 @@ def tile_scenario_book_pnl_e3_kernel(tc, g_words, g_scales, delta, carry, stress
                 out=gw[c][:, lo:hi].bitcast(I32), in_=gw_view[:, lo:hi, 4 * SC * c : 4 * SC * (c + 1)].bitcast(I32)
             )
 
+        def load_gs(c):
+            for r in range(4):
+                nc.sync.dma_start(
+                    out=gs[c][r:P:32].bitcast(I32), in_=gs_view[r:16:4, :, SC * c // 4 : SC * (c + 1) // 4]
+                )
+
         def load_st(k):
             nc.sync.dma_start(out=st[k][:], in_=rows(stress, k))
 
-        def load_st_half():
-            nc.sync.dma_start(out=st[6][:], in_=rows(stress, 6)[:, :, I // 2 : I])
-
-        def load_st_quad(m):
-            j, g = pieces[m]
-            blocks = stress[P * j : P * (j + 2), :].rearrange("(b r) i -> r b i", r=32)
+        def load_st_quads(g):
+            blocks = stress[PC * TURNED : PC * (TURNED + 1), :].rearrange("(b r) i -> r b i", r=32)
             for q in (0, 2, 1, 3):
                 nc.sync.dma_start(
-                    out=st_quad[m][32 * q : 32 * (q + 1)], in_=blocks[:, :, 512 * g + P * q : 512 * g + P * (q + 1)]
+                    out=st_quad[g][32 * q : 32 * (q + 1)], in_=blocks[:, :, 512 * g + P * q : 512 * g + P * (q + 1)]
                 )
 
         def load_hg(k):
@@ -118,26 +111,11 @@ def tile_scenario_book_pnl_e3_kernel(tc, g_words, g_scales, delta, carry, stress
         def load_h(g):
             nc.sync.dma_start(out=h_raw[g][:], in_=h_view[g])
 
-        def load_gs(k):
-            for r in range(4):
-                nc.sync.dma_start(
-                    out=gs[k][r:P:32].bitcast(I32),
-                    in_=gs_view[r:16:4, :, gs_cuts[k] // 4 : gs_cuts[k + 1] // 4],
-                )
-
-        def next_bank(ring):
-            k = ring[turn[0] % len(ring)]
-            turn[0] = turn[0] + 1
-            return banks[k]
-
-        def d_banks(i):
-            one = banks[4 + 2 * (i % 2)][:, 0:256].rearrange("p (u m) -> p u m", u=2)
-            two = banks[5 + 2 * (i % 2)][:].rearrange("p (a u m) -> p a u m", a=2, u=2)
-            return one, two
-
-        def t_delta(i):
-            one, two = d_banks(i)
-            for a in range(A):
+        def t_delta(i, passes, first, rest, half=0):
+            one = banks[first][:, 256 * half : 256 * (half + 1)].rearrange("p (u m) -> p u m", u=2)
+            two = banks[rest][:].rearrange("p (a u m) -> p a u m", a=2, u=2)
+            d_banks[i] = (one, two)
+            for a in passes:
                 for u in range(2):
                     dst = one[:, u, :] if a == 0 else two[:, a - 1, u, :]
                     if i in d_re:
@@ -146,61 +124,51 @@ def tile_scenario_book_pnl_e3_kernel(tc, g_words, g_scales, delta, carry, stress
                         words = d_raw[i][:].bitcast(F32)[:, 256 * a + u : 256 * (a + 1) : 2]
                     nc.tensor.transpose(dst, words, ident[:])
 
+        def t_pair(i, first, rest):
+            for m in range(2):
+                t_delta(i + m, [0], first, rest[m], m)
+            for m in range(2):
+                t_delta(i + m, [1, 2], first, rest[m], m)
+
         def r_delta(i):
-            d_re[i] = work.tile([P, A, 2, P], F32, name="d_words", bufs=4)
+            d_re[i] = work.tile([P, A, 2, P], F32, name="d_words", bufs=EARLY)
             nc.vector.tensor_copy(
                 out=d_re[i][:].rearrange("p a u (v m) -> p v a u m", v=2),
                 in_=d_raw[i][:].bitcast(F32).rearrange("p (a v m u) -> p v a u m", a=A, v=2, u=2),
             )
 
         def c_first(i, copy):
-            one, two = d_banks(i)
             d_grp[i] = work.tile([P, A, P, 4], BF16, name="d_grp", align_bytes=64)
             copy(
                 out=d_grp[i][:, 0].rearrange("p m t -> p (m t)").bitcast(F32).rearrange("p (m u) -> p m u", u=2),
-                in_=one.rearrange("p u m -> p m u"),
+                in_=d_banks[i][0].rearrange("p u m -> p m u"),
             )
 
         def c_rest(i, copy):
-            one, two = d_banks(i)
             copy(
                 out=d_grp[i][:, 1:3]
                 .rearrange("p a m t -> p a (m t)")
                 .bitcast(F32)
                 .rearrange("p a (m u) -> p a m u", u=2),
-                in_=two.rearrange("p a u m -> p a m u"),
+                in_=d_banks[i][1].rearrange("p a u m -> p a m u"),
             )
 
-        def q_delta(i, lo, hi):
+        def q_delta(i, lo=0, hi=A):
             nc.vector.quantize_mx(
                 out=d_codes[i][:, lo:hi].rearrange("p a m -> p (a m)").bitcast(E4),
                 scales=d_sc[i][:, lo:hi].rearrange("p a m -> p (a m)"),
                 in_=d_grp[i][:, lo:hi].rearrange("p a m t -> p (a m t)"),
             )
 
-        def mx1(s0, n, i, ring):
-            acc = next_bank(ring)[:, 0:n]
-            mx1_passes(s0, n, i, acc)
-            s_unit(s0, n, i, acc)
-
-        def mx1_two(s0, n, i, ring):
-            bank = next_bank(ring)
-            for m in range(2):
-                mx1_passes(s0, n, i + m, bank[:, n * m : n * (m + 1)])
-            for m in range(2):
-                s_unit(s0, n, i + m, bank[:, n * m : n * (m + 1)])
-
-        def mx1_passes(s0, n, i, acc, passes=range(A)):
-            c = s0 // SC
-            ks = c
-            w0, c0 = s0 - SC * c, s0 - gs_cuts[ks]
-            for a in passes:
+        def mx1_passes(s0, n, i, acc):
+            c, w0 = s0 // SC, s0 % SC
+            for a in range(A):
                 nc.tensor.matmul_mx(
                     out=acc,
                     lhsT=d_codes[i][:, a, :].bitcast(E4),
                     lhsT_scale=d_sc[i][:, a, :],
                     rhs=gw[c][:, a, w0 : w0 + n].bitcast(E5),
-                    rhs_scale=gs[ks][:, a, c0 : c0 + n],
+                    rhs_scale=gs[c][:, a, w0 : w0 + n],
                     start=(a == 0),
                     stop=(a == A - 1),
                 )
@@ -208,103 +176,99 @@ def tile_scenario_book_pnl_e3_kernel(tc, g_words, g_scales, delta, carry, stress
         def s_unit(s0, n, i, acc):
             g, t = i // 4, i % 4
             if t == 0:
-                tile = work.tile([P, 4, n], F32, name="unit", bufs=UNIT_BUFS)
+                tile = work.tile([P, 4, n], F32, name="unit", bufs=3)
                 for j in range(s0 // P, (s0 + n) // P):
                     units[(j, g)] = (tile, P * j - s0)
-            dst = units[(s0 // P, g)][0][:, t, :]
-            if s0 // (2 * P) not in PLAIN_ORDER:
+            tile, c0 = units[(s0 // P, g)]
+            dst = tile[:, t, c0 : c0 + n]
+            if s0 // PC not in PLAIN:
                 dst = dst.rearrange("p (k j m) -> p k j m", j=2, m=P)
                 acc = acc.rearrange("p (k m j) -> p k j m", j=2, m=P)
             nc.scalar.activation(out=dst, in_=acc, func=ACT.Identity, bias=ca[:, g, t : t + 1], scale=1.0)
 
-        def reorder(j, groups, copy):
-            if j not in st_re:
-                st_re[j] = work.tile([P, 2, G, 2, P], F32, name="st_re", bufs=4)
-            words = st[j // 2][:].bitcast(F32).rearrange("p j (g m u) -> p j g u m", g=G, u=2)
-            copy(out=st_re[j][:, :, groups], in_=words[:, :, groups])
+        def mx1(s0, n, i, bank, tiles=1):
+            for m in range(tiles):
+                mx1_passes(s0, n, i + m, banks[bank][:, n * m : n * (m + 1)])
+            for m in range(tiles):
+                s_unit(s0, n, i + m, banks[bank][:, n * m : n * (m + 1)])
 
-        def reorder_half():
-            st_re[12] = work.tile([P, 2, G, 2, P], F32, name="st_re", bufs=4)
-            words = st[6][:].bitcast(F32).rearrange("p j (m u) -> p j u m", u=2)
-            nc.scalar.copy(out=st_re[12][:, :, 1], in_=words)
+        def reorder(k, g, copy):
+            st_re[(k, g)] = work.tile([P, 2, 2, P], F32, name="st_re", bufs=8)
+            words = st[k][:].bitcast(F32).rearrange("p j (g m u) -> p j g u m", g=G, u=2)
+            copy(out=st_re[(k, g)][:], in_=words[:, :, g])
 
-        def reorder_quad(m):
-            st_re[("quad", m)] = work.tile([P, 2, 8, 32], F32, name="quad_re", bufs=2, align_bytes=64)
-            words = st_quad[m][:].bitcast(F32).rearrange("p b (w u) -> p u b w", u=2)
-            nc.scalar.copy(out=st_re[("quad", m)][:], in_=words)
+        def t_stress(k, g, bank, halves=(0, 1)):
+            st_words[(k, g)] = banks[bank]
+            for half in halves:
+                dst = banks[bank][:, 256 * half : 256 * (half + 1)].rearrange("p (c u i) -> p u c i", u=2, i=4)
+                for u in range(2):
+                    nc.tensor.transpose(dst[:, u], st_re[(k, g)][:, half, u, :], ident[:])
 
-        def v_turn(m):
-            st_turned[pieces[m]] = work.tile([P, 512], F32, name="quad_turned", bufs=3, align_bytes=64)
-            nc.vector.transpose(
-                out=st_turned[pieces[m]][:], in_=st_re[("quad", m)][:].rearrange("p u b w -> p (u b w)")
+        def reorder_quads(g):
+            st_re[(TURNED, g)] = work.tile([P, 2, 8, 32], F32, name="quad_re", bufs=2, align_bytes=64)
+            words = st_quad[g][:].bitcast(F32).rearrange("p b (w u) -> p u b w", u=2)
+            nc.scalar.copy(out=st_re[(TURNED, g)][:], in_=words)
+
+        def v_turn(g):
+            st_turned[g] = work.tile([P, 512], F32, name="quad_turned", bufs=2, align_bytes=64)
+            nc.vector.transpose(out=st_turned[g][:], in_=st_re[(TURNED, g)][:].rearrange("p u b w -> p (u b w)"))
+
+        def s_lay(g):
+            st_words[(TURNED, g)] = work.tile([P, 512], F32, name="quad_re", bufs=2, align_bytes=64)
+            nc.scalar.copy(
+                out=st_words[(TURNED, g)][:].rearrange("p (c u i) -> p c u i", u=2, i=4),
+                in_=st_turned[g][:].rearrange("p (u c i) -> p c u i", u=2, i=4),
             )
 
-        def t_run(lo, hi):
-            for m in range(lo, hi):
-                j, g = on_tensor[m // 4]
-                k, half, u = stress_banks[m // 4 % 4], m // 2 % 2, m % 2
-                dst = banks[k][:, 256 * half : 256 * (half + 1)]
-                nc.tensor.transpose(
-                    dst.rearrange("p (c u i) -> p u c i", u=2, i=4)[:, u], st_re[j][:, half, g, u, :], ident[:]
-                )
-                st_bank[(j + half, g)] = (k, half)
-
-        def v_mul(j, g, blocks=2):
-            n = P * blocks
-            if j not in pnl:
-                pnl[j] = work.tile([P, G, n, 4], BF16, name="pnl", align_bytes=64, bufs=PNL_BUFS)
-            tile, c0 = units[(j, g)]
-            if (j, g) in st_turned:
-                nc.vector.tensor_tensor(
-                    out=pnl[j][:, g].rearrange("p s (u e) -> p s u e", u=2),
-                    in0=tile[:, :, c0 : c0 + n].rearrange("p (u e) s -> p s u e", u=2),
-                    in1=st_turned[(j, g)][:].bitcast(BF16).rearrange("p (u s e) -> p s u e", u=2, e=2),
-                    op=ALU.mult,
-                )
-                return
-            k, half = st_bank[(j, g)]
+        def v_mul(k, g, lo=0, hi=2):
+            if k not in pnl:
+                pnl[k] = work.tile([P, G, PC, 4], BF16, name="pnl", align_bytes=64, bufs=4)
+            tile, c0 = units[(2 * k + lo, g)]
+            n = P * (hi - lo)
             nc.vector.tensor_tensor(
-                out=pnl[j][:, g].rearrange("p (c i) (u e) -> p c u e i", i=4, u=2),
+                out=pnl[k][:, g, P * lo : P * hi].rearrange("p (c i) (u e) -> p c u e i", i=4, u=2),
                 in0=tile[:, :, c0 : c0 + n].rearrange("p (u e) (c i) -> p c u e i", i=4, u=2),
-                in1=banks[k][:, 256 * half : 256 * (half + blocks)]
+                in1=st_words[(k, g)][:, 256 * lo : 256 * hi]
                 .bitcast(BF16)
                 .rearrange("p (c u i e) -> p c u e i", u=2, i=4, e=2),
                 op=ALU.mult,
             )
 
-        def v_quant(j, lo=0, hi=G):
-            n = pnl[j].shape[2]
-            if j not in pnl_codes:
-                pnl_codes[j] = work.tile([P, G, n], U32, name="pnl_codes", align_bytes=64, bufs=4)
-                pnl_sc[j] = work.tile([P, G, n], U8, name="pnl_sc", align_bytes=64, bufs=4)
+        def v_quant(k, g=None, lo=0, hi=2):
+            if k not in pnl_codes:
+                pnl_codes[k] = work.tile([P, G * PC], U32, name="pnl_codes", align_bytes=64, bufs=4)
+                pnl_sc[k] = work.tile([P, G * PC], U8, name="pnl_sc", align_bytes=64, bufs=4)
+            cols = slice(0, G * PC) if g is None else slice(PC * g + P * lo, PC * g + P * hi)
             nc.vector.quantize_mx(
-                out=pnl_codes[j][:, lo:hi].rearrange("p g s -> p (g s)").bitcast(E5),
-                scales=pnl_sc[j][:, lo:hi].rearrange("p g s -> p (g s)"),
-                in_=pnl[j][:, lo:hi].rearrange("p g s t -> p (g s t)"),
+                out=pnl_codes[k][:, cols].bitcast(E5),
+                scales=pnl_sc[k][:, cols],
+                in_=pnl[k][:].rearrange("p g s t -> p (g s) t")[:, cols].rearrange("p s t -> p (s t)"),
             )
 
         def mx2_pass(j, g, acc, b0=0, n=B):
-            j0 = j if j in pnl_codes else j - 1
-            cols = slice(P * (j - j0), P * (j - j0 + 1))
+            cols = slice(PC * g + P * (j % 2), PC * g + P * (j % 2 + 1))
             nc.tensor.matmul_mx(
                 out=acc,
-                lhsT=pnl_codes[j0][:, g, cols].bitcast(E5),
-                lhsT_scale=pnl_sc[j0][:, g, cols],
+                lhsT=pnl_codes[j // 2][:, cols].bitcast(E5),
+                lhsT_scale=pnl_sc[j // 2][:, cols],
                 rhs=h_codes[:, g, b0 : b0 + n].bitcast(E4),
                 rhs_scale=h_sc[:, g, b0 : b0 + n],
                 start=(g == 0),
                 stop=(g == G - 1),
             )
 
-        def mx2(j, ring):
-            acc_out[j] = next_bank(ring)
+        def mx2(j, bank):
+            book[j] = banks[bank]
             for g in range(G):
-                mx2_pass(j, g, acc_out[j][:])
+                mx2_pass(j, g, book[j][:])
+
+        def store(j):
+            nc.sync.dma_start(out=rows(out, j // 2)[:, j % 2], in_=res[j][:])
 
         def v_out(j):
-            res = work.tile([P, B], F32, name="res", bufs=6)
-            nc.vector.tensor_tensor(out=res[:], in0=acc_out[j][:], in1=hg[j // 2][:, j % 2, :], op=ALU.add)
-            nc.sync.dma_start(out=rows(out, j // 2)[:, j % 2], in_=res[:])
+            res[j] = work.tile([P, B], F32, name="res", bufs=6)
+            nc.vector.tensor_tensor(out=res[j][:], in0=book[j][:], in1=hg[j // 2][:, j % 2, :], op=ALU.add)
+            store(j)
 
         def i_hold(g, cols, copy):
             copy(
@@ -312,39 +276,39 @@ def tile_scenario_book_pnl_e3_kernel(tc, g_words, g_scales, delta, carry, stress
                 in_=h_raw[g][:, :, cols].rearrange("p t (c i) -> p c t i", i=4),
             )
 
-        def v_hold_q(g):
+        def q_hold(g):
             nc.vector.quantize_mx(
                 out=h_codes[:, g].bitcast(E4), scales=h_sc[:, g], in_=h_grp[g][:].rearrange("p w j -> p (w j)")
             )
 
-        def turn_carry():
+        def turn_carry(bank):
             for u in range(2):
-                nc.tensor.transpose(banks[3][:, P * u : P * (u + 1)], ca_raw[:].bitcast(F32)[:, u:256:2], ident[:])
+                nc.tensor.transpose(banks[bank][:, P * u : P * (u + 1)], ca_raw[:].bitcast(F32)[:, u:256:2], ident[:])
             nc.scalar.activation(
                 out=ca[:].rearrange("p g (u e) -> p u g e", u=2),
-                in_=banks[3][:, 0 : 2 * P].bitcast(BF16).rearrange("p (u r e) -> p u r e", u=2, e=2)[:, :, 0:G, :],
+                in_=banks[bank][:, 0 : 2 * P].bitcast(BF16).rearrange("p (u r e) -> p u r e", u=2, e=2)[:, :, 0:G, :],
                 func=ACT.Identity,
                 scale=1.0,
             )
 
         on_vector = nc.vector.tensor_copy
         on_scalar = nc.scalar.copy
+        left, right = slice(0, B // 2), slice(B // 2, B)
 
         with tc.manual_schedule():
             nc.vector.memset(ca_raw[:], 0)
-            for k in range(C):
-                nc.vector.memset(gs[k][:].rearrange("p a n -> p (a n)").bitcast(I32), 0)
+            for c in range(C):
+                nc.vector.memset(gs[c][:].rearrange("p a n -> p (a n)").bitcast(I32), 0)
             load_d(0)
             load_d(1)
             nc.sync.dma_start(out=ca_raw[0:G, :], in_=carry.rearrange("(g w) -> g w", g=G))
             load_d(2)
             load_d(3)
             load_gs(0)
-            load_g(0, 0, 1)
-            load_g(0, 1, 2)
+            for a in range(A):
+                load_g(0, a, a + 1)
             load_d(4)
             load_d(5)
-            load_g(0, 2, 3)
             load_d(6)
             load_d(7)
             load_st(0)
@@ -359,189 +323,188 @@ def tile_scenario_book_pnl_e3_kernel(tc, g_words, g_scales, delta, carry, stress
             load_st(4)
             load_gs(2)
             load_g(2)
-            load_st_quad(10)
-            load_st_half()
+            load_st(5)
             load_hg(0)
             load_st(7)
-            load_st_quad(11)
             load_hg(1)
-            load_st_quad(12)
+            load_st_quads(0)
             load_gs(3)
             load_g(3)
+            load_st_quads(1)
             load_hg(2)
             load_hg(3)
 
-            for i in range(4):
-                t_delta(i)
+            for i in range(EARLY):
+                t_delta(i, range(A), 4 + 2 * (i % 2), 5 + 2 * (i % 2))
                 c_first(i, on_vector)
                 c_rest(i, on_scalar)
                 if i == 1:
-                    turn_carry()
+                    turn_carry(3)
                 if i > 0:
                     q_delta(i - 1, 1, A)
                 q_delta(i, 0, 1)
             q_delta(3, 1, A)
-            for a in range(A - 1):
-                for i in range(4):
-                    mx1_passes(0, SC, i, banks[i][:], [a])
             r_delta(4)
             r_delta(5)
-            t_delta(4)
-            t_delta(5)
-            for i in range(4):
-                mx1_passes(0, SC, i, banks[i][:], [A - 1])
-            c_first(4, on_vector)
-            c_rest(4, on_scalar)
-            c_first(5, on_vector)
-            c_rest(5, on_scalar)
+            mx1(0, SC, 0, 0)
+            mx1(0, SC, 1, 1)
+            mx1(0, SC, 2, 2)
+            t_pair(4, 3, [4, 5])
             r_delta(6)
+            c_first(4, on_vector)
+            c_first(5, on_vector)
+            c_rest(4, on_scalar)
+            c_rest(5, on_scalar)
             r_delta(7)
-            q_delta(4, 0, A)
-            s_unit(0, SC, 0, banks[0][:])
-            s_unit(0, SC, 1, banks[1][:])
-            t_delta(6)
-            t_delta(7)
-            s_unit(0, SC, 2, banks[2][:])
-            s_unit(0, SC, 3, banks[3][:])
-            q_delta(5, 0, A)
-            reorder(0, BOTH, on_vector)
+            q_delta(4)
+            mx1(0, SC, 3, 6)
+            t_pair(6, 7, [0, 1])
+            q_delta(5)
+            reorder(0, 0, on_vector)
             c_first(6, on_vector)
-            c_rest(6, on_scalar)
-            reorder(2, BOTH, on_vector)
             c_first(7, on_vector)
+            c_rest(6, on_scalar)
             c_rest(7, on_scalar)
-            mx1(0, SC, 4, [0])
-            q_delta(6, 0, A)
-            mx1(0, SC, 5, [1])
-            t_run(0, 13)
-            q_delta(7, 0, A)
+            reorder(1, 0, on_vector)
+            reorder(0, 1, on_vector)
+            mx1(0, SC, 4, 6)
+            reorder(1, 1, on_scalar)
+            q_delta(6)
+            mx1(0, SC, 5, 7)
+            t_stress(0, 0, 2)
+            t_stress(1, 0, 3)
+            t_stress(0, 1, 4)
+            t_stress(1, 1, 5, [0])
+            q_delta(7)
             v_mul(0, 0)
-            v_mul(2, 0)
-            turn[0] = 0
-
-            def step(j, g):
-                mx1_two(P * j, 2 * P, 4 * g, ring)
-                mx1_two(P * j, 2 * P, 4 * g + 2, ring)
-
-            i_hold(0, slice(0, B // 2), on_scalar)
-            mx1(0, SC, 6, ring)
-            mx1(0, SC, 7, ring)
-            i_hold(0, slice(B // 2, B), on_vector)
-            reorder(4, BOTH, on_vector)
+            i_hold(0, left, on_scalar)
+            mx1(0, PC, 6, 0, 2)
+            v_mul(1, 0)
+            mx1(PC, PC, 6, 1, 2)
+            i_hold(0, right, on_scalar)
             v_mul(0, 1)
-            v_hold_q(0)
-            mx1(SC, SC, 0, ring)
-            reorder(6, slice(0, 1), on_scalar)
-            mx1(SC, SC, 1, ring)
-            mx1(SC, SC, 2, ring)
-            reorder(6, slice(1, 2), on_scalar)
-            t_run(13, 26)
-            v_mul(2, 1)
-            i_hold(1, slice(0, B // 2), on_scalar)
-            i_hold(1, slice(B // 2, B), on_vector)
+            reorder(2, 0, on_vector)
+            reorder(2, 1, on_vector)
+            v_mul(1, 1, 0, 1)
+            reorder(3, 0, on_vector)
             v_quant(0)
-            v_hold_q(1)
-            mx1(SC, SC, 3, ring)
-            v_mul(4, 0)
-            mx1(SC, SC, 4, ring)
-            reorder(8, BOTH, on_scalar)
-            mx1(SC, SC, 5, ring)
-            v_mul(6, 0)
+            q_hold(0)
+            mx1(SC, SC, 0, 6)
+            mx1(SC, SC, 1, 7)
+            mx1(SC, SC, 2, 0)
+            mx1(SC, SC, 3, 1)
+            t_stress(1, 1, 5, [1])
+            t_stress(2, 0, 2)
+            t_stress(3, 0, 3)
+            t_stress(2, 1, 4)
+            i_hold(1, right, on_scalar)
+            reorder(3, 1, on_scalar)
+            v_mul(1, 1, 1, 2)
+            i_hold(1, left, on_vector)
+            v_mul(2, 0)
+            v_mul(3, 0)
+
+            def step(k, g, one=6, two=7):
+                mx1(PC * k, PC, 4 * g, one, 2)
+                mx1(PC * k, PC, 4 * g + 2, two, 2)
+
+            step(2, 1)
+            reorder(4, 0, on_scalar)
+            v_quant(1)
+            v_mul(2, 1)
+            step(3, 1, 0, 1)
+            reorder(4, 1, on_scalar)
+            reorder(5, 0, on_scalar)
+            step(4, 0)
+            t_stress(3, 1, 5)
+            t_stress(4, 0, 2)
+            t_stress(4, 1, 3)
+            t_stress(5, 0, 4, [0])
+            q_hold(1)
             v_quant(2)
-            mx1(SC, SC, 6, ring)
-            mx1(SC, SC, 7, ring)
-            mx1_two(8 * P, 2 * P, 0, ring)
-            t_run(26, 39)
-            reorder_quad(10)
-            reorder_half()
-            mx1_two(8 * P, 2 * P, 2, ring)
-            reorder(14, BOTH, on_scalar)
-            v_mul(4, 1)
-            mx2(0, ring)
-            mx2(1, ring)
-            v_mul(6, 1)
-            v_turn(10)
+            v_mul(3, 1)
+            reorder(5, 1, on_scalar)
+            reorder(7, 0, on_scalar)
+            mx2(0, 0)
+            mx2(1, 1)
             v_out(0)
+            v_mul(4, 0)
+            step(4, 1)
+            reorder(7, 1, on_scalar)
+            reorder_quads(0)
             v_out(1)
-            v_quant(4)
-            step(8, 1)
-            reorder_quad(11)
-            reorder_quad(12)
-            mx2(2, ring)
-            mx2(3, ring)
-            v_mul(8, 0)
+            v_quant(3)
+            mx2(2, 0)
+            mx2(3, 1)
+            v_mul(4, 1)
+            step(5, 0)
+            reorder_quads(1)
+            t_stress(5, 0, 4, [1])
+            t_stress(5, 1, 5)
+            t_stress(7, 0, 2)
+            t_stress(7, 1, 3)
             v_out(2)
-            v_quant(6)
+            v_quant(4)
             v_out(3)
             load_hg(4)
             load_hg(5)
-            mx1_two(10 * P, 2 * P, 0, ring)
-            t_run(39, 52)
-            mx1_two(10 * P, 2 * P, 2, ring)
-            mx2(4, ring)
-            mx2(5, ring)
-            v_mul(8, 1)
-            v_turn(11)
-            v_turn(12)
-            v_quant(8)
+            mx2(4, 0)
+            mx2(5, 1)
+            v_mul(5, 0)
+            v_turn(0)
+            step(5, 1)
+            s_lay(0)
             v_out(4)
-            v_mul(10, 0)
             v_out(5)
             load_hg(6)
             load_hg(7)
-            step(10, 1)
-            mx2(6, [3])
-            mx2(7, [6])
+            v_turn(1)
+            mx2(6, 0)
+            mx2(7, 1)
             v_out(6)
-            v_mul(10, 1)
+            v_mul(5, 1)
+            s_lay(1)
+            step(6, 0)
             v_out(7)
-            mx1_two(12 * P, 2 * P, 0, [0])
-            mx1_two(12 * P, 2 * P, 2, [1])
-            mx1_two(12 * P, 2 * P, 4, [7])
-            mx1_two(12 * P, 2 * P, 6, [3])
-            v_quant(10)
-            v_mul(12, 0)
-            mx2(8, [0])
-            mx2(9, [6])
-            v_mul(12, 1)
+            v_quant(5)
+            mx2(8, 4)
+            mx2(9, 5)
+            v_mul(6, 0)
+            step(6, 1)
             v_out(8)
-            v_quant(12)
             v_out(9)
-            ja, jy, jz = S // P - 4, S // P - 2, S // P - 1
-            mx1_two(P * jy, P, 0, [1])
-            mx1_two(P * jy, P, 2, [7])
-            mx2(10, [3])
-            mx1_two(P * jy, P, 4, [1])
-            mx1_two(P * jy, P, 6, [7])
-            v_mul(jy, 0, 1)
+            mx2(10, 0)
+            mx2(11, 1)
             v_out(10)
-            mx2(11, [4])
-            mx1_two(P * jz, P, 0, [1])
-            mx1_two(P * jz, P, 2, [7])
-            v_mul(jy, 1, 1)
+            v_mul(6, 1)
+            step(7, 0)
             v_out(11)
-            v_quant(jy)
-            v_mul(jz, 0, 1)
-            mx2(ja, [0])
-            mx2(ja + 1, [6])
-            mx1_two(P * jz, P, 4, [1])
-            mx1(P * jz, P, 6, [7])
-            mx1(P * jz, P, 7, [3])
-            mx2(jy, [4])
-            v_out(ja)
-            v_quant(jz, 0, 1)
-            v_mul(jz, 1, 1)
-            v_out(ja + 1)
-            v_quant(jz, 1, G)
-            v_out(jy)
-            last_banks = [banks[5], banks[0]]
+            v_quant(6)
+            v_mul(7, 0)
+            mx1(7 * PC, P, 4, 4, 2)
+            mx1(7 * PC, P, 6, 5, 2)
+            mx2(12, 0)
+            v_mul(7, 1, 0, 1)
+            v_quant(7, 0)
+            mx1(7 * PC + P, P, 4, 6, 2)
+            mx1(7 * PC + P, P, 6, 7)
+            mx1(7 * PC + P, P, 7, 4)
+            v_quant(7, 1, 0, 1)
+            mx2(13, 1)
+            mx2(14, 2)
+            v_mul(7, 1, 1, 2)
+            v_out(12)
+            v_quant(7, 1, 1, 2)
+            v_out(13)
+            v_out(14)
+            jz = S // P - 1
+            last_banks = [banks[5], banks[6]]
             for g in range(G):
                 for h in range(2):
                     mx2_pass(jz, g, last_banks[h][:, 0 : B // 2], B // 2 * h, B // 2)
-            for h in range(2):
-                cols = slice(B // 2 * h, B // 2 * (h + 1))
-                res = work.tile([P, B // 2], F32, name="res", bufs=6)
+            for h, cols in enumerate((left, right)):
+                half = work.tile([P, B // 2], F32, name="res", bufs=6)
                 nc.vector.tensor_tensor(
-                    out=res[:], in0=last_banks[h][:, 0 : B // 2], in1=hg[PIECES - 1][:, 1, cols], op=ALU.add
+                    out=half[:], in0=last_banks[h][:, 0 : B // 2], in1=hg[LAST][:, 1, cols], op=ALU.add
                 )
-                nc.sync.dma_start(out=out[P * jz : P * (jz + 1), cols], in_=res[:])
+                nc.sync.dma_start(out=out[P * jz : P * (jz + 1), cols], in_=half[:])

@@ -88,9 +88,9 @@ def tile_scenario_book_pnl_e3_kernel(tc, g_words, g_scales, delta, carry, stress
                 out=gw[c][:, lo:hi].bitcast(I32), in_=gw_view[:, lo:hi, 4 * SC * c : 4 * SC * (c + 1)].bitcast(I32)
             )
 
-        def load_gs(c):
+        def load_gs(c, queue=nc.sync):
             for r in range(4):
-                nc.sync.dma_start(
+                queue.dma_start(
                     out=gs[c][r:P:32].bitcast(I32), in_=gs_view[r:16:4, :, SC * c // 4 : SC * (c + 1) // 4]
                 )
 
@@ -296,15 +296,16 @@ def tile_scenario_book_pnl_e3_kernel(tc, g_words, g_scales, delta, carry, stress
         left, right = slice(0, B // 2), slice(B // 2, B)
 
         with tc.manual_schedule():
-            nc.vector.memset(ca_raw[:], 0)
             for c in range(C):
                 nc.vector.memset(gs[c][:].rearrange("p a n -> p (a n)").bitcast(I32), 0)
+                if c == 0:
+                    nc.vector.memset(ca_raw[:], 0)
             load_d(0)
             load_d(1)
+            load_gs(0, nc.scalar)
             nc.sync.dma_start(out=ca_raw[0:G, :], in_=carry.rearrange("(g w) -> g w", g=G))
             load_d(2)
             load_d(3)
-            load_gs(0)
             for a in range(A):
                 load_g(0, a, a + 1)
             load_d(4)

@@ -47,7 +47,7 @@ def tile_scenario_book_pnl_e3_kernel(tc, g_words, g_scales, delta, carry, stress
         st = {k: keep.tile([P, 2, I], BF16, name="st%d" % k) for k in range(PIECES) if k != TURNED}
         st_quad = [keep.tile([P, 8, P], BF16, name="st_quad%d" % g) for g in range(G)]
         h_raw = [keep.tile([P, 4, B], BF16, name="h_raw%d" % g) for g in range(G)]
-        h_grp = [keep.tile([P, B, 4], BF16, name="h_grp%d" % g, align_bytes=64) for g in range(G)]
+        h_grp = [work.tile([P, B, 4], BF16, name="h_grp", align_bytes=64, bufs=G) for g in range(G)]
         h_codes = keep.tile([P, G, B], U32, name="h_codes", align_bytes=64)
         h_sc = keep.tile([P, G, B], U8, name="h_sc", align_bytes=64)
         ca_raw = keep.tile([P, 512], BF16, name="ca_raw")
@@ -105,7 +105,7 @@ def tile_scenario_book_pnl_e3_kernel(tc, g_words, g_scales, delta, carry, stress
                 )
 
         def load_hg(k):
-            hg[k] = work.tile([P, 2, B], BF16, name="hg", bufs=6)
+            hg[k] = work.tile([P, 2, B], BF16, name="hg", bufs=PIECES)
             nc.sync.dma_start(out=hg[k][:], in_=rows(hedge, k))
 
         def load_h(g):
@@ -265,8 +265,17 @@ def tile_scenario_book_pnl_e3_kernel(tc, g_words, g_scales, delta, carry, stress
         def store(j):
             nc.sync.dma_start(out=rows(out, j // 2)[:, j % 2], in_=res[j][:])
 
+        def result_tile(j, n):
+            if j < EARLY:
+                return work.tile([P, n], F32, name="d_words", bufs=EARLY)
+            if j < EARLY + 3:
+                return work.tile([P, n], F32, name="d_grp", align_bytes=64)
+            if j < EARLY + 3 + G:
+                return work.tile([P, n], F32, name="h_grp", align_bytes=64, bufs=G)
+            return work.tile([P, n], F32, name="st_re", bufs=8)
+
         def v_out(j):
-            res[j] = work.tile([P, B], F32, name="res", bufs=6)
+            res[j] = result_tile(j, B)
             nc.vector.tensor_tensor(out=res[j][:], in0=book[j][:], in1=hg[j // 2][:, j % 2, :], op=ALU.add)
             store(j)
 
@@ -504,7 +513,7 @@ def tile_scenario_book_pnl_e3_kernel(tc, g_words, g_scales, delta, carry, stress
                 for h in range(2):
                     mx2_pass(jz, g, last_banks[h][:, 0 : B // 2], B // 2 * h, B // 2)
             for h, cols in enumerate((left, right)):
-                half = work.tile([P, B // 2], F32, name="res", bufs=6)
+                half = result_tile(jz, B // 2)
                 nc.vector.tensor_tensor(
                     out=half[:], in0=last_banks[h][:, 0 : B // 2], in1=hg[LAST][:, 1, cols], op=ALU.add
                 )

@@ -24,8 +24,8 @@ C = S // SC
 PC = 2 * P
 PIECES = S // PC
 LAST = PIECES - 1
-TURNED = 6
-PLAIN = (TURNED, LAST)
+TURNED = ((5, 0), (6, 0), (6, 1))
+PLAIN = (5, 6, LAST)
 EARLY = 4
 
 
@@ -44,8 +44,9 @@ def tile_scenario_book_pnl_e3_kernel(tc, g_words, g_scales, delta, carry, stress
         d_raw = d_raw + [keep.tile([P, F], BF16, name="d_raw%d" % i) for i in range(EARLY, 8)]
         gw = [keep.tile([P, A, SC], U32, name="gw%d" % c, align_bytes=64) for c in range(C)]
         gs = [keep.tile([P, A, SC], U8, name="gs%d" % c, align_bytes=64) for c in range(C)]
-        st = {k: keep.tile([P, 2, I], BF16, name="st%d" % k) for k in range(PIECES) if k != TURNED}
-        st_quad = [keep.tile([P, 8, P], BF16, name="st_quad%d" % g) for g in range(G)]
+        st = {k: keep.tile([P, 2, I], BF16, name="st%d" % k) for k in (0, 1, 2, 3, 4, 7)}
+        st_half = keep.tile([P, 2, I // 2], BF16, name="st_half")
+        st_quad = {part: keep.tile([P, 8, P], BF16, name="st_quad%d%d" % part) for part in TURNED}
         h_raw = [keep.tile([P, 4, B], BF16, name="h_raw%d" % g) for g in range(G)]
         h_grp = [work.tile([P, B, 4], BF16, name="h_grp", align_bytes=64, bufs=G) for g in range(G)]
         h_codes = keep.tile([P, G, B], U32, name="h_codes", align_bytes=64)
@@ -88,20 +89,25 @@ def tile_scenario_book_pnl_e3_kernel(tc, g_words, g_scales, delta, carry, stress
                 out=gw[c][:, lo:hi].bitcast(I32), in_=gw_view[:, lo:hi, 4 * SC * c : 4 * SC * (c + 1)].bitcast(I32)
             )
 
-        def load_gs(c, queue=nc.sync):
+        def load_gs(c, lo=0, hi=A):
             for r in range(4):
-                queue.dma_start(
-                    out=gs[c][r:P:32].bitcast(I32), in_=gs_view[r:16:4, :, SC * c // 4 : SC * (c + 1) // 4]
+                nc.sync.dma_start(
+                    out=gs[c][r:P:32, lo:hi].bitcast(I32),
+                    in_=gs_view[r:16:4, lo:hi, SC * c // 4 : SC * (c + 1) // 4],
                 )
 
         def load_st(k):
             nc.sync.dma_start(out=st[k][:], in_=rows(stress, k))
 
-        def load_st_quads(g):
-            blocks = stress[PC * TURNED : PC * (TURNED + 1), :].rearrange("(b r) i -> r b i", r=32)
+        def load_st_half():
+            nc.sync.dma_start(out=st_half[:], in_=rows(stress, 5)[:, :, I // 2 : I])
+
+        def load_st_quads(k, g):
+            blocks = stress[PC * k : PC * (k + 1), :].rearrange("(b r) i -> r b i", r=32)
             for q in (0, 2, 1, 3):
                 nc.sync.dma_start(
-                    out=st_quad[g][32 * q : 32 * (q + 1)], in_=blocks[:, :, 512 * g + P * q : 512 * g + P * (q + 1)]
+                    out=st_quad[(k, g)][32 * q : 32 * (q + 1)],
+                    in_=blocks[:, :, 512 * g + P * q : 512 * g + P * (q + 1)],
                 )
 
         def load_hg(k):
@@ -160,9 +166,9 @@ def tile_scenario_book_pnl_e3_kernel(tc, g_words, g_scales, delta, carry, stress
                 in_=d_grp[i][:, lo:hi].rearrange("p a m t -> p (a m t)"),
             )
 
-        def mx1_passes(s0, n, i, acc):
+        def mx1_passes(s0, n, i, acc, passes=range(A)):
             c, w0 = s0 // SC, s0 % SC
-            for a in range(A):
+            for a in passes:
                 nc.tensor.matmul_mx(
                     out=acc,
                     lhsT=d_codes[i][:, a, :].bitcast(E4),
@@ -204,20 +210,24 @@ def tile_scenario_book_pnl_e3_kernel(tc, g_words, g_scales, delta, carry, stress
                 for u in range(2):
                     nc.tensor.transpose(dst[:, u], st_re[(k, g)][:, half, u, :], ident[:])
 
-        def reorder_quads(g):
-            st_re[(TURNED, g)] = work.tile([P, 2, 8, 32], F32, name="quad_re", bufs=2, align_bytes=64)
-            words = st_quad[g][:].bitcast(F32).rearrange("p b (w u) -> p u b w", u=2)
-            nc.scalar.copy(out=st_re[(TURNED, g)][:], in_=words)
+        def reorder_half():
+            st_re[(5, 1)] = work.tile([P, 2, 2, P], F32, name="st_re", bufs=8)
+            nc.scalar.copy(out=st_re[(5, 1)][:], in_=st_half[:].bitcast(F32).rearrange("p j (m u) -> p j u m", u=2))
 
-        def v_turn(g):
-            st_turned[g] = work.tile([P, 512], F32, name="quad_turned", bufs=2, align_bytes=64)
-            nc.vector.transpose(out=st_turned[g][:], in_=st_re[(TURNED, g)][:].rearrange("p u b w -> p (u b w)"))
+        def reorder_quads(k, g):
+            st_re[(k, g)] = work.tile([P, 2, 8, 32], F32, name="quad_re", bufs=2, align_bytes=64)
+            words = st_quad[(k, g)][:].bitcast(F32).rearrange("p b (w u) -> p u b w", u=2)
+            nc.scalar.copy(out=st_re[(k, g)][:], in_=words)
 
-        def s_lay(g):
-            st_words[(TURNED, g)] = work.tile([P, 512], F32, name="quad_re", bufs=2, align_bytes=64)
+        def v_turn(k, g):
+            st_turned[(k, g)] = work.tile([P, 512], F32, name="quad_turned", bufs=2, align_bytes=64)
+            nc.vector.transpose(out=st_turned[(k, g)][:], in_=st_re[(k, g)][:].rearrange("p u b w -> p (u b w)"))
+
+        def s_lay(k, g):
+            st_words[(k, g)] = work.tile([P, 512], F32, name="quad_laid", bufs=2, align_bytes=64)
             nc.scalar.copy(
-                out=st_words[(TURNED, g)][:].rearrange("p (c u i) -> p c u i", u=2, i=4),
-                in_=st_turned[g][:].rearrange("p (u c i) -> p c u i", u=2, i=4),
+                out=st_words[(k, g)][:].rearrange("p (c u i) -> p c u i", u=2, i=4),
+                in_=st_turned[(k, g)][:].rearrange("p (u c i) -> p c u i", u=2, i=4),
             )
 
         def v_mul(k, g, lo=0, hi=2):
@@ -311,12 +321,13 @@ def tile_scenario_book_pnl_e3_kernel(tc, g_words, g_scales, delta, carry, stress
                     nc.vector.memset(ca_raw[:], 0)
             load_d(0)
             load_d(1)
-            load_gs(0, nc.scalar)
             nc.sync.dma_start(out=ca_raw[0:G, :], in_=carry.rearrange("(g w) -> g w", g=G))
             load_d(2)
             load_d(3)
-            for a in range(A):
-                load_g(0, a, a + 1)
+            load_gs(0)
+            load_g(0, 0, 1)
+            load_g(0, 1, 2)
+            load_g(0, 2, 3)
             load_d(4)
             load_d(5)
             load_d(6)
@@ -333,14 +344,15 @@ def tile_scenario_book_pnl_e3_kernel(tc, g_words, g_scales, delta, carry, stress
             load_st(4)
             load_gs(2)
             load_g(2)
-            load_st(5)
             load_hg(0)
+            load_st_quads(5, 0)
+            load_st_half()
             load_st(7)
             load_hg(1)
-            load_st_quads(0)
+            load_st_quads(6, 0)
             load_gs(3)
             load_g(3)
-            load_st_quads(1)
+            load_st_quads(6, 1)
             load_hg(2)
             load_hg(3)
 
@@ -424,32 +436,32 @@ def tile_scenario_book_pnl_e3_kernel(tc, g_words, g_scales, delta, carry, stress
             v_mul(2, 1)
             step(3, 1, 0, 1)
             reorder(4, 1, on_scalar)
-            reorder(5, 0, on_scalar)
             step(4, 0)
             t_stress(3, 1, 5)
             t_stress(4, 0, 2)
             t_stress(4, 1, 3)
-            t_stress(5, 0, 4, [0])
             q_hold(1)
             v_quant(2)
             v_mul(3, 1)
-            reorder(5, 1, on_scalar)
-            reorder(7, 0, on_scalar)
+            reorder_quads(5, 0)
+            reorder_half()
             mx2(0, 0)
             mx2(1, 1)
             v_out(0)
             v_mul(4, 0)
             step(4, 1)
+            reorder(7, 0, on_scalar)
             reorder(7, 1, on_scalar)
-            reorder_quads(0)
             v_out(1)
             v_quant(3)
-            mx2(2, 0)
-            mx2(3, 1)
+            v_turn(5, 0)
+            mx2(2, 4)
+            mx2(3, 0)
             v_mul(4, 1)
+            s_lay(5, 0)
             step(5, 0)
-            reorder_quads(1)
-            t_stress(5, 0, 4, [1])
+            reorder_quads(6, 0)
+            reorder_quads(6, 1)
             t_stress(5, 1, 5)
             t_stress(7, 0, 2)
             t_stress(7, 1, 3)
@@ -458,47 +470,53 @@ def tile_scenario_book_pnl_e3_kernel(tc, g_words, g_scales, delta, carry, stress
             v_out(3)
             load_hg(4)
             load_hg(5)
-            mx2(4, 0)
-            mx2(5, 1)
+            mx2(4, 1)
+            mx2(5, 4)
             v_mul(5, 0)
-            v_turn(0)
+            v_turn(6, 0)
+            def late_step(k, g, three):
+                mx1(PC * k, PC, 4 * g, three[0], 2)
+                mx1(PC * k, PC, 4 * g + 2, three[1])
+                mx1(PC * k, PC, 4 * g + 3, three[2])
+
             step(5, 1)
-            s_lay(0)
+            s_lay(6, 0)
             v_out(4)
             v_out(5)
             load_hg(6)
             load_hg(7)
-            v_turn(1)
+            v_turn(6, 1)
             mx2(6, 0)
             mx2(7, 1)
             v_out(6)
             v_mul(5, 1)
-            s_lay(1)
+            s_lay(6, 1)
             step(6, 0)
             v_out(7)
             v_quant(5)
             mx2(8, 4)
-            mx2(9, 5)
+            mx2(9, 0)
             v_mul(6, 0)
-            step(6, 1)
+            late_step(6, 1, [6, 7, 5])
             v_out(8)
             v_out(9)
-            mx2(10, 0)
-            mx2(11, 1)
-            v_out(10)
+            mx2(10, 1)
+            mx2(11, 4)
             v_mul(6, 1)
-            step(7, 0)
-            v_out(11)
+            late_step(7, 0, [6, 7, 5])
+            v_out(10)
             v_quant(6)
+            v_out(11)
             v_mul(7, 0)
-            mx1(7 * PC, P, 4, 4, 2)
-            mx1(7 * PC, P, 6, 5, 2)
+            mx1(7 * PC, P, 4, 1, 2)
+            mx1(7 * PC, P, 6, 6)
+            mx1(7 * PC, P, 7, 7)
             mx2(12, 0)
             v_mul(7, 1, 0, 1)
             v_quant(7, 0)
-            mx1(7 * PC + P, P, 4, 6, 2)
-            mx1(7 * PC + P, P, 6, 7)
-            mx1(7 * PC + P, P, 7, 4)
+            mx1(7 * PC + P, P, 4, 4, 2)
+            mx1(7 * PC + P, P, 6, 5)
+            mx1(7 * PC + P, P, 7, 6)
             v_quant(7, 1, 0, 1)
             mx2(13, 1)
             mx2(14, 2)
@@ -508,7 +526,7 @@ def tile_scenario_book_pnl_e3_kernel(tc, g_words, g_scales, delta, carry, stress
             v_out(13)
             v_out(14)
             jz = S // P - 1
-            last_banks = [banks[5], banks[6]]
+            last_banks = [banks[7], banks[4]]
             for g in range(G):
                 for h in range(2):
                     mx2_pass(jz, g, last_banks[h][:, 0 : B // 2], B // 2 * h, B // 2)

@@ -337,24 +337,25 @@ def tile_scenario_book_pnl_e3_kernel(tc, g_words, g_scales, delta, carry, stress
             load_h(0)
             load_gs(1)
             load_g(1, 0, 1)
-            load_g(1, 1, A)
+            load_g(1, 1, 2)
             load_st(2)
+            load_g(1, 2, A)
             load_st(3)
             load_h(1)
             load_st(4)
             load_gs(2)
             load_g(2)
             load_hg(0)
-            load_st_quads(5, 0)
             load_st_half()
-            load_st(7)
+            load_st_quads(5, 0)
             load_hg(1)
             load_st_quads(6, 0)
+            load_hg(2)
+            load_st_quads(6, 1)
+            load_hg(3)
             load_gs(3)
             load_g(3)
-            load_st_quads(6, 1)
-            load_hg(2)
-            load_hg(3)
+            load_st(7)
 
             for i in range(EARLY):
                 t_delta(i, range(A), 4 + 2 * (i % 2), 5 + 2 * (i % 2))
@@ -380,9 +381,10 @@ def tile_scenario_book_pnl_e3_kernel(tc, g_words, g_scales, delta, carry, stress
             r_delta(7)
             q_delta(4)
             mx1(0, SC, 3, 6)
-            t_pair(6, 7, [0, 1])
-            q_delta(5)
             reorder(0, 0, on_vector)
+            t_pair(6, 7, [0, 1])
+            t_stress(0, 0, 2, [0])
+            q_delta(5)
             c_first(6, on_vector)
             c_first(7, on_vector)
             c_rest(6, on_scalar)
@@ -393,10 +395,10 @@ def tile_scenario_book_pnl_e3_kernel(tc, g_words, g_scales, delta, carry, stress
             reorder(1, 1, on_scalar)
             q_delta(6)
             mx1(0, SC, 5, 7)
-            t_stress(0, 0, 2)
+            t_stress(0, 0, 2, [1])
             t_stress(1, 0, 3)
             t_stress(0, 1, 4)
-            t_stress(1, 1, 5, [0])
+            t_stress(1, 1, 5)
             q_delta(7)
             v_mul(0, 0)
             i_hold(0, left, on_scalar)
@@ -404,129 +406,128 @@ def tile_scenario_book_pnl_e3_kernel(tc, g_words, g_scales, delta, carry, stress
             v_mul(1, 0)
             mx1(PC, PC, 6, 1, 2)
             i_hold(0, right, on_scalar)
-            v_mul(0, 1)
             reorder(2, 0, on_vector)
             reorder(2, 1, on_vector)
-            v_mul(1, 1, 0, 1)
+            v_mul(0, 1)
+            v_mul(1, 1)
             reorder(3, 0, on_vector)
+            reorder(3, 1, on_vector)
             v_quant(0)
             q_hold(0)
             mx1(SC, SC, 0, 6)
             mx1(SC, SC, 1, 7)
             mx1(SC, SC, 2, 0)
             mx1(SC, SC, 3, 1)
-            t_stress(1, 1, 5, [1])
             t_stress(2, 0, 2)
             t_stress(3, 0, 3)
             t_stress(2, 1, 4)
-            i_hold(1, right, on_scalar)
-            reorder(3, 1, on_scalar)
-            v_mul(1, 1, 1, 2)
-            i_hold(1, left, on_vector)
-            v_mul(2, 0)
-            v_mul(3, 0)
+            t_stress(3, 1, 5, [0])
 
             def step(k, g, one=6, two=7):
                 mx1(PC * k, PC, 4 * g, one, 2)
                 mx1(PC * k, PC, 4 * g + 2, two, 2)
 
-            step(2, 1)
-            reorder(4, 0, on_scalar)
-            v_quant(1)
-            v_mul(2, 1)
-            step(3, 1, 0, 1)
-            reorder(4, 1, on_scalar)
-            step(4, 0)
-            t_stress(3, 1, 5)
-            t_stress(4, 0, 2)
-            t_stress(4, 1, 3)
-            q_hold(1)
-            v_quant(2)
-            v_mul(3, 1)
-            reorder_quads(5, 0)
-            reorder_half()
-            mx2(0, 0)
-            mx2(1, 1)
-            v_out(0)
-            v_mul(4, 0)
-            step(4, 1)
-            reorder(7, 0, on_scalar)
-            reorder(7, 1, on_scalar)
-            v_out(1)
-            v_quant(3)
-            v_turn(5, 0)
-            mx2(2, 4)
-            mx2(3, 0)
-            v_mul(4, 1)
-            s_lay(5, 0)
-            step(5, 0)
-            reorder_quads(6, 0)
-            reorder_quads(6, 1)
-            t_stress(5, 1, 5)
-            t_stress(7, 0, 2)
-            t_stress(7, 1, 3)
-            v_out(2)
-            v_quant(4)
-            v_out(3)
-            load_hg(4)
-            load_hg(5)
-            mx2(4, 1)
-            mx2(5, 4)
-            v_mul(5, 0)
-            v_turn(6, 0)
             def late_step(k, g, three):
                 mx1(PC * k, PC, 4 * g, three[0], 2)
                 mx1(PC * k, PC, 4 * g + 2, three[1])
                 mx1(PC * k, PC, 4 * g + 3, three[2])
 
-            step(5, 1)
-            s_lay(6, 0)
+            i_hold(1, right, on_scalar)
+            reorder(4, 0, on_scalar)
+            i_hold(1, left, on_vector)
+            v_mul(2, 0)
+            q_hold(1)
+            v_mul(3, 0)
+            step(2, 1)
+            reorder(4, 1, on_scalar)
+            v_mul(2, 1)
+            v_quant(1)
+            step(3, 1, 0, 1)
+            reorder_half()
+            mx2(0, 6)
+            mx2(1, 7)
+            t_stress(3, 1, 5, [1])
+            t_stress(4, 0, 2)
+            t_stress(4, 1, 3)
+            t_stress(5, 1, 4)
+            v_out(0)
+            v_mul(3, 1)
+            v_out(1)
+            step(4, 0, 0, 1)
+            reorder_quads(5, 0)
+            v_quant(2)
+            mx2(2, 6)
+            mx2(3, 7)
+            v_quant(3)
+            v_out(2)
+            v_mul(4, 0)
+            step(4, 1, 0, 1)
+            reorder_quads(6, 0)
+            v_out(3)
+            load_hg(4)
+            load_hg(5)
+            v_turn(5, 0)
+            mx2(4, 5)
+            mx2(5, 6)
+            s_lay(5, 0)
+            v_mul(4, 1)
+            step(5, 0, 0, 1)
+            reorder_quads(6, 1)
             v_out(4)
+            v_quant(4)
             v_out(5)
             load_hg(6)
             load_hg(7)
-            v_turn(6, 1)
-            mx2(6, 0)
-            mx2(7, 1)
+            mx2(6, 7)
+            mx2(7, 2)
+            v_mul(5, 0)
+            v_turn(6, 0)
+            late_step(5, 1, [0, 1, 3])
+            s_lay(6, 0)
+            reorder(7, 0, on_scalar)
             v_out(6)
-            v_mul(5, 1)
-            s_lay(6, 1)
-            step(6, 0)
             v_out(7)
-            v_quant(5)
-            mx2(8, 4)
-            mx2(9, 0)
-            v_mul(6, 0)
-            late_step(6, 1, [6, 7, 5])
+            mx2(8, 5)
+            mx2(9, 6)
+            v_mul(5, 1)
+            v_turn(6, 1)
+            late_step(6, 0, [0, 1, 3])
+            s_lay(6, 1)
+            reorder(7, 1, on_scalar)
             v_out(8)
+            v_quant(5)
+            v_mul(6, 0)
+            late_step(6, 1, [7, 2, 4])
             v_out(9)
-            mx2(10, 1)
-            mx2(11, 4)
+            mx2(10, 5)
+            mx2(11, 3)
             v_mul(6, 1)
-            late_step(7, 0, [6, 7, 5])
+            late_step(7, 0, [0, 1, 7])
+            t_stress(7, 0, 2)
+            t_stress(7, 1, 6)
             v_out(10)
             v_quant(6)
             v_out(11)
             v_mul(7, 0)
-            mx1(7 * PC, P, 4, 1, 2)
-            mx1(7 * PC, P, 6, 6)
-            mx1(7 * PC, P, 7, 7)
-            mx2(12, 0)
+            mx1(7 * PC, P, 4, 4, 2)
+            mx1(7 * PC, P, 6, 0)
+            mx1(7 * PC, P, 7, 1)
+            mx2(12, 5)
             v_mul(7, 1, 0, 1)
             v_quant(7, 0)
-            mx1(7 * PC + P, P, 4, 4, 2)
-            mx1(7 * PC + P, P, 6, 5)
-            mx1(7 * PC + P, P, 7, 6)
+            mx1(7 * PC + P, P, 4, 7, 2)
+            mx1(7 * PC + P, P, 6, 4)
+            mx1(7 * PC + P, P, 7, 0)
             v_quant(7, 1, 0, 1)
-            mx2(13, 1)
+            v_out(12)
+            mx2(13, 3)
             mx2(14, 2)
             v_mul(7, 1, 1, 2)
-            v_out(12)
-            v_quant(7, 1, 1, 2)
             v_out(13)
+            v_quant(7, 1, 1, 2)
             v_out(14)
             jz = S // P - 1
-            last_banks = [banks[7], banks[4]]
+            last_banks = [banks[1], banks[7]]
             for g in range(G):
                 for h in range(2):
                     mx2_pass(jz, g, last_banks[h][:, 0 : B // 2], B // 2 * h, B // 2)

@@ -131,10 +131,8 @@ def tile_scenario_book_pnl_e3_kernel(tc, g_words, g_scales, delta, carry, stress
                     nc.tensor.transpose(dst, words, ident[:])
 
         def t_pair(i, first, rest):
-            for m in range(2):
-                t_delta(i + m, [0], first, rest[m], m)
-            for m in range(2):
-                t_delta(i + m, [1, 2], first, rest[m], m)
+            t_delta(i, [1, 2, 0], first, rest[0], 0)
+            t_delta(i + 1, [0, 1, 2], first, rest[1], 1)
 
         def r_delta(i):
             d_re[i] = work.tile([P, A, 2, P], F32, name="d_words", bufs=EARLY)
@@ -348,10 +346,10 @@ def tile_scenario_book_pnl_e3_kernel(tc, g_words, g_scales, delta, carry, stress
             load_hg(0)
             load_st_half()
             load_st_quads(5, 0)
-            load_hg(1)
             load_st_quads(6, 0)
-            load_hg(2)
+            load_hg(1)
             load_st_quads(6, 1)
+            load_hg(2)
             load_hg(3)
             load_gs(3)
             load_g(3)
@@ -382,7 +380,7 @@ def tile_scenario_book_pnl_e3_kernel(tc, g_words, g_scales, delta, carry, stress
             q_delta(4)
             mx1(0, SC, 3, 6)
             reorder(0, 0, on_vector)
-            t_pair(6, 7, [0, 1])
+            t_pair(6, 3, [0, 1])
             t_stress(0, 0, 2, [0])
             q_delta(5)
             c_first(6, on_vector)
@@ -391,8 +389,8 @@ def tile_scenario_book_pnl_e3_kernel(tc, g_words, g_scales, delta, carry, stress
             c_rest(7, on_scalar)
             reorder(1, 0, on_vector)
             reorder(0, 1, on_vector)
-            mx1(0, SC, 4, 6)
             reorder(1, 1, on_scalar)
+            mx1(0, SC, 4, 6)
             q_delta(6)
             mx1(0, SC, 5, 7)
             t_stress(0, 0, 2, [1])
@@ -442,37 +440,40 @@ def tile_scenario_book_pnl_e3_kernel(tc, g_words, g_scales, delta, carry, stress
             reorder(4, 1, on_scalar)
             v_mul(2, 1)
             v_quant(1)
-            step(3, 1, 0, 1)
+            mx1(3 * PC, PC, 4, 0, 2)
             reorder_half()
+            mx1(3 * PC, PC, 6, 1, 2)
             mx2(0, 6)
             mx2(1, 7)
             t_stress(3, 1, 5, [1])
             t_stress(4, 0, 2)
             t_stress(4, 1, 3)
             t_stress(5, 1, 4)
+            reorder_quads(5, 0)
+            reorder_quads(6, 0)
             v_out(0)
             v_mul(3, 1)
             v_out(1)
             step(4, 0, 0, 1)
-            reorder_quads(5, 0)
             v_quant(2)
             mx2(2, 6)
             mx2(3, 7)
             v_quant(3)
+            v_turn(5, 0)
+            s_lay(5, 0)
             v_out(2)
             v_mul(4, 0)
             step(4, 1, 0, 1)
-            reorder_quads(6, 0)
+            reorder_quads(6, 1)
             v_out(3)
             load_hg(4)
             load_hg(5)
-            v_turn(5, 0)
+            v_turn(6, 0)
             mx2(4, 5)
             mx2(5, 6)
-            s_lay(5, 0)
+            s_lay(6, 0)
             v_mul(4, 1)
             step(5, 0, 0, 1)
-            reorder_quads(6, 1)
             v_out(4)
             v_quant(4)
             v_out(5)
@@ -481,18 +482,16 @@ def tile_scenario_book_pnl_e3_kernel(tc, g_words, g_scales, delta, carry, stress
             mx2(6, 7)
             mx2(7, 2)
             v_mul(5, 0)
-            v_turn(6, 0)
+            v_turn(6, 1)
             late_step(5, 1, [0, 1, 3])
-            s_lay(6, 0)
+            s_lay(6, 1)
             reorder(7, 0, on_scalar)
             v_out(6)
             v_out(7)
             mx2(8, 5)
             mx2(9, 6)
             v_mul(5, 1)
-            v_turn(6, 1)
             late_step(6, 0, [0, 1, 3])
-            s_lay(6, 1)
             reorder(7, 1, on_scalar)
             v_out(8)
             v_quant(5)

@@ -42,19 +42,19 @@ def tile_scenario_book_pnl_e3_kernel(tc, g_words, g_scales, delta, carry, stress
 
         d_raw = [work.tile([P, F], BF16, name="d_words", bufs=EARLY) for i in range(EARLY)]
         d_raw = d_raw + [keep.tile([P, F], BF16, name="d_raw%d" % i) for i in range(EARLY, 8)]
-        gw = [keep.tile([P, A, SC], U32, name="gw%d" % c, align_bytes=64) for c in range(C)]
-        gs = [keep.tile([P, A, SC], U8, name="gs%d" % c, align_bytes=64) for c in range(C)]
+        gw = [keep.tile([P, A, SC], U32, name="gw%d" % c, align_bytes=256) for c in range(C)]
+        gs = [keep.tile([P, A, SC], U8, name="gs%d" % c, align_bytes=256) for c in range(C)]
         st = {k: keep.tile([P, 2, I], BF16, name="st%d" % k) for k in (0, 1, 2, 3, 4, 7)}
         st_half = keep.tile([P, 2, I // 2], BF16, name="st_half")
         st_quad = {part: keep.tile([P, 8, P], BF16, name="st_quad%d%d" % part) for part in TURNED}
         h_raw = [keep.tile([P, 4, B], BF16, name="h_raw%d" % g) for g in range(G)]
         h_grp = [work.tile([P, B, 4], BF16, name="h_grp", align_bytes=64, bufs=G) for g in range(G)]
-        h_codes = keep.tile([P, G, B], U32, name="h_codes", align_bytes=64)
-        h_sc = keep.tile([P, G, B], U8, name="h_sc", align_bytes=64)
+        h_codes = keep.tile([P, G, B], U32, name="h_codes", align_bytes=256)
+        h_sc = keep.tile([P, G, B], U8, name="h_sc", align_bytes=256)
         ca_raw = keep.tile([P, 512], BF16, name="ca_raw")
         ca = keep.tile([P, G, 4], F32, name="ca")
-        d_codes = [keep.tile([P, A, P], U32, name="d_codes%d" % i, align_bytes=64) for i in range(8)]
-        d_sc = [keep.tile([P, A, P], U8, name="d_sc%d" % i, align_bytes=64) for i in range(8)]
+        d_codes = [keep.tile([P, A, P], U32, name="d_codes%d" % i, align_bytes=256) for i in range(8)]
+        d_sc = [keep.tile([P, A, P], U8, name="d_sc%d" % i, align_bytes=256) for i in range(8)]
 
         d_view = delta.rearrange("(g m t) k -> g t m k", g=G, t=4)
         gw_view = g_words.rearrange("g p n t -> p g (n t)")
@@ -244,8 +244,8 @@ def tile_scenario_book_pnl_e3_kernel(tc, g_words, g_scales, delta, carry, stress
 
         def v_quant(k, g=None, lo=0, hi=2):
             if k not in pnl_codes:
-                pnl_codes[k] = work.tile([P, G * PC], U32, name="pnl_codes", align_bytes=64, bufs=4)
-                pnl_sc[k] = work.tile([P, G * PC], U8, name="pnl_sc", align_bytes=64, bufs=4)
+                pnl_codes[k] = work.tile([P, G * PC], U32, name="pnl_codes", align_bytes=256, bufs=4)
+                pnl_sc[k] = work.tile([P, G * PC], U8, name="pnl_sc", align_bytes=256, bufs=4)
             cols = slice(0, G * PC) if g is None else slice(PC * g + P * lo, PC * g + P * hi)
             nc.vector.quantize_mx(
                 out=pnl_codes[k][:, cols].bitcast(E5),

from contextlib import ExitStack

import concourse.mybir as mybir
from concourse.masks import make_identity

F, S, I, B = 1536, 2048, 1024, 512
FLOPS = 2 * S * F * I + 2 * S * I * B

F32 = mybir.dt.float32
BF16 = mybir.dt.bfloat16
U32 = mybir.dt.uint32
I32 = mybir.dt.int32
U8 = mybir.dt.uint8
E4 = mybir.dt.float8_e4m3fn_x4
E5 = mybir.dt.float8_e5m2_x4
ACT = mybir.ActivationFunctionType
ALU = mybir.AluOpType

P = 128
A = F // 512
G = I // 512
SC = 512
C = S // SC
PC = 2 * P
PIECES = S // PC
LAST = PIECES - 1
TURNED = ((5, 0), (6, 0), (6, 1))
PLAIN = (5, 6, LAST)
EARLY = 4


def tile_scenario_book_pnl_e3_kernel(tc, g_words, g_scales, delta, carry, stress, hold, hedge, out):
    nc = tc.nc
    with ExitStack() as ctx:
        keep = ctx.enter_context(tc.tile_pool(name="keep", bufs=1))
        work = ctx.enter_context(tc.tile_pool(name="work", bufs=3))
        psum = ctx.enter_context(tc.psum_pool(name="psum", bufs=1))

        ident = keep.tile([P, P], F32, name="ident")
        make_identity(nc, ident[:])
        banks = [psum.tile([P, 512], F32, name="bank%d" % k) for k in range(8)]

        d_raw = [work.tile([P, F], BF16, name="d_words", bufs=EARLY) for i in range(EARLY)]
        d_raw = d_raw + [keep.tile([P, F], BF16, name="d_raw%d" % i) for i in range(EARLY, 8)]
        gw = [keep.tile([P, A, SC], U32, name="gw%d" % c, align_bytes=256) for c in range(C)]
        gs = [keep.tile([P, A, SC], U8, name="gs%d" % c, align_bytes=256) for c in range(C)]
        st = {k: keep.tile([P, 2, I], BF16, name="st%d" % k) for k in (0, 1, 2, 3, 4, 7)}
        st_half = keep.tile([P, 2, I // 2], BF16, name="st_half")
        st_quad = {part: keep.tile([P, 8, P], BF16, name="st_quad%d%d" % part) for part in TURNED}
        h_raw = [keep.tile([P, 4, B], BF16, name="h_raw%d" % g) for g in range(G)]
        h_grp = [work.tile([P, B, 4], BF16, name="h_grp", align_bytes=64, bufs=G) for g in range(G)]
        h_codes = keep.tile([P, G, B], U32, name="h_codes", align_bytes=256)
        h_sc = keep.tile([P, G, B], U8, name="h_sc", align_bytes=256)
        ca_raw = keep.tile([P, 512], BF16, name="ca_raw")
        ca = keep.tile([P, G, 4], F32, name="ca")
        d_codes = [keep.tile([P, A, P], U32, name="d_codes%d" % i, align_bytes=256) for i in range(8)]
        d_sc = [keep.tile([P, A, P], U8, name="d_sc%d" % i, align_bytes=256) for i in range(8)]

        d_view = delta.rearrange("(g m t) k -> g t m k", g=G, t=4)
        gw_view = g_words.rearrange("g p n t -> p g (n t)")
        gs_view = g_scales.bitcast(I32).rearrange("a r n -> r a n")
        h_view = hold.rearrange("(g p j) w -> g p j w", g=G, j=4)

        def rows(array, k):
            piece = array[PC * k : PC * (k + 1), :]
            if k in PLAIN:
                return piece.rearrange("(j p) w -> p j w", j=2)
            return piece.rearrange("(p j) w -> p j w", j=2)

        hg = {}
        units = {}
        st_re = {}
        st_words = {}
        st_turned = {}
        pnl = {}
        pnl_codes = {}
        pnl_sc = {}
        d_grp = {}
        d_re = {}
        d_banks = {}
        book = {}
        res = {}

        def load_d(i):
            nc.sync.dma_start(out=d_raw[i][:], in_=d_view[i // 4, i % 4])

        def load_g(c, lo=0, hi=A):
            nc.sync.dma_start(
                out=gw[c][:, lo:hi].bitcast(I32), in_=gw_view[:, lo:hi, 4 * SC * c : 4 * SC * (c + 1)].bitcast(I32)
            )

        def load_gs(c, lo=0, hi=A):
            for r in range(4):
                nc.sync.dma_start(
                    out=gs[c][r:P:32, lo:hi].bitcast(I32),
                    in_=gs_view[r:16:4, lo:hi, SC * c // 4 : SC * (c + 1) // 4],
                )

        def load_st(k):
            nc.sync.dma_start(out=st[k][:], in_=rows(stress, k))

        def load_st_half():
            nc.sync.dma_start(out=st_half[:], in_=rows(stress, 5)[:, :, I // 2 : I])

        def load_st_quads(k, g):
            blocks = stress[PC * k : PC * (k + 1), :].rearrange("(b r) i -> r b i", r=32)
            for q in (0, 2, 1, 3):
                nc.sync.dma_start(
                    out=st_quad[(k, g)][32 * q : 32 * (q + 1)],
                    in_=blocks[:, :, 512 * g + P * q : 512 * g + P * (q + 1)],
                )

        def load_hg(k):
            hg[k] = work.tile([P, 2, B], BF16, name="hg", bufs=PIECES)
            nc.sync.dma_start(out=hg[k][:], in_=rows(hedge, k))

        def load_h(g):
            nc.sync.dma_start(out=h_raw[g][:], in_=h_view[g])

        def t_delta(i, passes, first, rest, half=0):
            one = banks[first][:, 256 * half : 256 * (half + 1)].rearrange("p (u m) -> p u m", u=2)
            two = banks[rest][:].rearrange("p (a u m) -> p a u m", a=2, u=2)
            d_banks[i] = (one, two)
            for a in passes:
                for u in range(2):
                    dst = one[:, u, :] if a == 0 else two[:, a - 1, u, :]
                    if i in d_re:
                        words = d_re[i][:, a, u, :]
                    else:
                        words = d_raw[i][:].bitcast(F32)[:, 256 * a + u : 256 * (a + 1) : 2]
                    nc.tensor.transpose(dst, words, ident[:])

        def t_pair(i, first, rest):
            t_delta(i, [1, 2, 0], first, rest[0], 0)
            t_delta(i + 1, [0, 1, 2], first, rest[1], 1)

        def r_delta(i):
            d_re[i] = work.tile([P, A, 2, P], F32, name="d_words", bufs=EARLY)
            nc.vector.tensor_copy(
                out=d_re[i][:].rearrange("p a u (v m) -> p v a u m", v=2),
                in_=d_raw[i][:].bitcast(F32).rearrange("p (a v m u) -> p v a u m", a=A, v=2, u=2),
            )

        def c_first(i, copy):
            d_grp[i] = work.tile([P, A, P, 4], BF16, name="d_grp", align_bytes=64)
            copy(
                out=d_grp[i][:, 0].rearrange("p m t -> p (m t)").bitcast(F32).rearrange("p (m u) -> p m u", u=2),
                in_=d_banks[i][0].rearrange("p u m -> p m u"),
            )

        def c_rest(i, copy):
            copy(
                out=d_grp[i][:, 1:3]
                .rearrange("p a m t -> p a (m t)")
                .bitcast(F32)
                .rearrange("p a (m u) -> p a m u", u=2),
                in_=d_banks[i][1].rearrange("p a u m -> p a m u"),
            )

        def q_delta(i, lo=0, hi=A):
            nc.vector.quantize_mx(
                out=d_codes[i][:, lo:hi].rearrange("p a m -> p (a m)").bitcast(E4),
                scales=d_sc[i][:, lo:hi].rearrange("p a m -> p (a m)"),
                in_=d_grp[i][:, lo:hi].rearrange("p a m t -> p (a m t)"),
            )

        def mx1_passes(s0, n, i, acc, passes=range(A)):
            c, w0 = s0 // SC, s0 % SC
            for a in passes:
                nc.tensor.matmul_mx(
                    out=acc,
                    lhsT=d_codes[i][:, a, :].bitcast(E4),
                    lhsT_scale=d_sc[i][:, a, :],
                    rhs=gw[c][:, a, w0 : w0 + n].bitcast(E5),
                    rhs_scale=gs[c][:, a, w0 : w0 + n],
                    start=(a == 0),
                    stop=(a == A - 1),
                )

        def s_unit(s0, n, i, acc):
            g, t = i // 4, i % 4
            if t == 0:
                tile = work.tile([P, 4, n], F32, name="unit", bufs=3)
                for j in range(s0 // P, (s0 + n) // P):
                    units[(j, g)] = (tile, P * j - s0)
            tile, c0 = units[(s0 // P, g)]
            dst = tile[:, t, c0 : c0 + n]
            if s0 // PC not in PLAIN:
                dst = dst.rearrange("p (k j m) -> p k j m", j=2, m=P)
                acc = acc.rearrange("p (k m j) -> p k j m", j=2, m=P)
            nc.scalar.activation(out=dst, in_=acc, func=ACT.Identity, bias=ca[:, g, t : t + 1], scale=1.0)

        def mx1(s0, n, i, bank, tiles=1):
            for m in range(tiles):
                mx1_passes(s0, n, i + m, banks[bank][:, n * m : n * (m + 1)])
            for m in range(tiles):
                s_unit(s0, n, i + m, banks[bank][:, n * m : n * (m + 1)])

        def reorder(k, g, copy):
            st_re[(k, g)] = work.tile([P, 2, 2, P], F32, name="st_re", bufs=8)
            words = st[k][:].bitcast(F32).rearrange("p j (g m u) -> p j g u m", g=G, u=2)
            copy(out=st_re[(k, g)][:], in_=words[:, :, g])

        def t_stress(k, g, bank, halves=(0, 1)):
            st_words[(k, g)] = banks[bank]
            for half in halves:
                dst = banks[bank][:, 256 * half : 256 * (half + 1)].rearrange("p (c u i) -> p u c i", u=2, i=4)
                for u in range(2):
                    nc.tensor.transpose(dst[:, u], st_re[(k, g)][:, half, u, :], ident[:])

        def reorder_half():
            st_re[(5, 1)] = work.tile([P, 2, 2, P], F32, name="st_re", bufs=8)
            nc.scalar.copy(out=st_re[(5, 1)][:], in_=st_half[:].bitcast(F32).rearrange("p j (m u) -> p j u m", u=2))

        def reorder_quads(k, g):
            st_re[(k, g)] = work.tile([P, 2, 8, 32], F32, name="quad_re", bufs=2, align_bytes=64)
            words = st_quad[(k, g)][:].bitcast(F32).rearrange("p b (w u) -> p u b w", u=2)
            nc.scalar.copy(out=st_re[(k, g)][:], in_=words)

        def v_turn(k, g):
            st_turned[(k, g)] = work.tile([P, 512], F32, name="quad_turned", bufs=2, align_bytes=64)
            nc.vector.transpose(out=st_turned[(k, g)][:], in_=st_re[(k, g)][:].rearrange("p u b w -> p (u b w)"))

        def s_lay(k, g):
            st_words[(k, g)] = work.tile([P, 512], F32, name="quad_laid", bufs=2, align_bytes=64)
            nc.scalar.copy(
                out=st_words[(k, g)][:].rearrange("p (c u i) -> p c u i", u=2, i=4),
                in_=st_turned[(k, g)][:].rearrange("p (u c i) -> p c u i", u=2, i=4),
            )

        def v_mul(k, g, lo=0, hi=2):
            if k not in pnl:
                pnl[k] = work.tile([P, G, PC, 4], BF16, name="pnl", align_bytes=64, bufs=4)
            tile, c0 = units[(2 * k + lo, g)]
            n = P * (hi - lo)
            nc.vector.tensor_tensor(
                out=pnl[k][:, g, P * lo : P * hi].rearrange("p (c i) (u e) -> p c u e i", i=4, u=2),
                in0=tile[:, :, c0 : c0 + n].rearrange("p (u e) (c i) -> p c u e i", i=4, u=2),
                in1=st_words[(k, g)][:, 256 * lo : 256 * hi]
                .bitcast(BF16)
                .rearrange("p (c u i e) -> p c u e i", u=2, i=4, e=2),
                op=ALU.mult,
            )

        def v_quant(k, g=None, lo=0, hi=2):
            if k not in pnl_codes:
                pnl_codes[k] = work.tile([P, G * PC], U32, name="pnl_codes", align_bytes=256, bufs=4)
                pnl_sc[k] = work.tile([P, G * PC], U8, name="pnl_sc", align_bytes=256, bufs=4)
            cols = slice(0, G * PC) if g is None else slice(PC * g + P * lo, PC * g + P * hi)
            nc.vector.quantize_mx(
                out=pnl_codes[k][:, cols].bitcast(E5),
                scales=pnl_sc[k][:, cols],
                in_=pnl[k][:].rearrange("p g s t -> p (g s) t")[:, cols].rearrange("p s t -> p (s t)"),
            )

        def mx2_pass(j, g, acc, b0=0, n=B):
            cols = slice(PC * g + P * (j % 2), PC * g + P * (j % 2 + 1))
            nc.tensor.matmul_mx(
                out=acc,
                lhsT=pnl_codes[j // 2][:, cols].bitcast(E5),
                lhsT_scale=pnl_sc[j // 2][:, cols],
                rhs=h_codes[:, g, b0 : b0 + n].bitcast(E4),
                rhs_scale=h_sc[:, g, b0 : b0 + n],
                start=(g == 0),
                stop=(g == G - 1),
            )

        def mx2(j, bank):
            book[j] = banks[bank]
            for g in range(G):
                mx2_pass(j, g, book[j][:])

        def store(j):
            nc.sync.dma_start(out=rows(out, j // 2)[:, j % 2], in_=res[j][:])

        def result_tile(j, n):
            if j < EARLY:
                return work.tile([P, n], F32, name="d_words", bufs=EARLY)
            if j < EARLY + 3:
                return work.tile([P, n], F32, name="d_grp", align_bytes=64)
            if j < EARLY + 3 + G:
                return work.tile([P, n], F32, name="h_grp", align_bytes=64, bufs=G)
            return work.tile([P, n], F32, name="st_re", bufs=8)

        def v_out(j):
            res[j] = result_tile(j, B)
            nc.vector.tensor_tensor(out=res[j][:], in0=book[j][:], in1=hg[j // 2][:, j % 2, :], op=ALU.add)
            store(j)

        def i_hold(g, cols, copy):
            copy(
                out=h_grp[g][:, cols, :].rearrange("p (c i) t -> p c t i", i=4),
                in_=h_raw[g][:, :, cols].rearrange("p t (c i) -> p c t i", i=4),
            )

        def q_hold(g):
            nc.vector.quantize_mx(
                out=h_codes[:, g].bitcast(E4), scales=h_sc[:, g], in_=h_grp[g][:].rearrange("p w j -> p (w j)")
            )

        def turn_carry(bank):
            for u in range(2):
                nc.tensor.transpose(banks[bank][:, P * u : P * (u + 1)], ca_raw[:].bitcast(F32)[:, u:256:2], ident[:])
            nc.scalar.activation(
                out=ca[:].rearrange("p g (u e) -> p u g e", u=2),
                in_=banks[bank][:, 0 : 2 * P].bitcast(BF16).rearrange("p (u r e) -> p u r e", u=2, e=2)[:, :, 0:G, :],
                func=ACT.Identity,
                scale=1.0,
            )

        on_vector = nc.vector.tensor_copy
        on_scalar = nc.scalar.copy
        left, right = slice(0, B // 2), slice(B // 2, B)

        with tc.manual_schedule():
            for c in range(C):
                nc.vector.memset(gs[c][:].rearrange("p a n -> p (a n)").bitcast(I32), 0)
                if c == 0:
                    nc.vector.memset(ca_raw[:], 0)
            load_d(0)
            load_d(1)
            nc.sync.dma_start(out=ca_raw[0:G, :], in_=carry.rearrange("(g w) -> g w", g=G))
            load_d(2)
            load_d(3)
            load_gs(0)
            load_g(0, 0, 1)
            load_g(0, 1, 2)
            load_g(0, 2, 3)
            load_d(4)
            load_d(5)
            load_d(6)
            load_d(7)
            load_st(0)
            load_st(1)
            load_h(0)
            load_gs(1)
            load_g(1, 0, 1)
            load_g(1, 1, 2)
            load_st(2)
            load_g(1, 2, A)
            load_st(3)
            load_h(1)
            load_st(4)
            load_gs(2)
            load_g(2)
            load_hg(0)
            load_st_half()
            load_st_quads(5, 0)
            load_st_quads(6, 0)
            load_hg(1)
            load_st_quads(6, 1)
            load_hg(2)
            load_hg(3)
            load_gs(3)
            load_g(3)
            load_st(7)

            for i in range(EARLY):
                t_delta(i, range(A), 4 + 2 * (i % 2), 5 + 2 * (i % 2))
                c_first(i, on_vector)
                c_rest(i, on_scalar)
                if i == 1:
                    turn_carry(3)
                if i > 0:
                    q_delta(i - 1, 1, A)
                q_delta(i, 0, 1)
            q_delta(3, 1, A)
            r_delta(4)
            r_delta(5)
            mx1(0, SC, 0, 0)
            mx1(0, SC, 1, 1)
            mx1(0, SC, 2, 2)
            t_pair(4, 3, [4, 5])
            r_delta(6)
            c_first(4, on_vector)
            c_first(5, on_vector)
            c_rest(4, on_scalar)
            c_rest(5, on_scalar)
            r_delta(7)
            q_delta(4)
            mx1(0, SC, 3, 6)
            reorder(0, 0, on_vector)
            t_pair(6, 3, [0, 1])
            t_stress(0, 0, 2, [0])
            q_delta(5)
            c_first(6, on_vector)
            c_first(7, on_vector)
            c_rest(6, on_scalar)
            c_rest(7, on_scalar)
            reorder(1, 0, on_vector)
            reorder(0, 1, on_vector)
            reorder(1, 1, on_scalar)
            mx1(0, SC, 4, 6)
            q_delta(6)
            mx1(0, SC, 5, 7)
            t_stress(0, 0, 2, [1])
            t_stress(1, 0, 3)
            t_stress(0, 1, 4)
            t_stress(1, 1, 5)
            q_delta(7)
            v_mul(0, 0)
            i_hold(0, left, on_scalar)
            mx1(0, PC, 6, 0, 2)
            v_mul(1, 0)
            mx1(PC, PC, 6, 1, 2)
            i_hold(0, right, on_scalar)
            reorder(2, 0, on_vector)
            reorder(2, 1, on_vector)
            v_mul(0, 1)
            v_mul(1, 1)
            reorder(3, 0, on_vector)
            reorder(3, 1, on_vector)
            v_quant(0)
            q_hold(0)
            mx1(SC, SC, 0, 6)
            mx1(SC, SC, 1, 7)
            mx1(SC, SC, 2, 0)
            mx1(SC, SC, 3, 1)
            t_stress(2, 0, 2)
            t_stress(3, 0, 3)
            t_stress(2, 1, 4)
            t_stress(3, 1, 5, [0])

            def step(k, g, one=6, two=7):
                mx1(PC * k, PC, 4 * g, one, 2)
                mx1(PC * k, PC, 4 * g + 2, two, 2)

            def late_step(k, g, three):
                mx1(PC * k, PC, 4 * g, three[0], 2)
                mx1(PC * k, PC, 4 * g + 2, three[1])
                mx1(PC * k, PC, 4 * g + 3, three[2])

            i_hold(1, right, on_scalar)
            reorder(4, 0, on_scalar)
            i_hold(1, left, on_vector)
            v_mul(2, 0)
            q_hold(1)
            v_mul(3, 0)
            step(2, 1)
            reorder(4, 1, on_scalar)
            v_mul(2, 1)
            v_quant(1)
            mx1(3 * PC, PC, 4, 0, 2)
            reorder_half()
            mx1(3 * PC, PC, 6, 1, 2)
            mx2(0, 6)
            mx2(1, 7)
            t_stress(3, 1, 5, [1])
            t_stress(4, 0, 2)
            t_stress(4, 1, 3)
            t_stress(5, 1, 4)
            reorder_quads(5, 0)
            reorder_quads(6, 0)
            v_out(0)
            v_mul(3, 1)
            v_out(1)
            step(4, 0, 0, 1)
            v_quant(2)
            mx2(2, 6)
            mx2(3, 7)
            v_quant(3)
            v_turn(5, 0)
            s_lay(5, 0)
            v_out(2)
            v_mul(4, 0)
            step(4, 1, 0, 1)
            reorder_quads(6, 1)
            v_out(3)
            load_hg(4)
            load_hg(5)
            v_turn(6, 0)
            mx2(4, 5)
            mx2(5, 6)
            s_lay(6, 0)
            v_mul(4, 1)
            step(5, 0, 0, 1)
            v_out(4)
            v_quant(4)
            v_out(5)
            load_hg(6)
            load_hg(7)
            mx2(6, 7)
            mx2(7, 2)
            v_mul(5, 0)
            v_turn(6, 1)
            late_step(5, 1, [0, 1, 3])
            s_lay(6, 1)
            reorder(7, 0, on_scalar)
            v_out(6)
            v_out(7)
            mx2(8, 5)
            mx2(9, 6)
            v_mul(5, 1)
            late_step(6, 0, [0, 1, 3])
            reorder(7, 1, on_scalar)
            v_out(8)
            v_quant(5)
            v_mul(6, 0)
            late_step(6, 1, [7, 2, 4])
            v_out(9)
            mx2(10, 5)
            mx2(11, 3)
            v_mul(6, 1)
            late_step(7, 0, [0, 1, 7])
            t_stress(7, 0, 2)
            t_stress(7, 1, 6)
            v_out(10)
            v_quant(6)
            v_out(11)
            v_mul(7, 0)
            mx1(7 * PC, P, 4, 4, 2)
            mx1(7 * PC, P, 6, 0)
            mx1(7 * PC, P, 7, 1)
            mx2(12, 5)
            v_mul(7, 1, 0, 1)
            v_quant(7, 0)
            mx1(7 * PC + P, P, 4, 7, 2)
            mx1(7 * PC + P, P, 6, 4)
            mx1(7 * PC + P, P, 7, 0)
            v_quant(7, 1, 0, 1)
            v_out(12)
            mx2(13, 3)
            mx2(14, 2)
            v_mul(7, 1, 1, 2)
            v_out(13)
            v_quant(7, 1, 1, 2)
            v_out(14)
            jz = S // P - 1
            last_banks = [banks[1], banks[7]]
            for g in range(G):
                for h in range(2):
                    mx2_pass(jz, g, last_banks[h][:, 0 : B // 2], B // 2 * h, B // 2)
            for h, cols in enumerate((left, right)):
                half = result_tile(jz, B // 2)
                nc.vector.tensor_tensor(
                    out=half[:], in0=last_banks[h][:, 0 : B // 2], in1=hg[LAST][:, 1, cols], op=ALU.add
                )
                nc.sync.dma_start(out=out[P * jz : P * (jz + 1), cols], in_=half[:])
